import numpy as np
import ml_dtypes


def mxq(x, axis, fmt="e4m3"):
    dtype, down = {"e4m3": (ml_dtypes.float8_e4m3fn, 7), "e5m2": (ml_dtypes.float8_e5m2, 14)}[fmt]
    v = np.moveaxis(np.asarray(x, np.float32).astype(ml_dtypes.bfloat16).astype(np.float64), axis, -1)
    blocks = v.reshape(v.shape[:-1] + (-1, 32))
    amax = np.abs(blocks).max(-1, keepdims=True)
    byte = np.maximum(np.where(amax > 0, np.frexp(amax)[1] - 1 + 127, 0) - down, 1)
    scale = np.exp2(byte - 127.0)
    codes = (blocks / scale).astype(np.float32).astype(dtype).astype(np.float64)
    return np.moveaxis((codes * scale).reshape(v.shape), -1, axis)


WIDE = False


def mx_kscale(k):
    if not WIDE:
        return np.ones(k)
    levels = np.array([10, -10, 5, -5, 0])
    if k % 512:
        return np.exp2(np.random.permutation(np.resize(levels, k // 32))).repeat(32)
    a = np.empty((k // 512, 16))
    for p in range(k // 512):
        a[p, :8] = np.random.permutation(np.resize(levels, 8))
        for g in range(8):
            far = levels[np.abs(levels - a[p, g]) >= 10]
            a[p, g + 8] = far[np.random.randint(len(far))]
    return np.exp2(a.ravel()).repeat(32)


def f64(x):
    return np.asarray(x).astype(np.float64)


def striped(idx):
    return np.tile(idx.reshape(-1, 16).T, (8, 1)).astype(np.uint16)


def unstriped(offs):
    return offs[:16].T.reshape(-1).astype(np.int64)


K, T, E, C, N = 2560, 640, 20, 128, 128
TOP = 4


def by_expert(wq, xq):
    return np.concatenate([wq[e].T @ xq[:, e * C:(e + 1) * C] for e in range(E)], axis=1)


def setup_inputs():
    n = np.random.standard_normal
    s = mx_kscale(K)[:, None]
    deal = np.repeat(np.arange(E), C).reshape(TOP, T)[:, np.random.permutation(T)]
    deal = np.take_along_axis(deal, np.argsort(np.random.rand(TOP, T), axis=0), axis=0)
    for _ in range(8):
        s_, t_ = np.random.permutation(T).reshape(2, -1); r = np.random.randint(TOP, size=T // 2); x, y = deal[r, s_].copy(), deal[r, t_].copy()
        ok = ~((deal[:, s_] == y).any(0) | (deal[:, t_] == x).any(0)); deal[r[ok], s_[ok]] = y[ok]; deal[r[ok], t_[ok]] = x[ok]
    order = np.lexsort((np.random.rand(TOP * T), deal.reshape(-1)))
    slot_token = order % T; pos = np.empty(TOP * T, np.int64); pos[order] = np.arange(TOP * T); pos = pos.reshape(TOP, T)
    g = np.random.uniform(0.5, 1.5, (TOP, T)); g = g / g.sum(0)
    return {
        "xT": (n((K, T)) * s).astype(np.float32),
        "w": (n((E, K, N)) / np.sqrt(K) / s[None]).astype(np.float32),
        "gate": np.stack([np.tile(r, (N, 1)) for r in g]).astype(np.float32),
        "offs": striped(slot_token),
        "pos1": striped(pos[0]),
        "pos2": striped(pos[1]),
        "pos3": striped(pos[2]),
        "pos4": striped(pos[3]),
    }


def reference(xT, w, gate, offs, pos1, pos2, pos3, pos4):
    idx = unstriped(offs)
    xq = mxq(f64(xT)[:, idx], 0, "e4m3")
    y = by_expert(mxq(f64(w), 1, "e4m3"), xq)
    return sum(f64(gate[r]) * y[:, unstriped(p)] for r, p in enumerate((pos1, pos2, pos3, pos4)))

@@ -1,0 +1,219 @@
+from contextlib import ExitStack
+
+import concourse.mybir as mybir
+
+K, T, E, C, N = 2560, 640, 20, 128, 128
+SLOTS = E * C
+P = 128
+PASSES = 5
+UNITS = E * PASSES
+FLOPS = 2 * SLOTS * K * N
+
+F32 = mybir.dt.float32
+BF16 = mybir.dt.bfloat16
+U32 = mybir.dt.uint32
+U16 = mybir.dt.uint16
+U8 = mybir.dt.uint8
+FP8X4 = mybir.dt.float8_e4m3fn_x4
+MULT = mybir.AluOpType.mult
+ADD = mybir.AluOpType.add
+
+GROUP = 2
+REGIONS = 9
+REGION = 4096
+AHEAD = 3
+EARLY = 2
+CHUNKS = [4] * 24 + [2, 1, 1]
+BANK_EXPERTS = [[0, 1, 2, 3], [4, 5, 6, 7], [8, 9, 10, 11], [12, 13, 14, 15], [16, 17, 18], [19]]
+
+
+def tile_moe_tk_lin_none_kernel(tc, xT, w, gate, offs, pos1, pos2, pos3, pos4, out):
+    nc = tc.nc
+    with ExitStack() as ctx:
+        keep = ctx.enter_context(tc.tile_pool(name="keep", bufs=1))
+        xraw_pool = ctx.enter_context(tc.tile_pool(name="xraw", bufs=3))
+        xgrp_pool = ctx.enter_context(tc.tile_pool(name="xgrp", bufs=2))
+        wraw_pool = ctx.enter_context(tc.tile_pool(name="wraw", bufs=9))
+        ring = ctx.enter_context(tc.tile_pool(name="ring", bufs=1))
+        wq_pool = ctx.enter_context(tc.tile_pool(name="wq", bufs=10))
+        psum = ctx.enter_context(tc.psum_pool(name="psum", bufs=1))
+
+        offs_t = keep.tile([P, SLOTS // 16], U16, name="offs_t")
+        nc.sync.dma_start(offs_t[:], offs)
+        pos_t = [keep.tile([P, T // 16], U16, name=f"pos_t{r}") for r in range(4)]
+
+        words = [keep.tile([P, T], U32, name=f"words{a}", align_bytes=64) for a in range(PASSES)]
+        bytes_a = keep.tile([P, T], U8, name="bytes_a", align_bytes=64)
+        bytes_b = keep.tile([P, T], U8, name="bytes_b", align_bytes=64)
+        gwords_early = [keep.tile([P, SLOTS], U32, name=f"gwords{a}", align_bytes=64) for a in range(EARLY)]
+        y = keep.tile([P, SLOTS], F32, name="y")
+        half = keep.tile([P, 2, T], F32, name="half")
+        res = keep.tile([P, T], F32, name="res")
+        banks = [psum.tile([P, 512], F32, name=f"bank{b}") for b in range(len(BANK_EXPERTS))]
+
+        nc.gpsimd.memset(bytes_a[:], 0)
+        nc.gpsimd.memset(bytes_b[:], 0)
+
+        def gather(dst, src, first, count):
+            nc.vector.tensor_copy(dst, src[:].indirect(offs_t[:, first // 16 : (first + count) // 16]))
+
+        for a in range(PASSES):
+            raw = xraw_pool.tile([P, 4, T], F32, name="xraw")
+            nc.sync.dma_start(raw[:], xT[512 * a : 512 * (a + 1), :].rearrange("(p j) t -> p j t", j=4))
+            grp = xgrp_pool.tile([P, T, 4], BF16, name="xgrp", align_bytes=64)
+            for lo, hi, eng in ((0, 256, "s"), (256, 640, "v")) if a == 0 else ((0, 640, "s"),):
+                dst = grp[:, lo:hi, :].rearrange("p (c i) t -> p c t i", i=4)
+                src = raw[:, :, lo:hi].rearrange("p t (c i) -> p c t i", i=4)
+                if eng == "s":
+                    nc.scalar.copy(dst, src)
+                else:
+                    nc.vector.tensor_copy(dst, src)
+            flat = grp[:].rearrange("p t j -> p (t j)")
+            plane, k = (bytes_a, 4 * a) if a < 4 else (bytes_b, 0)
+            for lo, hi in ((0, 512), (512, 640)):
+                nc.vector.quantize_mx(
+                    out=words[a][:, lo:hi].bitcast(FP8X4),
+                    scales=plane[k:P, lo:hi],
+                    in_=flat[:, 4 * lo : 4 * hi],
+                )
+            if a < EARLY:
+                for s in range(0, SLOTS, 480):
+                    c = min(480, SLOTS - s)
+                    gather(gwords_early[a][:, s : s + c], words[a], s, c)
+
+        w_units = w.rearrange("e (a p j) n -> p (e a) (j n)", a=PASSES, j=4)
+        bank_of = {e: (b, i) for b, es in enumerate(BANK_EXPERTS) for i, e in enumerate(es)}
+        firsts = [sum(CHUNKS[:i]) for i in range(len(CHUNKS))]
+        quantised = {}
+        groups = {}
+        n_groups = (E + GROUP - 1) // GROUP
+        first_use = {g: g * GROUP * PASSES // 4 for g in range(n_groups)}
+        after = {first_use[g] - AHEAD: g for g in range(n_groups) if first_use[g] >= AHEAD}
+        region_of = {g: c % REGIONS for c, g in after.items()}
+
+        def gather_group(g):
+            first = g * GROUP * C
+            count = min(GROUP * C, SLOTS - first)
+            at = (region_of[g] if g in region_of else REGIONS + g) * REGION
+            late = []
+            for a in range(EARLY, PASSES):
+                t = ring.tile([P, GROUP * C], U32, name=f"late{a}_{g}", align_bytes=64, offset=at)
+                at += 4 * GROUP * C
+                gather(t[:, 0:count], words[a], first, count)
+                late.append(t)
+            ta = ring.tile([P, GROUP * C], U8, name=f"gba{g}", align_bytes=64, offset=at)
+            gather(ta[:, 0:count], bytes_a, first, count)
+            tb = ring.tile([P, GROUP * C], U8, name=f"gbb{g}", align_bytes=64, offset=at + GROUP * C)
+            gather(tb[:, 0:count], bytes_b, first, count)
+            groups[g] = (late, ta, tb)
+
+        def interleave(eng, grp, raw, u0, u1, n0, n1):
+            dst = grp[:, u0:u1, n0:n1, :].rearrange("p u (c i) t -> p u c t i", i=4)
+            src = raw[:, u0:u1, :, n0:n1].rearrange("p u t (c i) -> p u c t i", i=4)
+            if eng == "s":
+                nc.scalar.copy(dst, src)
+            elif eng == "g":
+                nc.gpsimd.tensor_scalar(dst, src, 1.0, 0.0, MULT, ADD)
+            else:
+                nc.vector.tensor_copy(dst, src)
+
+        def prepare(ci):
+            unit, size = firsts[ci], CHUNKS[ci]
+            raw = wraw_pool.tile([P, 4, 4, N], F32, name="wraw")
+            nc.sync.dma_start(
+                raw[:, 0:size].rearrange("p u j n -> p u (j n)"), w_units[:, unit : unit + size, :]
+            )
+            grp = ring.tile([P, 4, N, 4], BF16, name=f"wgrp{ci}", align_bytes=64, offset=(ci % REGIONS) * REGION)
+            if 1 < size < 4 or ci == len(CHUNKS) - 2:
+                shares = (("s", 0, size, 0, N),)
+            elif size < 4:
+                shares = (("s", 0, size, 0, N // 2), ("v", 0, size, N // 2, N))
+            else:
+                shares = (("s", 0, 3, 0, N), ("g", 3, 4, 0, N))
+            for eng, u0, u1, n0, n1 in shares:
+                interleave(eng, grp, raw, u0, u1, n0, n1)
+            codes = wq_pool.tile([P, 4 * N], U32, name="wcodes", align_bytes=64)
+            scales = wq_pool.tile([P, 4 * N], U8, name="wscales", align_bytes=64)
+            nc.vector.quantize_mx(
+                out=codes[:, 0 : size * N].bitcast(FP8X4),
+                scales=scales[:, 0 : size * N],
+                in_=grp[:, 0:size].rearrange("p u n j -> p (u n j)"),
+            )
+            quantised[ci] = (codes, scales)
+
+        def multiply(ci):
+            unit, size = firsts[ci], CHUNKS[ci]
+            codes, scales = quantised.pop(ci)
+            for u in range(size):
+                e, a = divmod(unit + u, PASSES)
+                b, i = bank_of[e]
+                g = e // GROUP
+                late, ta, tb = groups[g]
+                here = slice((e - g * GROUP) * C, (e - g * GROUP + 1) * C)
+                plane, k = (ta, 4 * a) if a < 4 else (tb, 0)
+                rhs = gwords_early[a][:, e * C : (e + 1) * C] if a < EARLY else late[a - EARLY][:, here]
+                nc.tensor.matmul_mx(
+                    out=banks[b][:, i * C : (i + 1) * C],
+                    lhsT=codes[:, u * N : (u + 1) * N].bitcast(FP8X4),
+                    lhsT_scale=scales[:, u * N : (u + 1) * N],
+                    rhs=rhs.bitcast(FP8X4),
+                    rhs_scale=plane[k:P, here],
+                    start=(a == 0),
+                    stop=(a == PASSES - 1),
+                )
+
+        def evacuate(b):
+            first = BANK_EXPERTS[b][0] * C
+            width = len(BANK_EXPERTS[b]) * C
+            nc.scalar.copy(y[:, first : first + width], banks[b][:, 0:width])
+
+        LAG = 3
+        EVAC_LAG = 5
+        evac_at = {}
+        for b, es in enumerate(BANK_EXPERTS):
+            closed = max(i for i, f in enumerate(firsts) if f <= es[-1] * PASSES + PASSES - 1)
+            evac_at.setdefault(min(closed + LAG + (EVAC_LAG if b < 4 else 0), len(CHUNKS) + LAG - 1), []).append(b)
+        for g in range(n_groups):
+            if g not in region_of:
+                gather_group(g)
+        for ci in range(len(CHUNKS) + LAG):
+            if ci < len(CHUNKS):
+                prepare(ci)
+            if ci in after:
+                gather_group(after[ci])
+            if ci == 20:
+                for t, src in zip(pos_t, (pos1, pos2, pos3, pos4)):
+                    nc.sync.dma_start(t[:], src)
+            if ci == len(CHUNKS) - 1:
+                gate_t = xraw_pool.tile([P, 4, T], F32, name="xraw")
+                for r in range(4):
+                    nc.sync.dma_start(gate_t[:, r, :], gate[r])
+            if ci >= LAG:
+                multiply(ci - LAG)
+            for b in evac_at.get(ci, []):
+                evacuate(b)
+
+        prod = xraw_pool.tile([P, 4, T], F32, name="xraw")
+        def weigh(r, lo, hi):
+            nc.vector.tensor_tensor(
+                prod[:, r, lo:hi], y[:].indirect(pos_t[r][:, lo // 16 : hi // 16]), gate_t[:, r, lo:hi], MULT
+            )
+
+        def add_pairs(lo, hi):
+            nc.vector.tensor_add(half[:, :, lo:hi], prod[:, 0:2, lo:hi], prod[:, 2:4, lo:hi])
+
+        def finish(lo, hi):
+            nc.vector.tensor_add(res[:, lo:hi], half[:, 0, lo:hi], half[:, 1, lo:hi])
+            nc.sync.dma_start(out[:, lo:hi], res[:, lo:hi])
+
+        CUT = 384
+        for r in range(4):
+            weigh(r, 0, CUT)
+        weigh(0, CUT, T)
+        add_pairs(0, CUT)
+        weigh(1, CUT, T)
+        finish(0, CUT)
+        weigh(2, CUT, T)
+        weigh(3, CUT, T)
+        add_pairs(CUT, T)
+        finish(CUT, T)

@@ -11,6 +11,7 @@ FLOPS = 2 * SLOTS * K * N
 
 F32 = mybir.dt.float32
 BF16 = mybir.dt.bfloat16
+I32 = mybir.dt.int32
 U32 = mybir.dt.uint32
 U16 = mybir.dt.uint16
 U8 = mybir.dt.uint8
@@ -18,49 +19,65 @@ FP8X4 = mybir.dt.float8_e4m3fn_x4
 MULT = mybir.AluOpType.mult
 ADD = mybir.AluOpType.add
 
-GROUP = 2
-REGIONS = 9
-REGION = 4096
-AHEAD = 3
-EARLY = 2
 CHUNKS = [4] * 24 + [2, 1, 1]
 BANK_EXPERTS = [[0, 1, 2, 3], [4, 5, 6, 7], [8, 9, 10, 11], [12, 13, 14, 15], [16, 17, 18], [19]]
+GATHER = 480
+GPSIMD_UNTIL = 12
+VECTOR_FROM = 16
+HALF_FROM = 22
+Y_AFTER = 17
+GATE_AFTER = 22
+
+BIG = 4 * T * 4
+RAW = 4 * 4 * N * 4
+GRP = 4 * N * 4 * 2
+XGRP = T * 4 * 2
+GRP_SLOTS = 18
+XRAW_AT = [0] + [a * BIG + XGRP for a in range(1, PASSES)]
+WRAW_AT = [BIG + XGRP - RAW] + XRAW_AT[1:]
+GRP_AT = PASSES * BIG + XGRP
+GW_AT = GRP_AT + GRP_SLOTS * GRP
+XGRP_AT = [BIG, GW_AT + 3 * BIG + 512, GW_AT + BIG, GW_AT + 4 * BIG + XGRP, GW_AT + 2 * BIG]
+SHIFT_AFTER = 5
 
 
 def tile_moe_tk_lin_none_kernel(tc, xT, w, gate, offs, pos1, pos2, pos3, pos4, out):
     nc = tc.nc
     with ExitStack() as ctx:
         keep = ctx.enter_context(tc.tile_pool(name="keep", bufs=1))
-        xraw_pool = ctx.enter_context(tc.tile_pool(name="xraw", bufs=3))
-        xgrp_pool = ctx.enter_context(tc.tile_pool(name="xgrp", bufs=2))
-        wraw_pool = ctx.enter_context(tc.tile_pool(name="wraw", bufs=9))
-        ring = ctx.enter_context(tc.tile_pool(name="ring", bufs=1))
-        wq_pool = ctx.enter_context(tc.tile_pool(name="wq", bufs=10))
+        arena = ctx.enter_context(tc.tile_pool(name="arena", bufs=1))
+        wq_pool = ctx.enter_context(tc.tile_pool(name="wq", bufs=8))
         psum = ctx.enter_context(tc.psum_pool(name="psum", bufs=1))
 
         offs_t = keep.tile([P, SLOTS // 16], U16, name="offs_t")
-        nc.sync.dma_start(offs_t[:], offs)
         pos_t = [keep.tile([P, T // 16], U16, name=f"pos_t{r}") for r in range(4)]
 
         words = [keep.tile([P, T], U32, name=f"words{a}", align_bytes=64) for a in range(PASSES)]
-        bytes_a = keep.tile([P, T], U8, name="bytes_a", align_bytes=64)
+        bytes_a = arena.tile([P, T], U8, name="bytes_a", align_bytes=64, offset=GW_AT + 4 * BIG - T // 2)
         bytes_b = keep.tile([P, T], U8, name="bytes_b", align_bytes=64)
-        gwords_early = [keep.tile([P, SLOTS], U32, name=f"gwords{a}", align_bytes=64) for a in range(EARLY)]
-        y = keep.tile([P, SLOTS], F32, name="y")
-        half = keep.tile([P, 2, T], F32, name="half")
-        res = keep.tile([P, T], F32, name="res")
+        merged = arena.tile([P, T], U8, name="merged", align_bytes=64, offset=GW_AT + 3 * BIG - T // 2)
+        gwords = [
+            arena.tile([P, SLOTS], U32, name=f"gwords{a}", align_bytes=64, offset=GW_AT + a * BIG)
+            for a in range(PASSES)
+        ]
+        gbytes_a = keep.tile([P, SLOTS], U8, name="gbytes_a", align_bytes=64)
+        gbytes_b = arena.tile([P, SLOTS], U8, name="gbytes_b", align_bytes=64, offset=0)
         banks = [psum.tile([P, 512], F32, name=f"bank{b}") for b in range(len(BANK_EXPERTS))]
 
-        nc.gpsimd.memset(bytes_a[:], 0)
         nc.gpsimd.memset(bytes_b[:], 0)
+        nc.gpsimd.memset(bytes_a[:], 0)
 
-        def gather(dst, src, first, count):
-            nc.vector.tensor_copy(dst, src[:].indirect(offs_t[:, first // 16 : (first + count) // 16]))
+        def gather_all(dst, src):
+            for s in range(0, SLOTS, GATHER):
+                c = min(GATHER, SLOTS - s)
+                nc.vector.tensor_copy(dst[:, s : s + c], src[:].indirect(offs_t[:, s // 16 : (s + c) // 16]))
 
         for a in range(PASSES):
-            raw = xraw_pool.tile([P, 4, T], F32, name="xraw")
+            raw = arena.tile([P, 4, T], F32, name=f"xraw{a}", align_bytes=64, offset=XRAW_AT[a])
             nc.sync.dma_start(raw[:], xT[512 * a : 512 * (a + 1), :].rearrange("(p j) t -> p j t", j=4))
-            grp = xgrp_pool.tile([P, T, 4], BF16, name="xgrp", align_bytes=64)
+            if a == 0:
+                nc.sync.dma_start(offs_t[:], offs)
+            grp = arena.tile([P, T, 4], BF16, name=f"xgrp{a}", align_bytes=64, offset=XGRP_AT[a])
             for lo, hi, eng in ((0, 256, "s"), (256, 640, "v")) if a == 0 else ((0, 640, "s"),):
                 dst = grp[:, lo:hi, :].rearrange("p (c i) t -> p c t i", i=4)
                 src = raw[:, :, lo:hi].rearrange("p t (c i) -> p c t i", i=4)
@@ -69,43 +86,28 @@ def tile_moe_tk_lin_none_kernel(tc, xT, w, gate, offs, pos1, pos2, pos3, pos4, o
                 else:
                     nc.vector.tensor_copy(dst, src)
             flat = grp[:].rearrange("p t j -> p (t j)")
-            plane, k = (bytes_a, 4 * a) if a < 4 else (bytes_b, 0)
+            plane, k = (bytes_a, 4 * (a - 1)) if a else (bytes_b, 0)
             for lo, hi in ((0, 512), (512, 640)):
                 nc.vector.quantize_mx(
                     out=words[a][:, lo:hi].bitcast(FP8X4),
                     scales=plane[k:P, lo:hi],
                     in_=flat[:, 4 * lo : 4 * hi],
                 )
-            if a < EARLY:
-                for s in range(0, SLOTS, 480):
-                    c = min(480, SLOTS - s)
-                    gather(gwords_early[a][:, s : s + c], words[a], s, c)
+            if a == 0:
+                nc.sync.dma_start(merged[16:P, :].bitcast(I32), bytes_b[0 : P - 16, :].bitcast(I32))
+                gather_all(gwords[0], words[0])
+            if a == 2:
+                gather_all(gwords[1], words[1])
+        for q in range(0, P, 32):
+            nc.vector.tensor_copy(merged[q : q + 16, :].bitcast(I32), bytes_a[q : q + 16, :].bitcast(I32))
+        gather_all(gbytes_a, merged)
+        for a in range(2, PASSES):
+            gather_all(gwords[a], words[a])
 
         w_units = w.rearrange("e (a p j) n -> p (e a) (j n)", a=PASSES, j=4)
         bank_of = {e: (b, i) for b, es in enumerate(BANK_EXPERTS) for i, e in enumerate(es)}
         firsts = [sum(CHUNKS[:i]) for i in range(len(CHUNKS))]
         quantised = {}
-        groups = {}
-        n_groups = (E + GROUP - 1) // GROUP
-        first_use = {g: g * GROUP * PASSES // 4 for g in range(n_groups)}
-        after = {first_use[g] - AHEAD: g for g in range(n_groups) if first_use[g] >= AHEAD}
-        region_of = {g: c % REGIONS for c, g in after.items()}
-
-        def gather_group(g):
-            first = g * GROUP * C
-            count = min(GROUP * C, SLOTS - first)
-            at = (region_of[g] if g in region_of else REGIONS + g) * REGION
-            late = []
-            for a in range(EARLY, PASSES):
-                t = ring.tile([P, GROUP * C], U32, name=f"late{a}_{g}", align_bytes=64, offset=at)
-                at += 4 * GROUP * C
-                gather(t[:, 0:count], words[a], first, count)
-                late.append(t)
-            ta = ring.tile([P, GROUP * C], U8, name=f"gba{g}", align_bytes=64, offset=at)
-            gather(ta[:, 0:count], bytes_a, first, count)
-            tb = ring.tile([P, GROUP * C], U8, name=f"gbb{g}", align_bytes=64, offset=at + GROUP * C)
-            gather(tb[:, 0:count], bytes_b, first, count)
-            groups[g] = (late, ta, tb)
 
         def interleave(eng, grp, raw, u0, u1, n0, n1):
             dst = grp[:, u0:u1, n0:n1, :].rearrange("p u (c i) t -> p u c t i", i=4)
@@ -119,17 +121,24 @@ def tile_moe_tk_lin_none_kernel(tc, xT, w, gate, offs, pos1, pos2, pos3, pos4, o
 
         def prepare(ci):
             unit, size = firsts[ci], CHUNKS[ci]
-            raw = wraw_pool.tile([P, 4, 4, N], F32, name="wraw")
-            nc.sync.dma_start(
-                raw[:, 0:size].rearrange("p u j n -> p u (j n)"), w_units[:, unit : unit + size, :]
+            raw_at = WRAW_AT[unit // 4 % PASSES] + unit % 4 * (RAW // 4)
+            if ci == SHIFT_AFTER:
+                raw_at = 2048
+            raw = arena.tile([P, size, 4, N], F32, name=f"wraw{ci}", align_bytes=64, offset=raw_at)
+            nc.sync.dma_start(raw[:].rearrange("p u j n -> p u (j n)"), w_units[:, unit : unit + size, :])
+            grp = arena.tile(
+                [P, 4, N, 4], BF16, name=f"wgrp{ci}", align_bytes=64, offset=GRP_AT + (ci % GRP_SLOTS) * GRP
             )
-            grp = ring.tile([P, 4, N, 4], BF16, name=f"wgrp{ci}", align_bytes=64, offset=(ci % REGIONS) * REGION)
-            if 1 < size < 4 or ci == len(CHUNKS) - 2:
-                shares = (("s", 0, size, 0, N),)
-            elif size < 4:
+            if size == 1:
                 shares = (("s", 0, size, 0, N // 2), ("v", 0, size, N // 2, N))
-            else:
+            elif ci >= HALF_FROM:
+                shares = (("s", 0, size // 2, 0, N), ("v", size // 2, size, 0, N))
+            elif ci < GPSIMD_UNTIL:
                 shares = (("s", 0, 3, 0, N), ("g", 3, 4, 0, N))
+            elif ci >= VECTOR_FROM:
+                shares = (("s", 0, 3, 0, N), ("v", 3, 4, 0, N))
+            else:
+                shares = (("s", 0, 4, 0, N),)
             for eng, u0, u1, n0, n1 in shares:
                 interleave(eng, grp, raw, u0, u1, n0, n1)
             codes = wq_pool.tile([P, 4 * N], U32, name="wcodes", align_bytes=64)
@@ -147,53 +156,53 @@ def tile_moe_tk_lin_none_kernel(tc, xT, w, gate, offs, pos1, pos2, pos3, pos4, o
             for u in range(size):
                 e, a = divmod(unit + u, PASSES)
                 b, i = bank_of[e]
-                g = e // GROUP
-                late, ta, tb = groups[g]
-                here = slice((e - g * GROUP) * C, (e - g * GROUP + 1) * C)
-                plane, k = (ta, 4 * a) if a < 4 else (tb, 0)
-                rhs = gwords_early[a][:, e * C : (e + 1) * C] if a < EARLY else late[a - EARLY][:, here]
+                here = slice(e * C, (e + 1) * C)
+                plane, k = (gbytes_a, 4 * (a - 1)) if a else (gbytes_b, 0)
                 nc.tensor.matmul_mx(
                     out=banks[b][:, i * C : (i + 1) * C],
                     lhsT=codes[:, u * N : (u + 1) * N].bitcast(FP8X4),
                     lhsT_scale=scales[:, u * N : (u + 1) * N],
-                    rhs=rhs.bitcast(FP8X4),
+                    rhs=gwords[a][:, here].bitcast(FP8X4),
                     rhs_scale=plane[k:P, here],
                     start=(a == 0),
                     stop=(a == PASSES - 1),
                 )
+
+        y = arena.tile([P, SLOTS], F32, name="y", align_bytes=64, offset=GRP_AT + (Y_AFTER - 2) * GRP)
 
         def evacuate(b):
             first = BANK_EXPERTS[b][0] * C
             width = len(BANK_EXPERTS[b]) * C
             nc.scalar.copy(y[:, first : first + width], banks[b][:, 0:width])
 
-        LAG = 3
-        EVAC_LAG = 5
         evac_at = {}
         for b, es in enumerate(BANK_EXPERTS):
             closed = max(i for i, f in enumerate(firsts) if f <= es[-1] * PASSES + PASSES - 1)
-            evac_at.setdefault(min(closed + LAG + (EVAC_LAG if b < 4 else 0), len(CHUNKS) + LAG - 1), []).append(b)
-        for g in range(n_groups):
-            if g not in region_of:
-                gather_group(g)
-        for ci in range(len(CHUNKS) + LAG):
+            evac_at.setdefault(max(closed + 1, Y_AFTER + 1), []).append(b)
+        for ci in range(SHIFT_AFTER + 1):
+            prepare(ci)
+        nc.gpsimd.memset(gbytes_b[:].bitcast(I32), 0)
+        nc.sync.dma_start(gbytes_b[0 : P - 16, :].bitcast(I32), gbytes_a[16:P, :].bitcast(I32))
+        for ci in range(SHIFT_AFTER):
+            multiply(ci)
+        for ci in range(SHIFT_AFTER + 1, len(CHUNKS) + 1):
             if ci < len(CHUNKS):
                 prepare(ci)
-            if ci in after:
-                gather_group(after[ci])
             if ci == 20:
                 for t, src in zip(pos_t, (pos1, pos2, pos3, pos4)):
                     nc.sync.dma_start(t[:], src)
             if ci == len(CHUNKS) - 1:
-                gate_t = xraw_pool.tile([P, 4, T], F32, name="xraw")
+                gate_t = arena.tile([P, 4, T], F32, name="gate_t", align_bytes=64, offset=GRP_AT + (GATE_AFTER - 2) % GRP_SLOTS * GRP)
                 for r in range(4):
                     nc.sync.dma_start(gate_t[:, r, :], gate[r])
-            if ci >= LAG:
-                multiply(ci - LAG)
+            multiply(ci - 1)
             for b in evac_at.get(ci, []):
                 evacuate(b)
 
-        prod = xraw_pool.tile([P, 4, T], F32, name="xraw")
+        prod = arena.tile([P, 4, T], F32, name="prod", align_bytes=64, offset=GRP_AT + 9 * GRP)
+        half = arena.tile([P, 2, T], F32, name="half", align_bytes=64, offset=GRP_AT + 12 * GRP)
+        res = arena.tile([P, T], F32, name="res", align_bytes=64, offset=GRP_AT + 14 * GRP)
+
         def weigh(r, lo, hi):
             nc.vector.tensor_tensor(
                 prod[:, r, lo:hi], y[:].indirect(pos_t[r][:, lo // 16 : hi // 16]), gate_t[:, r, lo:hi], MULT

@@ -21,24 +21,31 @@ ADD = mybir.AluOpType.add
 
 CHUNKS = [4] * 24 + [2, 1, 1]
 BANK_EXPERTS = [[0, 1, 2, 3], [4, 5, 6, 7], [8, 9, 10, 11], [12, 13, 14, 15], [16, 17, 18], [19]]
-GATHER = 480
-GPSIMD_UNTIL = 12
+GATHER = 512
+WINDOW = 704
+EARLY = 2
 VECTOR_FROM = 16
 HALF_FROM = 22
-Y_AFTER = 17
+Y_AFTER = 19
 GATE_AFTER = 22
 
 BIG = 4 * T * 4
 RAW = 4 * 4 * N * 4
 GRP = 4 * N * 4 * 2
 XGRP = T * 4 * 2
-GRP_SLOTS = 18
+RANGES = SLOTS // GATHER
+LATE = [(b, a) for b in range(RANGES) for a in range(EARLY, PASSES)]
+LATE_AFTER = {1 + j: j for j in range(len(LATE))}
 XRAW_AT = [0] + [a * BIG + XGRP for a in range(1, PASSES)]
-WRAW_AT = [BIG + XGRP - RAW] + XRAW_AT[1:]
-GRP_AT = PASSES * BIG + XGRP
-GW_AT = GRP_AT + GRP_SLOTS * GRP
-XGRP_AT = [BIG, GW_AT + 3 * BIG + 512, GW_AT + BIG, GW_AT + 4 * BIG + XGRP, GW_AT + 2 * BIG]
-SHIFT_AFTER = 5
+SPARE_AT = PASSES * BIG + XGRP
+WRAW_AT = [BIG + XGRP - RAW, XRAW_AT[1], SPARE_AT, XRAW_AT[2], XRAW_AT[3], SPARE_AT + RAW, XRAW_AT[4]]
+GW_AT = SPARE_AT + 2 * RAW
+Y_AT = GW_AT + EARLY * BIG
+GATE_AT = Y_AT + BIG
+PROD_AT = GATE_AT + BIG
+LATE_AT = PROD_AT + BIG
+XGRP_AT = [BIG, SPARE_AT, GW_AT + BIG, SPARE_AT + RAW, PROD_AT]
+SHIFT_AFTER = 11
 
 
 def tile_moe_tk_lin_none_kernel(tc, xT, w, gate, offs, pos1, pos2, pos3, pos4, out):
@@ -46,31 +53,36 @@ def tile_moe_tk_lin_none_kernel(tc, xT, w, gate, offs, pos1, pos2, pos3, pos4, o
     with ExitStack() as ctx:
         keep = ctx.enter_context(tc.tile_pool(name="keep", bufs=1))
         arena = ctx.enter_context(tc.tile_pool(name="arena", bufs=1))
-        wq_pool = ctx.enter_context(tc.tile_pool(name="wq", bufs=8))
+        wq_pool = ctx.enter_context(tc.tile_pool(name="wq", bufs=13))
         psum = ctx.enter_context(tc.psum_pool(name="psum", bufs=1))
 
         offs_t = keep.tile([P, SLOTS // 16], U16, name="offs_t")
         pos_t = [keep.tile([P, T // 16], U16, name=f"pos_t{r}") for r in range(4)]
 
-        words = [keep.tile([P, T], U32, name=f"words{a}", align_bytes=64) for a in range(PASSES)]
-        bytes_a = arena.tile([P, T], U8, name="bytes_a", align_bytes=64, offset=GW_AT + 4 * BIG - T // 2)
-        bytes_b = keep.tile([P, T], U8, name="bytes_b", align_bytes=64)
-        merged = arena.tile([P, T], U8, name="merged", align_bytes=64, offset=GW_AT + 3 * BIG - T // 2)
+        words = [keep.tile([P, WINDOW], U32, name=f"words{a}", align_bytes=64) for a in range(PASSES)]
+        bytes_a = keep.tile([P, WINDOW], U8, name="bytes_a", align_bytes=64)
+        bytes_b = keep.tile([P, WINDOW], U8, name="bytes_b", align_bytes=64)
+        merged = keep.tile([P, WINDOW], U8, name="merged", align_bytes=64)
         gwords = [
             arena.tile([P, SLOTS], U32, name=f"gwords{a}", align_bytes=64, offset=GW_AT + a * BIG)
-            for a in range(PASSES)
+            for a in range(EARLY)
         ]
         gbytes_a = keep.tile([P, SLOTS], U8, name="gbytes_a", align_bytes=64)
-        gbytes_b = arena.tile([P, SLOTS], U8, name="gbytes_b", align_bytes=64, offset=0)
+        gbytes_b = keep.tile([P, SLOTS], U8, name="gbytes_b", align_bytes=64)
         banks = [psum.tile([P, 512], F32, name=f"bank{b}") for b in range(len(BANK_EXPERTS))]
 
         nc.gpsimd.memset(bytes_b[:], 0)
         nc.gpsimd.memset(bytes_a[:], 0)
+        for a in range(PASSES):
+            nc.gpsimd.memset(words[a][:, T:WINDOW].bitcast(I32), 0)
+        nc.gpsimd.memset(gbytes_b[96:P, :].bitcast(I32), 0)
+
+        def gather(dst, src, b):
+            nc.vector.tensor_copy(dst, src[:].indirect(offs_t[:, b * GATHER // 16 : (b + 1) * GATHER // 16]))
 
         def gather_all(dst, src):
-            for s in range(0, SLOTS, GATHER):
-                c = min(GATHER, SLOTS - s)
-                nc.vector.tensor_copy(dst[:, s : s + c], src[:].indirect(offs_t[:, s // 16 : (s + c) // 16]))
+            for b in range(RANGES):
+                gather(dst[:, b * GATHER : (b + 1) * GATHER], src, b)
 
         for a in range(PASSES):
             raw = arena.tile([P, 4, T], F32, name=f"xraw{a}", align_bytes=64, offset=XRAW_AT[a])
@@ -94,81 +106,104 @@ def tile_moe_tk_lin_none_kernel(tc, xT, w, gate, offs, pos1, pos2, pos3, pos4, o
                     in_=flat[:, 4 * lo : 4 * hi],
                 )
             if a == 0:
-                nc.sync.dma_start(merged[16:P, :].bitcast(I32), bytes_b[0 : P - 16, :].bitcast(I32))
                 gather_all(gwords[0], words[0])
             if a == 2:
                 gather_all(gwords[1], words[1])
+        nc.sync.dma_start(merged[16:P, :].bitcast(I32), bytes_b[0 : P - 16, :].bitcast(I32))
         for q in range(0, P, 32):
             nc.vector.tensor_copy(merged[q : q + 16, :].bitcast(I32), bytes_a[q : q + 16, :].bitcast(I32))
         gather_all(gbytes_a, merged)
-        for a in range(2, PASSES):
-            gather_all(gwords[a], words[a])
 
         w_units = w.rearrange("e (a p j) n -> p (e a) (j n)", a=PASSES, j=4)
         bank_of = {e: (b, i) for b, es in enumerate(BANK_EXPERTS) for i, e in enumerate(es)}
         firsts = [sum(CHUNKS[:i]) for i in range(len(CHUNKS))]
         quantised = {}
+        late = {}
 
-        def interleave(eng, grp, raw, u0, u1, n0, n1):
-            dst = grp[:, u0:u1, n0:n1, :].rearrange("p u (c i) t -> p u c t i", i=4)
+        def grp_at(ci):
+            if ci in LATE_AFTER:
+                return LATE_AT + LATE_AFTER[ci] * GRP
+            if ci in (0, Y_AFTER):
+                return Y_AT
+            if ci == GATE_AFTER:
+                return GATE_AT
+            if ci < GATE_AFTER:
+                return LATE_AT + (ci - len(LATE) - 1) * 2 * GRP + GRP // 2
+            return PROD_AT + sum(widths[23:ci]) * (GRP // 4)
+
+        def interleave(eng, grp, raw, to, u0, u1, n0, n1):
+            dst = grp[:, to : to + u1 - u0, n0:n1, :].rearrange("p u (c i) t -> p u c t i", i=4)
             src = raw[:, u0:u1, :, n0:n1].rearrange("p u t (c i) -> p u c t i", i=4)
             if eng == "s":
                 nc.scalar.copy(dst, src)
-            elif eng == "g":
-                nc.gpsimd.tensor_scalar(dst, src, 1.0, 0.0, MULT, ADD)
             else:
                 nc.vector.tensor_copy(dst, src)
 
+        deferred = [0 if ci < VECTOR_FROM or s < 4 else 1 if ci < HALF_FROM else 2 for ci, s in enumerate(CHUNKS)]
+        carried = [0] + deferred[:-1]
+        widths = [s + c - d for s, c, d in zip(CHUNKS, carried, deferred)]
+        grps = {}
+
+        def grp_of(ci):
+            if ci not in grps:
+                grps[ci] = arena.tile([P, widths[ci], N, 4], BF16, name=f"wgrp{ci}", align_bytes=64, offset=grp_at(ci))
+            return grps[ci]
+
         def prepare(ci):
             unit, size = firsts[ci], CHUNKS[ci]
-            raw_at = WRAW_AT[unit // 4 % PASSES] + unit % 4 * (RAW // 4)
-            if ci == SHIFT_AFTER:
-                raw_at = 2048
+            raw_at = WRAW_AT[unit // 4 % len(WRAW_AT)] + unit % 4 * (RAW // 4)
             raw = arena.tile([P, size, 4, N], F32, name=f"wraw{ci}", align_bytes=64, offset=raw_at)
             nc.sync.dma_start(raw[:].rearrange("p u j n -> p u (j n)"), w_units[:, unit : unit + size, :])
-            grp = arena.tile(
-                [P, 4, N, 4], BF16, name=f"wgrp{ci}", align_bytes=64, offset=GRP_AT + (ci % GRP_SLOTS) * GRP
-            )
+            grp = grp_of(ci)
+            at = carried[ci]
             if size == 1:
-                shares = (("s", 0, size, 0, N // 2), ("v", 0, size, N // 2, N))
-            elif ci >= HALF_FROM:
-                shares = (("s", 0, size // 2, 0, N), ("v", size // 2, size, 0, N))
-            elif ci < GPSIMD_UNTIL:
-                shares = (("s", 0, 3, 0, N), ("g", 3, 4, 0, N))
-            elif ci >= VECTOR_FROM:
-                shares = (("s", 0, 3, 0, N), ("v", 3, 4, 0, N))
+                interleave("s", grp, raw, at, 0, 1, 0, N // 2)
+                interleave("v", grp, raw, at, 0, 1, N // 2, N)
+            elif size == 2:
+                interleave("s", grp, raw, at, 0, 1, 0, N)
+                interleave("v", grp, raw, at + 1, 1, 2, 0, N)
             else:
-                shares = (("s", 0, 4, 0, N),)
-            for eng, u0, u1, n0, n1 in shares:
-                interleave(eng, grp, raw, u0, u1, n0, n1)
+                interleave("s", grp, raw, at, 0, size - deferred[ci], 0, N)
+                if deferred[ci]:
+                    interleave("v", grp_of(ci + 1), raw, 0, size - deferred[ci], size, 0, N)
             codes = wq_pool.tile([P, 4 * N], U32, name="wcodes", align_bytes=64)
             scales = wq_pool.tile([P, 4 * N], U8, name="wscales", align_bytes=64)
-            nc.vector.quantize_mx(
-                out=codes[:, 0 : size * N].bitcast(FP8X4),
-                scales=scales[:, 0 : size * N],
-                in_=grp[:, 0:size].rearrange("p u n j -> p (u n j)"),
-            )
+            for u0, u1 in ((0, 1), (1, 3)) if widths[ci] == 3 else ((0, widths[ci]),):
+                nc.vector.quantize_mx(
+                    out=codes[:, u0 * N : u1 * N].bitcast(FP8X4),
+                    scales=scales[:, u0 * N : u1 * N],
+                    in_=grp[:, u0:u1].rearrange("p u n j -> p (u n j)"),
+                )
             quantised[ci] = (codes, scales)
+            if ci in LATE_AFTER:
+                b, a = LATE[LATE_AFTER[ci]]
+                late_at = grp_at(ci) + LATE_AFTER[ci] % 2 * (GRP // 2)
+                late[b, a] = arena.tile([P, GATHER], U32, name=f"late{b}_{a}", align_bytes=64, offset=late_at)
+                gather(late[b, a][:], words[a], b)
 
         def multiply(ci):
-            unit, size = firsts[ci], CHUNKS[ci]
+            unit, size = firsts[ci] - carried[ci], widths[ci]
             codes, scales = quantised.pop(ci)
             for u in range(size):
                 e, a = divmod(unit + u, PASSES)
                 b, i = bank_of[e]
                 here = slice(e * C, (e + 1) * C)
                 plane, k = (gbytes_a, 4 * (a - 1)) if a else (gbytes_b, 0)
+                if a < EARLY:
+                    rhs = gwords[a][:, here]
+                else:
+                    rhs = late[e * C // GATHER, a][:, e * C % GATHER : e * C % GATHER + C]
                 nc.tensor.matmul_mx(
                     out=banks[b][:, i * C : (i + 1) * C],
                     lhsT=codes[:, u * N : (u + 1) * N].bitcast(FP8X4),
                     lhsT_scale=scales[:, u * N : (u + 1) * N],
-                    rhs=gwords[a][:, here].bitcast(FP8X4),
+                    rhs=rhs.bitcast(FP8X4),
                     rhs_scale=plane[k:P, here],
                     start=(a == 0),
                     stop=(a == PASSES - 1),
                 )
 
-        y = arena.tile([P, SLOTS], F32, name="y", align_bytes=64, offset=GRP_AT + (Y_AFTER - 2) * GRP)
+        y = arena.tile([P, SLOTS], F32, name="y", align_bytes=64, offset=Y_AT)
 
         def evacuate(b):
             first = BANK_EXPERTS[b][0] * C
@@ -177,11 +212,10 @@ def tile_moe_tk_lin_none_kernel(tc, xT, w, gate, offs, pos1, pos2, pos3, pos4, o
 
         evac_at = {}
         for b, es in enumerate(BANK_EXPERTS):
-            closed = max(i for i, f in enumerate(firsts) if f <= es[-1] * PASSES + PASSES - 1)
+            closed = max(i for i, f in enumerate(firsts) if f - carried[i] <= es[-1] * PASSES + PASSES - 1)
             evac_at.setdefault(max(closed + 1, Y_AFTER + 1), []).append(b)
         for ci in range(SHIFT_AFTER + 1):
             prepare(ci)
-        nc.gpsimd.memset(gbytes_b[:].bitcast(I32), 0)
         nc.sync.dma_start(gbytes_b[0 : P - 16, :].bitcast(I32), gbytes_a[16:P, :].bitcast(I32))
         for ci in range(SHIFT_AFTER):
             multiply(ci)
@@ -192,16 +226,16 @@ def tile_moe_tk_lin_none_kernel(tc, xT, w, gate, offs, pos1, pos2, pos3, pos4, o
                 for t, src in zip(pos_t, (pos1, pos2, pos3, pos4)):
                     nc.sync.dma_start(t[:], src)
             if ci == len(CHUNKS) - 1:
-                gate_t = arena.tile([P, 4, T], F32, name="gate_t", align_bytes=64, offset=GRP_AT + (GATE_AFTER - 2) % GRP_SLOTS * GRP)
+                gate_t = arena.tile([P, 4, T], F32, name="gate_t", align_bytes=64, offset=GATE_AT)
                 for r in range(4):
                     nc.sync.dma_start(gate_t[:, r, :], gate[r])
             multiply(ci - 1)
             for b in evac_at.get(ci, []):
                 evacuate(b)
 
-        prod = arena.tile([P, 4, T], F32, name="prod", align_bytes=64, offset=GRP_AT + 9 * GRP)
-        half = arena.tile([P, 2, T], F32, name="half", align_bytes=64, offset=GRP_AT + 12 * GRP)
-        res = arena.tile([P, T], F32, name="res", align_bytes=64, offset=GRP_AT + 14 * GRP)
+        prod = arena.tile([P, 4, T], F32, name="prod", align_bytes=64, offset=PROD_AT)
+        half = arena.tile([P, 2, T], F32, name="half", align_bytes=64, offset=XRAW_AT[4])
+        res = arena.tile([P, T], F32, name="res", align_bytes=64, offset=XRAW_AT[4] + XGRP)
 
         def weigh(r, lo, hi):
             nc.vector.tensor_tensor(

@@ -1,6 +1,7 @@
 from contextlib import ExitStack
 
 import concourse.mybir as mybir
+from concourse.masks import make_identity
 
 K, T, E, C, N = 2560, 640, 20, 128, 128
 SLOTS = E * C
@@ -19,14 +20,13 @@ FP8X4 = mybir.dt.float8_e4m3fn_x4
 MULT = mybir.AluOpType.mult
 ADD = mybir.AluOpType.add
 
-CHUNKS = [4] * 24 + [2, 1, 1]
+CHUNKS = [4] * 23 + [2, 2, 2, 1, 1]
 BANK_EXPERTS = [[0, 1, 2, 3], [4, 5, 6, 7], [8, 9, 10, 11], [12, 13, 14, 15], [16, 17, 18], [19]]
 GATHER = 512
 WINDOW = 704
 EARLY = 2
-VECTOR_FROM = 16
-HALF_FROM = 22
-Y_AFTER = 19
+VECTOR_FROM = 19
+Y_AFTER = 17
 GATE_AFTER = 22
 
 BIG = 4 * T * 4
@@ -45,7 +45,7 @@ GATE_AT = Y_AT + BIG
 PROD_AT = GATE_AT + BIG
 LATE_AT = PROD_AT + BIG
 XGRP_AT = [BIG, SPARE_AT, GW_AT + BIG, SPARE_AT + RAW, PROD_AT]
-SHIFT_AFTER = 11
+FIRST_MULTIPLY = 3
 
 
 def tile_moe_tk_lin_none_kernel(tc, xT, w, gate, offs, pos1, pos2, pos3, pos4, out):
@@ -53,7 +53,7 @@ def tile_moe_tk_lin_none_kernel(tc, xT, w, gate, offs, pos1, pos2, pos3, pos4, o
     with ExitStack() as ctx:
         keep = ctx.enter_context(tc.tile_pool(name="keep", bufs=1))
         arena = ctx.enter_context(tc.tile_pool(name="arena", bufs=1))
-        wq_pool = ctx.enter_context(tc.tile_pool(name="wq", bufs=13))
+        wq_pool = ctx.enter_context(tc.tile_pool(name="wq", bufs=8))
         psum = ctx.enter_context(tc.psum_pool(name="psum", bufs=1))
 
         offs_t = keep.tile([P, SLOTS // 16], U16, name="offs_t")
@@ -62,7 +62,6 @@ def tile_moe_tk_lin_none_kernel(tc, xT, w, gate, offs, pos1, pos2, pos3, pos4, o
         words = [keep.tile([P, WINDOW], U32, name=f"words{a}", align_bytes=64) for a in range(PASSES)]
         bytes_a = keep.tile([P, WINDOW], U8, name="bytes_a", align_bytes=64)
         bytes_b = keep.tile([P, WINDOW], U8, name="bytes_b", align_bytes=64)
-        merged = keep.tile([P, WINDOW], U8, name="merged", align_bytes=64)
         gwords = [
             arena.tile([P, SLOTS], U32, name=f"gwords{a}", align_bytes=64, offset=GW_AT + a * BIG)
             for a in range(EARLY)
@@ -75,7 +74,8 @@ def tile_moe_tk_lin_none_kernel(tc, xT, w, gate, offs, pos1, pos2, pos3, pos4, o
         nc.gpsimd.memset(bytes_a[:], 0)
         for a in range(PASSES):
             nc.gpsimd.memset(words[a][:, T:WINDOW].bitcast(I32), 0)
-        nc.gpsimd.memset(gbytes_b[96:P, :].bitcast(I32), 0)
+        ident = keep.tile([P, P], F32, name="ident")
+        make_identity(nc, ident[:])
 
         def gather(dst, src, b):
             nc.vector.tensor_copy(dst, src[:].indirect(offs_t[:, b * GATHER // 16 : (b + 1) * GATHER // 16]))
@@ -98,7 +98,7 @@ def tile_moe_tk_lin_none_kernel(tc, xT, w, gate, offs, pos1, pos2, pos3, pos4, o
                 else:
                     nc.vector.tensor_copy(dst, src)
             flat = grp[:].rearrange("p t j -> p (t j)")
-            plane, k = (bytes_a, 4 * (a - 1)) if a else (bytes_b, 0)
+            plane, k = (bytes_a, 4 * a) if a < 4 else (bytes_b, 0)
             for lo, hi in ((0, 512), (512, 640)):
                 nc.vector.quantize_mx(
                     out=words[a][:, lo:hi].bitcast(FP8X4),
@@ -109,10 +109,8 @@ def tile_moe_tk_lin_none_kernel(tc, xT, w, gate, offs, pos1, pos2, pos3, pos4, o
                 gather_all(gwords[0], words[0])
             if a == 2:
                 gather_all(gwords[1], words[1])
-        nc.sync.dma_start(merged[16:P, :].bitcast(I32), bytes_b[0 : P - 16, :].bitcast(I32))
-        for q in range(0, P, 32):
-            nc.vector.tensor_copy(merged[q : q + 16, :].bitcast(I32), bytes_a[q : q + 16, :].bitcast(I32))
-        gather_all(gbytes_a, merged)
+        gather_all(gbytes_a, bytes_a)
+        gather_all(gbytes_b, bytes_b)
 
         w_units = w.rearrange("e (a p j) n -> p (e a) (j n)", a=PASSES, j=4)
         bank_of = {e: (b, i) for b, es in enumerate(BANK_EXPERTS) for i, e in enumerate(es)}
@@ -123,7 +121,7 @@ def tile_moe_tk_lin_none_kernel(tc, xT, w, gate, offs, pos1, pos2, pos3, pos4, o
         def grp_at(ci):
             if ci in LATE_AFTER:
                 return LATE_AT + LATE_AFTER[ci] * GRP
-            if ci in (0, Y_AFTER):
+            if ci == 0:
                 return Y_AT
             if ci == GATE_AFTER:
                 return GATE_AT
@@ -139,7 +137,7 @@ def tile_moe_tk_lin_none_kernel(tc, xT, w, gate, offs, pos1, pos2, pos3, pos4, o
             else:
                 nc.vector.tensor_copy(dst, src)
 
-        deferred = [0 if ci < VECTOR_FROM or s < 4 else 1 if ci < HALF_FROM else 2 for ci, s in enumerate(CHUNKS)]
+        deferred = [1 if ci >= VECTOR_FROM and s > 1 else 0 for ci, s in enumerate(CHUNKS)]
         carried = [0] + deferred[:-1]
         widths = [s + c - d for s, c, d in zip(CHUNKS, carried, deferred)]
         grps = {}
@@ -152,6 +150,8 @@ def tile_moe_tk_lin_none_kernel(tc, xT, w, gate, offs, pos1, pos2, pos3, pos4, o
         def prepare(ci):
             unit, size = firsts[ci], CHUNKS[ci]
             raw_at = WRAW_AT[unit // 4 % len(WRAW_AT)] + unit % 4 * (RAW // 4)
+            if ci == Y_AFTER:
+                raw_at = Y_AT
             raw = arena.tile([P, size, 4, N], F32, name=f"wraw{ci}", align_bytes=64, offset=raw_at)
             nc.sync.dma_start(raw[:].rearrange("p u j n -> p u (j n)"), w_units[:, unit : unit + size, :])
             grp = grp_of(ci)
@@ -159,9 +159,6 @@ def tile_moe_tk_lin_none_kernel(tc, xT, w, gate, offs, pos1, pos2, pos3, pos4, o
             if size == 1:
                 interleave("s", grp, raw, at, 0, 1, 0, N // 2)
                 interleave("v", grp, raw, at, 0, 1, N // 2, N)
-            elif size == 2:
-                interleave("s", grp, raw, at, 0, 1, 0, N)
-                interleave("v", grp, raw, at + 1, 1, 2, 0, N)
             else:
                 interleave("s", grp, raw, at, 0, size - deferred[ci], 0, N)
                 if deferred[ci]:
@@ -188,7 +185,7 @@ def tile_moe_tk_lin_none_kernel(tc, xT, w, gate, offs, pos1, pos2, pos3, pos4, o
                 e, a = divmod(unit + u, PASSES)
                 b, i = bank_of[e]
                 here = slice(e * C, (e + 1) * C)
-                plane, k = (gbytes_a, 4 * (a - 1)) if a else (gbytes_b, 0)
+                plane, k = (gbytes_a, 4 * a) if a < 4 else (gbytes_b, 0)
                 if a < EARLY:
                     rhs = gwords[a][:, here]
                 else:
@@ -213,13 +210,12 @@ def tile_moe_tk_lin_none_kernel(tc, xT, w, gate, offs, pos1, pos2, pos3, pos4, o
         evac_at = {}
         for b, es in enumerate(BANK_EXPERTS):
             closed = max(i for i, f in enumerate(firsts) if f - carried[i] <= es[-1] * PASSES + PASSES - 1)
-            evac_at.setdefault(max(closed + 1, Y_AFTER + 1), []).append(b)
-        for ci in range(SHIFT_AFTER + 1):
+            evac_at.setdefault(max(closed + 1, Y_AFTER + 1 + b), []).append(b)
+        for ci in range(FIRST_MULTIPLY + 1):
             prepare(ci)
-        nc.sync.dma_start(gbytes_b[0 : P - 16, :].bitcast(I32), gbytes_a[16:P, :].bitcast(I32))
-        for ci in range(SHIFT_AFTER):
+        for ci in range(FIRST_MULTIPLY):
             multiply(ci)
-        for ci in range(SHIFT_AFTER + 1, len(CHUNKS) + 1):
+        for ci in range(FIRST_MULTIPLY + 1, len(CHUNKS) + 1):
             if ci < len(CHUNKS):
                 prepare(ci)
             if ci == 20:
@@ -227,8 +223,8 @@ def tile_moe_tk_lin_none_kernel(tc, xT, w, gate, offs, pos1, pos2, pos3, pos4, o
                     nc.sync.dma_start(t[:], src)
             if ci == len(CHUNKS) - 1:
                 gate_t = arena.tile([P, 4, T], F32, name="gate_t", align_bytes=64, offset=GATE_AT)
-                for r in range(4):
-                    nc.sync.dma_start(gate_t[:, r, :], gate[r])
+                for lo, hi in ((0, 2 * P), (2 * P, T)):
+                    nc.sync.dma_start(gate_t[:, :, lo:hi], gate[:, :, lo:hi].rearrange("r n t -> n r t"))
             multiply(ci - 1)
             for b in evac_at.get(ci, []):
                 evacuate(b)
@@ -242,21 +238,32 @@ def tile_moe_tk_lin_none_kernel(tc, xT, w, gate, offs, pos1, pos2, pos3, pos4, o
                 prod[:, r, lo:hi], y[:].indirect(pos_t[r][:, lo // 16 : hi // 16]), gate_t[:, r, lo:hi], MULT
             )
 
-        def add_pairs(lo, hi):
-            nc.vector.tensor_add(half[:, :, lo:hi], prod[:, 0:2, lo:hi], prod[:, 2:4, lo:hi])
+        for piece in range(2):
+            lo = 2 * piece * P
+            for r in range(4):
+                weigh(r, lo, lo + 2 * P)
+                for i in range(2):
+                    nc.tensor.matmul(
+                        banks[2 * piece + i][:, 0:P],
+                        lhsT=prod[:, r, lo + i * P : lo + (i + 1) * P],
+                        rhs=ident[:],
+                        is_transpose=True,
+                        start=(r == 0),
+                        stop=(r == 3),
+                    )
+            back = psum.tile([P, 512], F32, name=f"back{piece}")
+            for i in range(2):
+                turned = half[:, piece, i * P : (i + 1) * P]
+                nc.scalar.copy(turned, banks[2 * piece + i][:, 0:P])
+                nc.tensor.transpose(back[:, i * P : (i + 1) * P], turned, ident[:])
+            nc.scalar.copy(res[:, lo : lo + 2 * P], back[:, 0 : 2 * P])
+            nc.sync.dma_start(out[:, lo : lo + 2 * P], res[:, lo : lo + 2 * P])
 
-        def finish(lo, hi):
-            nc.vector.tensor_add(res[:, lo:hi], half[:, 0, lo:hi], half[:, 1, lo:hi])
-            nc.sync.dma_start(out[:, lo:hi], res[:, lo:hi])
-
-        CUT = 384
-        for r in range(4):
-            weigh(r, 0, CUT)
-        weigh(0, CUT, T)
-        add_pairs(0, CUT)
-        weigh(1, CUT, T)
-        finish(0, CUT)
-        weigh(2, CUT, T)
-        weigh(3, CUT, T)
-        add_pairs(CUT, T)
-        finish(CUT, T)
+        lo = 4 * P
+        for r in range(3):
+            weigh(r, lo, T)
+        nc.vector.tensor_add(half[:, 0, lo:T], prod[:, 0, lo:T], prod[:, 1, lo:T])
+        weigh(3, lo, T)
+        nc.vector.tensor_add(half[:, 1, lo:T], half[:, 0, lo:T], prod[:, 2, lo:T])
+        nc.vector.tensor_add(res[:, lo:T], half[:, 1, lo:T], prod[:, 3, lo:T])
+        nc.sync.dma_start(out[:, lo:T], res[:, lo:T])

@@ -134,6 +134,8 @@ def tile_moe_tk_lin_none_kernel(tc, xT, w, gate, offs, pos1, pos2, pos3, pos4, o
             src = raw[:, u0:u1, :, n0:n1].rearrange("p u t (c i) -> p u c t i", i=4)
             if eng == "s":
                 nc.scalar.copy(dst, src)
+            elif eng == "g":
+                nc.gpsimd.tensor_scalar(dst, src, 1.0, 0.0, MULT, ADD)
             else:
                 nc.vector.tensor_copy(dst, src)
 
@@ -147,22 +149,34 @@ def tile_moe_tk_lin_none_kernel(tc, xT, w, gate, offs, pos1, pos2, pos3, pos4, o
                 grps[ci] = arena.tile([P, widths[ci], N, 4], BF16, name=f"wgrp{ci}", align_bytes=64, offset=grp_at(ci))
             return grps[ci]
 
-        def prepare(ci):
+        raws = {}
+
+        def load(ci):
             unit, size = firsts[ci], CHUNKS[ci]
             raw_at = WRAW_AT[unit // 4 % len(WRAW_AT)] + unit % 4 * (RAW // 4)
             if ci == Y_AFTER:
                 raw_at = Y_AT
             raw = arena.tile([P, size, 4, N], F32, name=f"wraw{ci}", align_bytes=64, offset=raw_at)
             nc.sync.dma_start(raw[:].rearrange("p u j n -> p u (j n)"), w_units[:, unit : unit + size, :])
+            raws[ci] = raw
+
+        def prepare(ci):
+            size, raw = CHUNKS[ci], raws.pop(ci)
             grp = grp_of(ci)
             at = carried[ci]
             if size == 1:
                 interleave("s", grp, raw, at, 0, 1, 0, N // 2)
                 interleave("v", grp, raw, at, 0, 1, N // 2, N)
+            elif ci < VECTOR_FROM and ci % 2 == 0:
+                interleave("s", grp, raw, at, 0, size - 1, 0, N)
+                interleave("g", grp, raw, at + size - 1, size - 1, size, 0, N)
             else:
                 interleave("s", grp, raw, at, 0, size - deferred[ci], 0, N)
                 if deferred[ci]:
                     interleave("v", grp_of(ci + 1), raw, 0, size - deferred[ci], size, 0, N)
+            for cj in range(ci + 1, len(CHUNKS)):
+                if firsts[cj] // 4 == ci + len(WRAW_AT):
+                    load(cj)
             codes = wq_pool.tile([P, 4 * N], U32, name="wcodes", align_bytes=64)
             scales = wq_pool.tile([P, 4 * N], U8, name="wscales", align_bytes=64)
             for u0, u1 in ((0, 1), (1, 3)) if widths[ci] == 3 else ((0, widths[ci]),):
@@ -211,6 +225,8 @@ def tile_moe_tk_lin_none_kernel(tc, xT, w, gate, offs, pos1, pos2, pos3, pos4, o
         for b, es in enumerate(BANK_EXPERTS):
             closed = max(i for i, f in enumerate(firsts) if f - carried[i] <= es[-1] * PASSES + PASSES - 1)
             evac_at.setdefault(max(closed + 1, Y_AFTER + 1 + b), []).append(b)
+        for ci in range(len(WRAW_AT)):
+            load(ci)
         for ci in range(FIRST_MULTIPLY + 1):
             prepare(ci)
         for ci in range(FIRST_MULTIPLY):
@@ -218,10 +234,9 @@ def tile_moe_tk_lin_none_kernel(tc, xT, w, gate, offs, pos1, pos2, pos3, pos4, o
         for ci in range(FIRST_MULTIPLY + 1, len(CHUNKS) + 1):
             if ci < len(CHUNKS):
                 prepare(ci)
-            if ci == 20:
+            if ci == len(CHUNKS) - 1:
                 for t, src in zip(pos_t, (pos1, pos2, pos3, pos4)):
                     nc.sync.dma_start(t[:], src)
-            if ci == len(CHUNKS) - 1:
                 gate_t = arena.tile([P, 4, T], F32, name="gate_t", align_bytes=64, offset=GATE_AT)
                 for lo, hi in ((0, 2 * P), (2 * P, T)):
                     nc.sync.dma_start(gate_t[:, :, lo:hi], gate[:, :, lo:hi].rearrange("r n t -> n r t"))

@@ -235,17 +235,20 @@ def tile_moe_tk_lin_none_kernel(tc, xT, w, gate, offs, pos1, pos2, pos3, pos4, o
             if ci < len(CHUNKS):
                 prepare(ci)
             if ci == len(CHUNKS) - 1:
-                for t, src in zip(pos_t, (pos1, pos2, pos3, pos4)):
-                    nc.sync.dma_start(t[:], src)
                 gate_t = arena.tile([P, 4, T], F32, name="gate_t", align_bytes=64, offset=GATE_AT)
-                for lo, hi in ((0, 2 * P), (2 * P, T)):
-                    nc.sync.dma_start(gate_t[:, :, lo:hi], gate[:, :, lo:hi].rearrange("r n t -> n r t"))
+                for r, src in enumerate((pos1, pos2, pos3, pos4)):
+                    nc.sync.dma_start(pos_t[r][:], src)
+                    if r % 2 == 1:
+                        pair = slice(r - 1, r + 1)
+                        nc.sync.dma_start(gate_t[:, pair, 0 : 2 * P], gate[pair, :, 0 : 2 * P].rearrange("r n t -> n r t"))
+                nc.sync.dma_start(gate_t[:, :, 2 * P : T], gate[:, :, 2 * P : T].rearrange("r n t -> n r t"))
             multiply(ci - 1)
             for b in evac_at.get(ci, []):
                 evacuate(b)
 
         prod = arena.tile([P, 4, T], F32, name="prod", align_bytes=64, offset=PROD_AT)
         half = arena.tile([P, 2, T], F32, name="half", align_bytes=64, offset=XRAW_AT[4])
+        turned = arena.tile([P, 4 * P], F32, name="turned", align_bytes=64, offset=XRAW_AT[4] + XGRP + T * 4)
         res = arena.tile([P, T], F32, name="res", align_bytes=64, offset=XRAW_AT[4] + XGRP)
 
         def weigh(r, lo, hi):
@@ -253,26 +256,33 @@ def tile_moe_tk_lin_none_kernel(tc, xT, w, gate, offs, pos1, pos2, pos3, pos4, o
                 prod[:, r, lo:hi], y[:].indirect(pos_t[r][:, lo // 16 : hi // 16]), gate_t[:, r, lo:hi], MULT
             )
 
-        for piece in range(2):
-            lo = 2 * piece * P
+        def add_turned(r, block):
+            nc.tensor.matmul(
+                banks[block][:, 0:P],
+                lhsT=prod[:, r, block * P : (block + 1) * P],
+                rhs=ident[:],
+                is_transpose=True,
+                start=(r == 0),
+                stop=(r == 3),
+            )
+
+        def turn_back(block):
+            cols = slice(block * P, (block + 1) * P)
+            back = psum.tile([P, P], F32, name=f"back{block % 2}")
+            nc.scalar.copy(turned[:, cols], banks[block][:, 0:P])
+            nc.tensor.transpose(back[:], turned[:, cols], ident[:])
+            nc.scalar.copy(res[:, cols], back[:])
+
+        for blocks in ((0, 1), (2,), (3,)):
             for r in range(4):
-                weigh(r, lo, lo + 2 * P)
-                for i in range(2):
-                    nc.tensor.matmul(
-                        banks[2 * piece + i][:, 0:P],
-                        lhsT=prod[:, r, lo + i * P : lo + (i + 1) * P],
-                        rhs=ident[:],
-                        is_transpose=True,
-                        start=(r == 0),
-                        stop=(r == 3),
-                    )
-            back = psum.tile([P, 512], F32, name=f"back{piece}")
-            for i in range(2):
-                turned = half[:, piece, i * P : (i + 1) * P]
-                nc.scalar.copy(turned, banks[2 * piece + i][:, 0:P])
-                nc.tensor.transpose(back[:, i * P : (i + 1) * P], turned, ident[:])
-            nc.scalar.copy(res[:, lo : lo + 2 * P], back[:, 0 : 2 * P])
-            nc.sync.dma_start(out[:, lo : lo + 2 * P], res[:, lo : lo + 2 * P])
+                weigh(r, blocks[0] * P, (blocks[-1] + 1) * P)
+                for block in blocks:
+                    add_turned(r, block)
+            for block in blocks:
+                turn_back(block)
+            if blocks[-1] % 2 == 1:
+                cols = slice((blocks[-1] - 1) * P, (blocks[-1] + 1) * P)
+                nc.sync.dma_start(out[:, cols], res[:, cols])
 
         lo = 4 * P
         for r in range(3):

@@ -63,7 +63,7 @@ def tile_moe_tk_lin_none_kernel(tc, xT, w, gate, offs, pos1, pos2, pos3, pos4, o
         bytes_a = keep.tile([P, WINDOW], U8, name="bytes_a", align_bytes=64)
         bytes_b = keep.tile([P, WINDOW], U8, name="bytes_b", align_bytes=64)
         gwords = [
-            arena.tile([P, SLOTS], U32, name=f"gwords{a}", align_bytes=64, offset=GW_AT + a * BIG)
+            arena.tile([P, SLOTS], U32, name=f"gwords{a}", align_bytes=256, offset=GW_AT + a * BIG)
             for a in range(EARLY)
         ]
         gbytes_a = keep.tile([P, SLOTS], U8, name="gbytes_a", align_bytes=64)
@@ -85,11 +85,11 @@ def tile_moe_tk_lin_none_kernel(tc, xT, w, gate, offs, pos1, pos2, pos3, pos4, o
                 gather(dst[:, b * GATHER : (b + 1) * GATHER], src, b)
 
         for a in range(PASSES):
-            raw = arena.tile([P, 4, T], F32, name=f"xraw{a}", align_bytes=64, offset=XRAW_AT[a])
+            raw = arena.tile([P, 4, T], F32, name=f"xraw{a}", align_bytes=256, offset=XRAW_AT[a])
             nc.sync.dma_start(raw[:], xT[512 * a : 512 * (a + 1), :].rearrange("(p j) t -> p j t", j=4))
             if a == 0:
                 nc.sync.dma_start(offs_t[:], offs)
-            grp = arena.tile([P, T, 4], BF16, name=f"xgrp{a}", align_bytes=64, offset=XGRP_AT[a])
+            grp = arena.tile([P, T, 4], BF16, name=f"xgrp{a}", align_bytes=256, offset=XGRP_AT[a])
             for lo, hi, eng in ((0, 256, "s"), (256, 640, "v")) if a == 0 else ((0, 640, "s"),):
                 dst = grp[:, lo:hi, :].rearrange("p (c i) t -> p c t i", i=4)
                 src = raw[:, :, lo:hi].rearrange("p t (c i) -> p c t i", i=4)
@@ -146,7 +146,7 @@ def tile_moe_tk_lin_none_kernel(tc, xT, w, gate, offs, pos1, pos2, pos3, pos4, o
 
         def grp_of(ci):
             if ci not in grps:
-                grps[ci] = arena.tile([P, widths[ci], N, 4], BF16, name=f"wgrp{ci}", align_bytes=64, offset=grp_at(ci))
+                grps[ci] = arena.tile([P, widths[ci], N, 4], BF16, name=f"wgrp{ci}", align_bytes=256, offset=grp_at(ci))
             return grps[ci]
 
         raws = {}
@@ -156,7 +156,7 @@ def tile_moe_tk_lin_none_kernel(tc, xT, w, gate, offs, pos1, pos2, pos3, pos4, o
             raw_at = WRAW_AT[unit // 4 % len(WRAW_AT)] + unit % 4 * (RAW // 4)
             if ci == Y_AFTER:
                 raw_at = Y_AT
-            raw = arena.tile([P, size, 4, N], F32, name=f"wraw{ci}", align_bytes=64, offset=raw_at)
+            raw = arena.tile([P, size, 4, N], F32, name=f"wraw{ci}", align_bytes=256, offset=raw_at)
             nc.sync.dma_start(raw[:].rearrange("p u j n -> p u (j n)"), w_units[:, unit : unit + size, :])
             raws[ci] = raw
 
@@ -189,7 +189,7 @@ def tile_moe_tk_lin_none_kernel(tc, xT, w, gate, offs, pos1, pos2, pos3, pos4, o
             if ci in LATE_AFTER:
                 b, a = LATE[LATE_AFTER[ci]]
                 late_at = grp_at(ci) + LATE_AFTER[ci] % 2 * (GRP // 2)
-                late[b, a] = arena.tile([P, GATHER], U32, name=f"late{b}_{a}", align_bytes=64, offset=late_at)
+                late[b, a] = arena.tile([P, GATHER], U32, name=f"late{b}_{a}", align_bytes=256, offset=late_at)
                 gather(late[b, a][:], words[a], b)
 
         def multiply(ci):
@@ -214,7 +214,7 @@ def tile_moe_tk_lin_none_kernel(tc, xT, w, gate, offs, pos1, pos2, pos3, pos4, o
                     stop=(a == PASSES - 1),
                 )
 
-        y = arena.tile([P, SLOTS], F32, name="y", align_bytes=64, offset=Y_AT)
+        y = arena.tile([P, SLOTS], F32, name="y", align_bytes=256, offset=Y_AT)
 
         def evacuate(b):
             first = BANK_EXPERTS[b][0] * C
@@ -235,7 +235,7 @@ def tile_moe_tk_lin_none_kernel(tc, xT, w, gate, offs, pos1, pos2, pos3, pos4, o
             if ci < len(CHUNKS):
                 prepare(ci)
             if ci == len(CHUNKS) - 1:
-                gate_t = arena.tile([P, 4, T], F32, name="gate_t", align_bytes=64, offset=GATE_AT)
+                gate_t = arena.tile([P, 4, T], F32, name="gate_t", align_bytes=256, offset=GATE_AT)
                 for r, src in enumerate((pos1, pos2, pos3, pos4)):
                     nc.sync.dma_start(pos_t[r][:], src)
                     if r % 2 == 1:
@@ -246,10 +246,10 @@ def tile_moe_tk_lin_none_kernel(tc, xT, w, gate, offs, pos1, pos2, pos3, pos4, o
             for b in evac_at.get(ci, []):
                 evacuate(b)
 
-        prod = arena.tile([P, 4, T], F32, name="prod", align_bytes=64, offset=PROD_AT)
-        half = arena.tile([P, 2, T], F32, name="half", align_bytes=64, offset=XRAW_AT[4])
-        turned = arena.tile([P, 4 * P], F32, name="turned", align_bytes=64, offset=XRAW_AT[4] + XGRP + T * 4)
-        res = arena.tile([P, T], F32, name="res", align_bytes=64, offset=XRAW_AT[4] + XGRP)
+        prod = arena.tile([P, 4, T], F32, name="prod", align_bytes=256, offset=PROD_AT)
+        half = arena.tile([P, 2, T], F32, name="half", align_bytes=256, offset=XRAW_AT[4])
+        turned = arena.tile([P, 4 * P], F32, name="turned", align_bytes=256, offset=XRAW_AT[4] + XGRP + T * 4)
+        res = arena.tile([P, T], F32, name="res", align_bytes=256, offset=XRAW_AT[4] + XGRP)
 
         def weigh(r, lo, hi):
             nc.vector.tensor_tensor(

@@ -7,7 +7,6 @@ K, T, E, C, N = 2560, 640, 20, 128, 128
 SLOTS = E * C
 P = 128
 PASSES = 5
-UNITS = E * PASSES
 FLOPS = 2 * SLOTS * K * N
 
 F32 = mybir.dt.float32
@@ -20,14 +19,21 @@ FP8X4 = mybir.dt.float8_e4m3fn_x4
 MULT = mybir.AluOpType.mult
 ADD = mybir.AluOpType.add
 
-CHUNKS = [4] * 23 + [2, 2, 2, 1, 1]
-BANK_EXPERTS = [[0, 1, 2, 3], [4, 5, 6, 7], [8, 9, 10, 11], [12, 13, 14, 15], [16, 17, 18], [19]]
+FULL_CHUNKS = 23
+CHUNKS = [4] * FULL_CHUNKS + [2, 2, 2, 1, 1]
+BANK_EXPERTS = [[0, 1, 2, 3], [4, 5, 6, 7], [8, 9, 10, 11], [12, 13, 14, 15], [16], [17, 18, 19]]
+VECTOR_BANK = 4
 GATHER = 512
 WINDOW = 704
 EARLY = 2
+WALK = 4
+X_SCALAR = 256
 VECTOR_FROM = 19
 Y_AFTER = 17
 GATE_AFTER = 22
+SPLIT = 384
+CODE_BUFFERS = 8
+FIRST_MULTIPLY = 3
 
 BIG = 4 * T * 4
 RAW = 4 * 4 * N * 4
@@ -45,7 +51,6 @@ GATE_AT = Y_AT + BIG
 PROD_AT = GATE_AT + BIG
 LATE_AT = PROD_AT + BIG
 XGRP_AT = [BIG, SPARE_AT, GW_AT + BIG, SPARE_AT + RAW, PROD_AT]
-FIRST_MULTIPLY = 3
 
 
 def tile_moe_tk_lin_none_kernel(tc, xT, w, gate, offs, pos1, pos2, pos3, pos4, out):
@@ -53,7 +58,7 @@ def tile_moe_tk_lin_none_kernel(tc, xT, w, gate, offs, pos1, pos2, pos3, pos4, o
     with ExitStack() as ctx:
         keep = ctx.enter_context(tc.tile_pool(name="keep", bufs=1))
         arena = ctx.enter_context(tc.tile_pool(name="arena", bufs=1))
-        wq_pool = ctx.enter_context(tc.tile_pool(name="wq", bufs=8))
+        wq_pool = ctx.enter_context(tc.tile_pool(name="wq", bufs=CODE_BUFFERS))
         psum = ctx.enter_context(tc.psum_pool(name="psum", bufs=1))
 
         offs_t = keep.tile([P, SLOTS // 16], U16, name="offs_t")
@@ -68,7 +73,7 @@ def tile_moe_tk_lin_none_kernel(tc, xT, w, gate, offs, pos1, pos2, pos3, pos4, o
         ]
         gbytes_a = keep.tile([P, SLOTS], U8, name="gbytes_a", align_bytes=64)
         gbytes_b = keep.tile([P, SLOTS], U8, name="gbytes_b", align_bytes=64)
-        banks = [psum.tile([P, 512], F32, name=f"bank{b}") for b in range(len(BANK_EXPERTS))]
+        banks = [psum.tile([P, 512], F32, name=f"bank{b}") for b in range(8)]
 
         nc.gpsimd.memset(bytes_b[:], 0)
         nc.gpsimd.memset(bytes_a[:], 0)
@@ -84,22 +89,29 @@ def tile_moe_tk_lin_none_kernel(tc, xT, w, gate, offs, pos1, pos2, pos3, pos4, o
             for b in range(RANGES):
                 gather(dst[:, b * GATHER : (b + 1) * GATHER], src, b)
 
+        def interleave(eng, dst, src):
+            if eng == "scalar":
+                nc.scalar.copy(dst, src)
+            elif eng == "gpsimd":
+                nc.gpsimd.tensor_scalar(dst, src, 1.0, 0.0, MULT, ADD)
+            else:
+                nc.vector.tensor_copy(dst, src)
+
         for a in range(PASSES):
             raw = arena.tile([P, 4, T], F32, name=f"xraw{a}", align_bytes=256, offset=XRAW_AT[a])
             nc.sync.dma_start(raw[:], xT[512 * a : 512 * (a + 1), :].rearrange("(p j) t -> p j t", j=4))
             if a == 0:
                 nc.sync.dma_start(offs_t[:], offs)
             grp = arena.tile([P, T, 4], BF16, name=f"xgrp{a}", align_bytes=256, offset=XGRP_AT[a])
-            for lo, hi, eng in ((0, 256, "s"), (256, 640, "v")) if a == 0 else ((0, 640, "s"),):
-                dst = grp[:, lo:hi, :].rearrange("p (c i) t -> p c t i", i=4)
-                src = raw[:, :, lo:hi].rearrange("p t (c i) -> p c t i", i=4)
-                if eng == "s":
-                    nc.scalar.copy(dst, src)
-                else:
-                    nc.vector.tensor_copy(dst, src)
+            for lo, hi, eng in ((0, X_SCALAR, "scalar"), (X_SCALAR, T, "vector")) if a == 0 else ((0, T, "scalar"),):
+                interleave(
+                    eng,
+                    grp[:, lo:hi, :].rearrange("p (c i) t -> p c t i", i=WALK),
+                    raw[:, :, lo:hi].rearrange("p t (c i) -> p c t i", i=WALK),
+                )
             flat = grp[:].rearrange("p t j -> p (t j)")
             plane, k = (bytes_a, 4 * a) if a < 4 else (bytes_b, 0)
-            for lo, hi in ((0, 512), (512, 640)):
+            for lo, hi in ((0, 512), (512, T)):
                 nc.vector.quantize_mx(
                     out=words[a][:, lo:hi].bitcast(FP8X4),
                     scales=plane[k:P, lo:hi],
@@ -112,7 +124,7 @@ def tile_moe_tk_lin_none_kernel(tc, xT, w, gate, offs, pos1, pos2, pos3, pos4, o
         gather_all(gbytes_a, bytes_a)
         gather_all(gbytes_b, bytes_b)
 
-        w_units = w.rearrange("e (a p j) n -> p (e a) (j n)", a=PASSES, j=4)
+        w_slabs = w.rearrange("e (a p j) n -> p (e a) (j n)", a=PASSES, j=4)
         bank_of = {e: (b, i) for b, es in enumerate(BANK_EXPERTS) for i, e in enumerate(es)}
         firsts = [sum(CHUNKS[:i]) for i in range(len(CHUNKS))]
         quantised = {}
@@ -127,18 +139,16 @@ def tile_moe_tk_lin_none_kernel(tc, xT, w, gate, offs, pos1, pos2, pos3, pos4, o
                 return GATE_AT
             if ci < GATE_AFTER:
                 return LATE_AT + (ci - len(LATE) - 1) * 2 * GRP + GRP // 2
-            return PROD_AT + sum(widths[23:ci]) * (GRP // 4)
+            return PROD_AT + sum(widths[FULL_CHUNKS:ci]) * (GRP // 4)
 
-        def interleave(eng, grp, raw, to, u0, u1, n0, n1):
-            dst = grp[:, to : to + u1 - u0, n0:n1, :].rearrange("p u (c i) t -> p u c t i", i=4)
-            src = raw[:, u0:u1, :, n0:n1].rearrange("p u t (c i) -> p u c t i", i=4)
-            if eng == "s":
-                nc.scalar.copy(dst, src)
-            elif eng == "g":
-                nc.gpsimd.tensor_scalar(dst, src, 1.0, 0.0, MULT, ADD)
-            else:
-                nc.vector.tensor_copy(dst, src)
+        def round_slabs(eng, grp, to, raw, u0, u1):
+            interleave(
+                eng,
+                grp[:, to : to + u1 - u0].rearrange("p u (c i) t -> p u c t i", i=WALK),
+                raw[:, u0:u1].rearrange("p u t (c i) -> p u c t i", i=WALK),
+            )
 
+        last = len(CHUNKS) - 1
         deferred = [1 if ci >= VECTOR_FROM and s > 1 else 0 for ci, s in enumerate(CHUNKS)]
         carried = [0] + deferred[:-1]
         widths = [s + c - d for s, c, d in zip(CHUNKS, carried, deferred)]
@@ -152,28 +162,27 @@ def tile_moe_tk_lin_none_kernel(tc, xT, w, gate, offs, pos1, pos2, pos3, pos4, o
         raws = {}
 
         def load(ci):
-            unit, size = firsts[ci], CHUNKS[ci]
-            raw_at = WRAW_AT[unit // 4 % len(WRAW_AT)] + unit % 4 * (RAW // 4)
+            slab, size = firsts[ci], CHUNKS[ci]
+            raw_at = WRAW_AT[slab // 4 % len(WRAW_AT)] + slab % 4 * (RAW // 4)
             if ci == Y_AFTER:
                 raw_at = Y_AT
             raw = arena.tile([P, size, 4, N], F32, name=f"wraw{ci}", align_bytes=256, offset=raw_at)
-            nc.sync.dma_start(raw[:].rearrange("p u j n -> p u (j n)"), w_units[:, unit : unit + size, :])
+            nc.sync.dma_start(raw[:].rearrange("p u j n -> p u (j n)"), w_slabs[:, slab : slab + size, :])
             raws[ci] = raw
 
         def prepare(ci):
             size, raw = CHUNKS[ci], raws.pop(ci)
             grp = grp_of(ci)
             at = carried[ci]
-            if size == 1:
-                interleave("s", grp, raw, at, 0, 1, 0, N // 2)
-                interleave("v", grp, raw, at, 0, 1, N // 2, N)
+            if ci == last:
+                round_slabs("vector", grp, at, raw, 0, size)
             elif ci < VECTOR_FROM and ci % 2 == 0:
-                interleave("s", grp, raw, at, 0, size - 1, 0, N)
-                interleave("g", grp, raw, at + size - 1, size - 1, size, 0, N)
+                round_slabs("scalar", grp, at, raw, 0, size - 1)
+                round_slabs("gpsimd", grp, at + size - 1, raw, size - 1, size)
             else:
-                interleave("s", grp, raw, at, 0, size - deferred[ci], 0, N)
+                round_slabs("scalar", grp, at, raw, 0, size - deferred[ci])
                 if deferred[ci]:
-                    interleave("v", grp_of(ci + 1), raw, 0, size - deferred[ci], size, 0, N)
+                    round_slabs("vector", grp_of(ci + 1), 0, raw, size - deferred[ci], size)
             for cj in range(ci + 1, len(CHUNKS)):
                 if firsts[cj] // 4 == ci + len(WRAW_AT):
                     load(cj)
@@ -193,10 +202,10 @@ def tile_moe_tk_lin_none_kernel(tc, xT, w, gate, offs, pos1, pos2, pos3, pos4, o
                 gather(late[b, a][:], words[a], b)
 
         def multiply(ci):
-            unit, size = firsts[ci] - carried[ci], widths[ci]
+            slab, size = firsts[ci] - carried[ci], widths[ci]
             codes, scales = quantised.pop(ci)
             for u in range(size):
-                e, a = divmod(unit + u, PASSES)
+                e, a = divmod(slab + u, PASSES)
                 b, i = bank_of[e]
                 here = slice(e * C, (e + 1) * C)
                 plane, k = (gbytes_a, 4 * a) if a < 4 else (gbytes_b, 0)
@@ -219,7 +228,10 @@ def tile_moe_tk_lin_none_kernel(tc, xT, w, gate, offs, pos1, pos2, pos3, pos4, o
         def evacuate(b):
             first = BANK_EXPERTS[b][0] * C
             width = len(BANK_EXPERTS[b]) * C
-            nc.scalar.copy(y[:, first : first + width], banks[b][:, 0:width])
+            if b == VECTOR_BANK:
+                nc.vector.tensor_copy(y[:, first : first + width], banks[b][:, 0:width])
+            else:
+                nc.scalar.copy(y[:, first : first + width], banks[b][:, 0:width])
 
         evac_at = {}
         for b, es in enumerate(BANK_EXPERTS):
@@ -234,61 +246,51 @@ def tile_moe_tk_lin_none_kernel(tc, xT, w, gate, offs, pos1, pos2, pos3, pos4, o
         for ci in range(FIRST_MULTIPLY + 1, len(CHUNKS) + 1):
             if ci < len(CHUNKS):
                 prepare(ci)
-            if ci == len(CHUNKS) - 1:
+            if ci == last:
                 gate_t = arena.tile([P, 4, T], F32, name="gate_t", align_bytes=256, offset=GATE_AT)
                 for r, src in enumerate((pos1, pos2, pos3, pos4)):
                     nc.sync.dma_start(pos_t[r][:], src)
-                    if r % 2 == 1:
-                        pair = slice(r - 1, r + 1)
-                        nc.sync.dma_start(gate_t[:, pair, 0 : 2 * P], gate[pair, :, 0 : 2 * P].rearrange("r n t -> n r t"))
-                nc.sync.dma_start(gate_t[:, :, 2 * P : T], gate[:, :, 2 * P : T].rearrange("r n t -> n r t"))
+                    nc.sync.dma_start(gate_t[:, r, :], gate[r])
             multiply(ci - 1)
             for b in evac_at.get(ci, []):
                 evacuate(b)
 
-        prod = arena.tile([P, 4, T], F32, name="prod", align_bytes=256, offset=PROD_AT)
-        half = arena.tile([P, 2, T], F32, name="half", align_bytes=256, offset=XRAW_AT[4])
-        turned = arena.tile([P, 4 * P], F32, name="turned", align_bytes=256, offset=XRAW_AT[4] + XGRP + T * 4)
-        res = arena.tile([P, T], F32, name="res", align_bytes=256, offset=XRAW_AT[4] + XGRP)
+        prod = [
+            arena.tile([P, T], F32, name=f"prod{r}", align_bytes=256, offset=PROD_AT + r * T * 4) for r in range(4)
+        ]
+        turned = arena.tile([P, T], F32, name="turned", align_bytes=256, offset=XRAW_AT[4])
+        res = arena.tile([P, T], F32, name="res", align_bytes=256, offset=XRAW_AT[4] + T * 4)
 
-        def weigh(r, lo, hi):
-            nc.vector.tensor_tensor(
-                prod[:, r, lo:hi], y[:].indirect(pos_t[r][:, lo // 16 : hi // 16]), gate_t[:, r, lo:hi], MULT
-            )
+        def weigh(r, cols):
+            offsets = pos_t[r][:, cols.start // 16 : cols.stop // 16]
+            nc.vector.tensor_tensor(prod[r][:, cols], y[:].indirect(offsets), gate_t[:, r, cols], MULT)
 
-        def add_turned(r, block):
-            nc.tensor.matmul(
-                banks[block][:, 0:P],
-                lhsT=prod[:, r, block * P : (block + 1) * P],
-                rhs=ident[:],
-                is_transpose=True,
-                start=(r == 0),
-                stop=(r == 3),
-            )
+        def add_turned(r, cols):
+            for lo in range(cols.start, cols.stop, P):
+                nc.tensor.matmul(
+                    banks[lo // P][:, 0:P],
+                    lhsT=prod[r][:, lo : lo + P],
+                    rhs=ident[:],
+                    is_transpose=True,
+                    start=(r == 0),
+                    stop=(r == 2),
+                )
 
-        def turn_back(block):
-            cols = slice(block * P, (block + 1) * P)
-            back = psum.tile([P, P], F32, name=f"back{block % 2}")
-            nc.scalar.copy(turned[:, cols], banks[block][:, 0:P])
-            nc.tensor.transpose(back[:], turned[:, cols], ident[:])
-            nc.scalar.copy(res[:, cols], back[:])
+        def turn_back(cols, back):
+            for lo in range(cols.start, cols.stop, P):
+                nc.scalar.copy(turned[:, lo : lo + P], banks[lo // P][:, 0:P])
+                nc.tensor.transpose(back[:, lo - cols.start : lo - cols.start + P], turned[:, lo : lo + P], ident[:])
 
-        for blocks in ((0, 1), (2,), (3,)):
-            for r in range(4):
-                weigh(r, blocks[0] * P, (blocks[-1] + 1) * P)
-                for block in blocks:
-                    add_turned(r, block)
-            for block in blocks:
-                turn_back(block)
-            if blocks[-1] % 2 == 1:
-                cols = slice((blocks[-1] - 1) * P, (blocks[-1] + 1) * P)
-                nc.sync.dma_start(out[:, cols], res[:, cols])
-
-        lo = 4 * P
-        for r in range(3):
-            weigh(r, lo, T)
-        nc.vector.tensor_add(half[:, 0, lo:T], prod[:, 0, lo:T], prod[:, 1, lo:T])
-        weigh(3, lo, T)
-        nc.vector.tensor_add(half[:, 1, lo:T], half[:, 0, lo:T], prod[:, 2, lo:T])
-        nc.vector.tensor_add(res[:, lo:T], half[:, 1, lo:T], prod[:, 3, lo:T])
-        nc.sync.dma_start(out[:, lo:T], res[:, lo:T])
+        parts = [(slice(0, SPLIT), banks[6]), (slice(SPLIT, T), banks[7])]
+        for r in range(2):
+            weigh(r, slice(0, T))
+            add_turned(r, slice(0, T))
+        for cols, back in parts:
+            weigh(2, cols)
+            add_turned(2, cols)
+            turn_back(cols, back)
+        for cols, back in parts:
+            weigh(3, cols)
+        for cols, back in parts:
+            nc.vector.tensor_add(res[:, cols], prod[3][:, cols], back[:, 0 : cols.stop - cols.start])
+            nc.sync.dma_start(out[:, cols], res[:, cols])

@@ -18,6 +18,7 @@ U8 = mybir.dt.uint8
 FP8X4 = mybir.dt.float8_e4m3fn_x4
 MULT = mybir.AluOpType.mult
 ADD = mybir.AluOpType.add
+COPY = mybir.ActivationFunctionType.Copy
 
 FULL_CHUNKS = 23
 CHUNKS = [4] * FULL_CHUNKS + [2, 2, 2, 1, 1]
@@ -30,7 +31,7 @@ WALK = 4
 X_SCALAR = 256
 VECTOR_FROM = 19
 Y_AFTER = 17
-GATE_AFTER = 22
+GATE_AFTER = 20
 SPLIT = 384
 CODE_BUFFERS = 8
 FIRST_MULTIPLY = 3
@@ -50,6 +51,7 @@ Y_AT = GW_AT + EARLY * BIG
 GATE_AT = Y_AT + BIG
 PROD_AT = GATE_AT + BIG
 LATE_AT = PROD_AT + BIG
+TURNED_AT = XRAW_AT[4] + 3 * T * 4
 XGRP_AT = [BIG, SPARE_AT, GW_AT + BIG, SPARE_AT + RAW, PROD_AT]
 
 
@@ -137,8 +139,8 @@ def tile_moe_tk_lin_none_kernel(tc, xT, w, gate, offs, pos1, pos2, pos3, pos4, o
                 return Y_AT
             if ci == GATE_AFTER:
                 return GATE_AT
-            if ci < GATE_AFTER:
-                return LATE_AT + (ci - len(LATE) - 1) * 2 * GRP + GRP // 2
+            if ci < FULL_CHUNKS:
+                return LATE_AT + (ci - len(LATE) - 1 - (ci > GATE_AFTER)) * 2 * GRP + GRP // 2
             return PROD_AT + sum(widths[FULL_CHUNKS:ci]) * (GRP // 4)
 
         def round_slabs(eng, grp, to, raw, u0, u1):
@@ -248,49 +250,75 @@ def tile_moe_tk_lin_none_kernel(tc, xT, w, gate, offs, pos1, pos2, pos3, pos4, o
                 prepare(ci)
             if ci == last:
                 gate_t = arena.tile([P, 4, T], F32, name="gate_t", align_bytes=256, offset=GATE_AT)
-                for r, src in enumerate((pos1, pos2, pos3, pos4)):
-                    nc.sync.dma_start(pos_t[r][:], src)
-                    nc.sync.dma_start(gate_t[:, r, :], gate[r])
+                lists = (pos1, pos2, pos3, pos4)
+                for r in (0, 3):
+                    nc.sync.dma_start(pos_t[r][:], lists[r])
+                nc.sync.dma_start(gate_t[:, 0, :], gate[0])
+                nc.sync.dma_start(pos_t[2][:], lists[2])
+                nc.sync.dma_start(gate_t[:, 3, SPLIT:T], gate[3, :, SPLIT:T])
+                nc.sync.dma_start(gate_t[:, 2, :], gate[2])
+                nc.sync.dma_start(pos_t[1][:], lists[1])
+                gate_col = arena.tile([P, SPLIT // P], F32, name="gate_col", align_bytes=256, offset=TURNED_AT)
+                with nc.allow_non_contiguous_dma(reason="one weight a token and partition"):
+                    nc.sync.dma_start(gate_col[:], gate[3, 0, 0:SPLIT].rearrange("(j p) -> p j", p=P))
+                nc.sync.dma_start(gate_t[:, 1, :], gate[1])
             multiply(ci - 1)
             for b in evac_at.get(ci, []):
                 evacuate(b)
 
-        prod = [
-            arena.tile([P, T], F32, name=f"prod{r}", align_bytes=256, offset=PROD_AT + r * T * 4) for r in range(4)
-        ]
-        turned = arena.tile([P, T], F32, name="turned", align_bytes=256, offset=XRAW_AT[4])
-        res = arena.tile([P, T], F32, name="res", align_bytes=256, offset=XRAW_AT[4] + T * 4)
+        whole = slice(0, T)
+        parts = [slice(0, SPLIT), slice(SPLIT, T)]
+        backs = [banks[6], banks[7]]
+        free_at = XRAW_AT[4]
 
-        def weigh(r, cols):
-            offsets = pos_t[r][:, cols.start // 16 : cols.stop // 16]
-            nc.vector.tensor_tensor(prod[r][:, cols], y[:].indirect(offsets), gate_t[:, r, cols], MULT)
+        def floats(name, width, at):
+            return arena.tile([P, width], F32, name=name, align_bytes=256, offset=at)
 
-        def add_turned(r, cols):
-            for lo in range(cols.start, cols.stop, P):
-                nc.tensor.matmul(
-                    banks[lo // P][:, 0:P],
-                    lhsT=prod[r][:, lo : lo + P],
-                    rhs=ident[:],
-                    is_transpose=True,
-                    start=(r == 0),
-                    stop=(r == 2),
-                )
+        prod0 = floats("prod0", T, PROD_AT)
+        prod2 = floats("prod2", T, PROD_AT + T * 4)
+        picked3 = floats("picked3", SPLIT, PROD_AT + 2 * T * 4)
+        prod3 = floats("prod3", T - SPLIT, PROD_AT + 2 * T * 4 + SPLIT * 4)
+        turned = floats("turned", T, TURNED_AT)
+        res = floats("res", T, free_at)
+        scaled = floats("scaled", SPLIT, free_at + T * 4)
+        picked2 = floats("picked2", T, free_at + 2 * T * 4)
+        prod1 = floats("prod1", T, free_at + 2 * T * 4)
 
-        def turn_back(cols, back):
-            for lo in range(cols.start, cols.stop, P):
-                nc.scalar.copy(turned[:, lo : lo + P], banks[lo // P][:, 0:P])
-                nc.tensor.transpose(back[:, lo - cols.start : lo - cols.start + P], turned[:, lo : lo + P], ident[:])
+        def window(r, cols):
+            return y[:].indirect(pos_t[r][:, cols.start // 16 : cols.stop // 16])
 
-        parts = [(slice(0, SPLIT), banks[6]), (slice(SPLIT, T), banks[7])]
-        for r in range(2):
-            weigh(r, slice(0, T))
-            add_turned(r, slice(0, T))
-        for cols, back in parts:
-            weigh(2, cols)
-            add_turned(2, cols)
-            turn_back(cols, back)
-        for cols, back in parts:
-            weigh(3, cols)
-        for cols, back in parts:
-            nc.vector.tensor_add(res[:, cols], prod[3][:, cols], back[:, 0 : cols.stop - cols.start])
+        def turn(dst, src, start, stop):
+            nc.tensor.matmul(dst, lhsT=src, rhs=ident[:], is_transpose=True, start=start, stop=stop)
+
+        def block(j):
+            return slice(j * P, (j + 1) * P)
+
+        first = SPLIT // P
+        nc.scalar.activation(picked3[:], window(3, parts[0]), COPY)
+        for j in range(first):
+            turn(banks[5][:, block(j)], picked3[:, block(j)], True, True)
+        for cols in parts:
+            nc.scalar.activation(picked2[:, cols], window(2, cols), COPY)
+        nc.vector.tensor_tensor(prod0[:], window(0, whole), gate_t[:, 0, :], MULT)
+        for j in range(T // P):
+            turn(banks[j][:, 0:P], prod0[:, block(j)], True, False)
+        nc.vector.tensor_tensor(prod3[:], window(3, parts[1]), gate_t[:, 3, parts[1]], MULT)
+        for j in range(first, T // P):
+            turn(banks[j][:, 0:P], prod3[:, block(j - first)], False, False)
+        for cols in parts:
+            nc.vector.tensor_tensor(prod2[:, cols], picked2[:, cols], gate_t[:, 2, cols], MULT)
+            for j in range(cols.start // P, cols.stop // P):
+                turn(banks[j][:, 0:P], prod2[:, block(j)], False, True)
+        nc.vector.tensor_tensor(prod1[:], window(1, whole), gate_t[:, 1, :], MULT)
+        for j in range(first):
+            nc.scalar.activation(scaled[:, block(j)], banks[5][:, block(j)], COPY, scale=gate_col[:, j : j + 1])
+        for j in range(T // P):
+            nc.scalar.copy(turned[:, block(j)], banks[j][:, 0:P])
+            if j < first:
+                turn(backs[0][:, block(j)], scaled[:, block(j)], True, False)
+                turn(backs[0][:, block(j)], turned[:, block(j)], False, True)
+            else:
+                turn(backs[1][:, block(j - first)], turned[:, block(j)], True, True)
+        for cols, back in zip(parts, backs):
+            nc.vector.tensor_add(res[:, cols], prod1[:, cols], back[:, 0 : cols.stop - cols.start])
             nc.sync.dma_start(out[:, cols], res[:, cols])

@@ -43,16 +43,16 @@ XGRP = T * 4 * 2
 RANGES = SLOTS // GATHER
 LATE = [(b, a) for b in range(RANGES) for a in range(EARLY, PASSES)]
 LATE_AFTER = {1 + j: j for j in range(len(LATE))}
-XRAW_AT = [0] + [a * BIG + XGRP for a in range(1, PASSES)]
-SPARE_AT = PASSES * BIG + XGRP
-WRAW_AT = [BIG + XGRP - RAW, XRAW_AT[1], SPARE_AT, XRAW_AT[2], XRAW_AT[3], SPARE_AT + RAW, XRAW_AT[4]]
-GW_AT = SPARE_AT + 2 * RAW
+WRAW_AT = [i * RAW for i in range(8)]
+XRAW_AT = [0, 2 * RAW, 4 * RAW, 6 * RAW, 6 * RAW + BIG]
+GW_AT = XRAW_AT[4] + BIG
 Y_AT = GW_AT + EARLY * BIG
 GATE_AT = Y_AT + BIG
 PROD_AT = GATE_AT + BIG
 LATE_AT = PROD_AT + BIG
-TURNED_AT = XRAW_AT[4] + 3 * T * 4
-XGRP_AT = [BIG, SPARE_AT, GW_AT + BIG, SPARE_AT + RAW, PROD_AT]
+TURNED_AT = XRAW_AT[4]
+XGRP_AT = [BIG, XRAW_AT[1] + BIG, GW_AT + BIG, XRAW_AT[2] + BIG, PROD_AT]
+PAIRED = 14
 
 
 def tile_moe_tk_lin_none_kernel(tc, xT, w, gate, offs, pos1, pos2, pos3, pos4, out):
@@ -164,13 +164,17 @@ def tile_moe_tk_lin_none_kernel(tc, xT, w, gate, offs, pos1, pos2, pos3, pos4, o
         raws = {}
 
         def load(ci):
-            slab, size = firsts[ci], CHUNKS[ci]
+            if ci < PAIRED and ci % 2:
+                return
+            slab, size = firsts[ci], CHUNKS[ci] * (2 if ci < PAIRED else 1)
             raw_at = WRAW_AT[slab // 4 % len(WRAW_AT)] + slab % 4 * (RAW // 4)
             if ci == Y_AFTER:
                 raw_at = Y_AT
             raw = arena.tile([P, size, 4, N], F32, name=f"wraw{ci}", align_bytes=256, offset=raw_at)
             nc.sync.dma_start(raw[:].rearrange("p u j n -> p u (j n)"), w_slabs[:, slab : slab + size, :])
-            raws[ci] = raw
+            raws[ci] = raw[:, 0 : CHUNKS[ci]]
+            if ci < PAIRED:
+                raws[ci + 1] = raw[:, CHUNKS[ci] : size]
 
         def prepare(ci):
             size, raw = CHUNKS[ci], raws.pop(ci)
@@ -186,7 +190,7 @@ def tile_moe_tk_lin_none_kernel(tc, xT, w, gate, offs, pos1, pos2, pos3, pos4, o
                 if deferred[ci]:
                     round_slabs("vector", grp_of(ci + 1), 0, raw, size - deferred[ci], size)
             for cj in range(ci + 1, len(CHUNKS)):
-                if firsts[cj] // 4 == ci + len(WRAW_AT):
+                if firsts[cj] // 4 + (cj < PAIRED) == ci + len(WRAW_AT):
                     load(cj)
             codes = wq_pool.tile([P, 4 * N], U32, name="wcodes", align_bytes=64)
             scales = wq_pool.tile([P, 4 * N], U8, name="wscales", align_bytes=64)
@@ -279,7 +283,7 @@ def tile_moe_tk_lin_none_kernel(tc, xT, w, gate, offs, pos1, pos2, pos3, pos4, o
         picked3 = floats("picked3", SPLIT, PROD_AT + 2 * T * 4)
         prod3 = floats("prod3", T - SPLIT, PROD_AT + 2 * T * 4 + SPLIT * 4)
         turned = floats("turned", T, TURNED_AT)
-        res = floats("res", T, free_at)
+        res = floats("res", T, free_at + 3 * T * 4)
         scaled = floats("scaled", SPLIT, free_at + T * 4)
         picked2 = floats("picked2", T, free_at + 2 * T * 4)
         prod1 = floats("prod1", T, free_at + 2 * T * 4)

@@ -22,8 +22,9 @@ COPY = mybir.ActivationFunctionType.Copy
 
 FULL_CHUNKS = 23
 CHUNKS = [4] * FULL_CHUNKS + [2, 2, 2, 1, 1]
-BANK_EXPERTS = [[0, 1, 2, 3], [4, 5, 6, 7], [8, 9, 10, 11], [12, 13, 14, 15], [16], [17, 18, 19]]
-VECTOR_BANK = 4
+SLABS = E * PASSES
+ORDER = list(range(SLABS - PASSES - 1)) + list(range(SLABS - PASSES, SLABS - 1)) + [SLABS - PASSES - 1, SLABS - 1]
+BANK_EXPERTS = [[0, 1, 2, 3], [4, 5, 6, 7], [8, 9, 10, 11], [12, 13, 14, 15], [16, 17, 18], [19]]
 GATHER = 512
 WINDOW = 704
 EARLY = 2
@@ -50,7 +51,6 @@ Y_AT = GW_AT + EARLY * BIG
 GATE_AT = Y_AT + BIG
 PROD_AT = GATE_AT + BIG
 LATE_AT = PROD_AT + BIG
-TURNED_AT = XRAW_AT[4]
 XGRP_AT = [BIG, XRAW_AT[1] + BIG, GW_AT + BIG, XRAW_AT[2] + BIG, PROD_AT]
 PAIRED = 14
 
@@ -171,7 +171,7 @@ def tile_moe_tk_lin_none_kernel(tc, xT, w, gate, offs, pos1, pos2, pos3, pos4, o
             if ci == Y_AFTER:
                 raw_at = Y_AT
             raw = arena.tile([P, size, 4, N], F32, name=f"wraw{ci}", align_bytes=256, offset=raw_at)
-            nc.sync.dma_start(raw[:].rearrange("p u j n -> p u (j n)"), w_slabs[:, slab : slab + size, :])
+            nc.sync.dma_start(raw[:].rearrange("p u j n -> p u (j n)"), w_slabs[:, ORDER[slab] : ORDER[slab] + size, :])
             raws[ci] = raw[:, 0 : CHUNKS[ci]]
             if ci < PAIRED:
                 raws[ci + 1] = raw[:, CHUNKS[ci] : size]
@@ -180,9 +180,7 @@ def tile_moe_tk_lin_none_kernel(tc, xT, w, gate, offs, pos1, pos2, pos3, pos4, o
             size, raw = CHUNKS[ci], raws.pop(ci)
             grp = grp_of(ci)
             at = carried[ci]
-            if ci == last:
-                round_slabs("vector", grp, at, raw, 0, size)
-            elif ci < VECTOR_FROM and ci % 2 == 0:
+            if ci < VECTOR_FROM and ci % 2 == 0:
                 round_slabs("scalar", grp, at, raw, 0, size - 1)
                 round_slabs("gpsimd", grp, at + size - 1, raw, size - 1, size)
             else:
@@ -211,7 +209,7 @@ def tile_moe_tk_lin_none_kernel(tc, xT, w, gate, offs, pos1, pos2, pos3, pos4, o
             slab, size = firsts[ci] - carried[ci], widths[ci]
             codes, scales = quantised.pop(ci)
             for u in range(size):
-                e, a = divmod(slab + u, PASSES)
+                e, a = divmod(ORDER[slab + u], PASSES)
                 b, i = bank_of[e]
                 here = slice(e * C, (e + 1) * C)
                 plane, k = (gbytes_a, 4 * a) if a < 4 else (gbytes_b, 0)
@@ -234,14 +232,11 @@ def tile_moe_tk_lin_none_kernel(tc, xT, w, gate, offs, pos1, pos2, pos3, pos4, o
         def evacuate(b):
             first = BANK_EXPERTS[b][0] * C
             width = len(BANK_EXPERTS[b]) * C
-            if b == VECTOR_BANK:
-                nc.vector.tensor_copy(y[:, first : first + width], banks[b][:, 0:width])
-            else:
-                nc.scalar.copy(y[:, first : first + width], banks[b][:, 0:width])
+            nc.scalar.copy(y[:, first : first + width], banks[b][:, 0:width])
 
         evac_at = {}
         for b, es in enumerate(BANK_EXPERTS):
-            closed = max(i for i, f in enumerate(firsts) if f - carried[i] <= es[-1] * PASSES + PASSES - 1)
+            closed = max(i for i, f in enumerate(firsts) if f - carried[i] <= ORDER.index(es[-1] * PASSES + PASSES - 1))
             evac_at.setdefault(max(closed + 1, Y_AFTER + 1 + b), []).append(b)
         for ci in range(len(WRAW_AT)):
             load(ci)
@@ -262,7 +257,7 @@ def tile_moe_tk_lin_none_kernel(tc, xT, w, gate, offs, pos1, pos2, pos3, pos4, o
                 nc.sync.dma_start(gate_t[:, 3, SPLIT:T], gate[3, :, SPLIT:T])
                 nc.sync.dma_start(gate_t[:, 2, :], gate[2])
                 nc.sync.dma_start(pos_t[1][:], lists[1])
-                gate_col = arena.tile([P, SPLIT // P], F32, name="gate_col", align_bytes=256, offset=TURNED_AT)
+                gate_col = arena.tile([P, SPLIT // P], F32, name="gate_col", align_bytes=256, offset=grp_at(GATE_AFTER + 1))
                 with nc.allow_non_contiguous_dma(reason="one weight a token and partition"):
                     nc.sync.dma_start(gate_col[:], gate[3, 0, 0:SPLIT].rearrange("(j p) -> p j", p=P))
                 nc.sync.dma_start(gate_t[:, 1, :], gate[1])
@@ -282,11 +277,11 @@ def tile_moe_tk_lin_none_kernel(tc, xT, w, gate, offs, pos1, pos2, pos3, pos4, o
         prod2 = floats("prod2", T, PROD_AT + T * 4)
         picked3 = floats("picked3", SPLIT, PROD_AT + 2 * T * 4)
         prod3 = floats("prod3", T - SPLIT, PROD_AT + 2 * T * 4 + SPLIT * 4)
-        turned = floats("turned", T, TURNED_AT)
+        turned = floats("turned", T, grp_at(GATE_AFTER + 1))
         res = floats("res", T, free_at + 3 * T * 4)
         scaled = floats("scaled", SPLIT, free_at + T * 4)
-        picked2 = floats("picked2", T, free_at + 2 * T * 4)
-        prod1 = floats("prod1", T, free_at + 2 * T * 4)
+        picked2 = [floats("picked2_0", SPLIT, free_at + 2 * T * 4), floats("picked2_1", T - SPLIT, free_at + 2 * T * 4 + SPLIT * 4)]
+        prod1 = [floats("prod1_0", SPLIT, GW_AT), floats("prod1_1", T - SPLIT, free_at + 2 * T * 4)]
 
         def window(r, cols):
             return y[:].indirect(pos_t[r][:, cols.start // 16 : cols.stop // 16])
@@ -301,19 +296,19 @@ def tile_moe_tk_lin_none_kernel(tc, xT, w, gate, offs, pos1, pos2, pos3, pos4, o
         nc.scalar.activation(picked3[:], window(3, parts[0]), COPY)
         for j in range(first):
             turn(banks[5][:, block(j)], picked3[:, block(j)], True, True)
-        for cols in parts:
-            nc.scalar.activation(picked2[:, cols], window(2, cols), COPY)
+        for i, cols in enumerate(parts):
+            nc.scalar.activation(picked2[i][:], window(2, cols), COPY)
         nc.vector.tensor_tensor(prod0[:], window(0, whole), gate_t[:, 0, :], MULT)
         for j in range(T // P):
             turn(banks[j][:, 0:P], prod0[:, block(j)], True, False)
         nc.vector.tensor_tensor(prod3[:], window(3, parts[1]), gate_t[:, 3, parts[1]], MULT)
         for j in range(first, T // P):
             turn(banks[j][:, 0:P], prod3[:, block(j - first)], False, False)
-        for cols in parts:
-            nc.vector.tensor_tensor(prod2[:, cols], picked2[:, cols], gate_t[:, 2, cols], MULT)
+        for i, cols in enumerate(parts):
+            nc.vector.tensor_tensor(prod2[:, cols], picked2[i][:], gate_t[:, 2, cols], MULT)
             for j in range(cols.start // P, cols.stop // P):
                 turn(banks[j][:, 0:P], prod2[:, block(j)], False, True)
-        nc.vector.tensor_tensor(prod1[:], window(1, whole), gate_t[:, 1, :], MULT)
+            nc.vector.tensor_tensor(prod1[i][:], window(1, cols), gate_t[:, 1, cols], MULT)
         for j in range(first):
             nc.scalar.activation(scaled[:, block(j)], banks[5][:, block(j)], COPY, scale=gate_col[:, j : j + 1])
         for j in range(T // P):
@@ -323,6 +318,6 @@ def tile_moe_tk_lin_none_kernel(tc, xT, w, gate, offs, pos1, pos2, pos3, pos4, o
                 turn(backs[0][:, block(j)], turned[:, block(j)], False, True)
             else:
                 turn(backs[1][:, block(j - first)], turned[:, block(j)], True, True)
-        for cols, back in zip(parts, backs):
-            nc.vector.tensor_add(res[:, cols], prod1[:, cols], back[:, 0 : cols.stop - cols.start])
+        for i, cols in enumerate(parts):
+            nc.vector.tensor_add(res[:, cols], prod1[i][:], backs[i][:, 0 : cols.stop - cols.start])
             nc.sync.dma_start(out[:, cols], res[:, cols])

@@ -33,6 +33,7 @@ X_SCALAR = 256
 VECTOR_FROM = 19
 Y_AFTER = 17
 GATE_AFTER = 20
+SHARE = 512
 SPLIT = 384
 CODE_BUFFERS = 8
 FIRST_MULTIPLY = 3
@@ -250,38 +251,35 @@ def tile_moe_tk_lin_none_kernel(tc, xT, w, gate, offs, pos1, pos2, pos3, pos4, o
             if ci == last:
                 gate_t = arena.tile([P, 4, T], F32, name="gate_t", align_bytes=256, offset=GATE_AT)
                 lists = (pos1, pos2, pos3, pos4)
-                for r in (0, 3):
+                for r in (0, 2):
                     nc.sync.dma_start(pos_t[r][:], lists[r])
                 nc.sync.dma_start(gate_t[:, 0, :], gate[0])
-                nc.sync.dma_start(pos_t[2][:], lists[2])
-                nc.sync.dma_start(gate_t[:, 3, SPLIT:T], gate[3, :, SPLIT:T])
-                nc.sync.dma_start(gate_t[:, 2, :], gate[2])
-                nc.sync.dma_start(pos_t[1][:], lists[1])
-                gate_col = arena.tile([P, SPLIT // P], F32, name="gate_col", align_bytes=256, offset=grp_at(GATE_AFTER + 1))
-                with nc.allow_non_contiguous_dma(reason="one weight a token and partition"):
-                    nc.sync.dma_start(gate_col[:], gate[3, 0, 0:SPLIT].rearrange("(j p) -> p j", p=P))
+                for r in (3, 1):
+                    nc.sync.dma_start(pos_t[r][:], lists[r])
                 nc.sync.dma_start(gate_t[:, 1, :], gate[1])
+                gate_col = arena.tile([P, 16], F32, name="gate_col", align_bytes=256, offset=grp_at(GATE_AFTER + 1))
+                with nc.allow_non_contiguous_dma(reason="one weight a token and partition"):
+                    for r in (2, 3):
+                        tokens = SHARE if r == 2 else T
+                        columns = gate_col[:, (r - 2) * 8 : (r - 2) * 8 + tokens // P]
+                        nc.sync.dma_start(columns, gate[r, 0, 0:tokens].rearrange("(j p) -> p j", p=P))
+                nc.sync.dma_start(gate_t[:, 2, SHARE:T], gate[2, :, SHARE:T])
             multiply(ci - 1)
             for b in evac_at.get(ci, []):
                 evacuate(b)
 
-        whole = slice(0, T)
-        parts = [slice(0, SPLIT), slice(SPLIT, T)]
-        backs = [banks[6], banks[7]]
-        free_at = XRAW_AT[4]
+        whole, shared, rest = slice(0, T), slice(0, SHARE), slice(SHARE, T)
+        blocks = {2: SHARE // P, 3: T // P}
 
         def floats(name, width, at):
             return arena.tile([P, width], F32, name=name, align_bytes=256, offset=at)
 
-        prod0 = floats("prod0", T, PROD_AT)
-        prod2 = floats("prod2", T, PROD_AT + T * 4)
-        picked3 = floats("picked3", SPLIT, PROD_AT + 2 * T * 4)
-        prod3 = floats("prod3", T - SPLIT, PROD_AT + 2 * T * 4 + SPLIT * 4)
-        turned = floats("turned", T, grp_at(GATE_AFTER + 1))
-        res = floats("res", T, free_at + 3 * T * 4)
-        scaled = floats("scaled", SPLIT, free_at + T * 4)
-        picked2 = [floats("picked2_0", SPLIT, free_at + 2 * T * 4), floats("picked2_1", T - SPLIT, free_at + 2 * T * 4 + SPLIT * 4)]
-        prod1 = [floats("prod1_0", SPLIT, GW_AT), floats("prod1_1", T - SPLIT, free_at + 2 * T * 4)]
+        prod = [floats(f"prod{r}", T if r < 2 else T - SHARE, PROD_AT + r * T * 4) for r in range(3)]
+        picked = {r: floats(f"picked{r}", blocks[r] * P, GW_AT + r * T * 4) for r in (2, 3)}
+        scaled = {r: floats(f"scaled{r}", blocks[r] * P, GW_AT + (r - 2) * T * 4) for r in (2, 3)}
+        pair = floats("pair", T, XRAW_AT[4])
+        triple = floats("triple", T - SHARE, XRAW_AT[4] + T * 4)
+        res = floats("res", T, XRAW_AT[4] + 2 * T * 4)
 
         def window(r, cols):
             return y[:].indirect(pos_t[r][:, cols.start // 16 : cols.stop // 16])
@@ -292,32 +290,26 @@ def tile_moe_tk_lin_none_kernel(tc, xT, w, gate, offs, pos1, pos2, pos3, pos4, o
         def block(j):
             return slice(j * P, (j + 1) * P)
 
-        first = SPLIT // P
-        nc.scalar.activation(picked3[:], window(3, parts[0]), COPY)
-        for j in range(first):
-            turn(banks[5][:, block(j)], picked3[:, block(j)], True, True)
-        for i, cols in enumerate(parts):
-            nc.scalar.activation(picked2[i][:], window(2, cols), COPY)
-        nc.vector.tensor_tensor(prod0[:], window(0, whole), gate_t[:, 0, :], MULT)
-        for j in range(T // P):
-            turn(banks[j][:, 0:P], prod0[:, block(j)], True, False)
-        nc.vector.tensor_tensor(prod3[:], window(3, parts[1]), gate_t[:, 3, parts[1]], MULT)
-        for j in range(first, T // P):
-            turn(banks[j][:, 0:P], prod3[:, block(j - first)], False, False)
-        for i, cols in enumerate(parts):
-            nc.vector.tensor_tensor(prod2[:, cols], picked2[i][:], gate_t[:, 2, cols], MULT)
+        picks = [(2, shared), (3, slice(0, SPLIT)), (3, slice(SPLIT, T))]
+        back = [banks[len(picks) + j][:, 0:P] for j in range(T // P)]
+        turned = {}
+        for b, (r, cols) in enumerate(picks):
+            nc.scalar.activation(picked[r][:, cols], window(r, cols), COPY)
             for j in range(cols.start // P, cols.stop // P):
-                turn(banks[j][:, 0:P], prod2[:, block(j)], False, True)
-            nc.vector.tensor_tensor(prod1[i][:], window(1, cols), gate_t[:, 1, cols], MULT)
-        for j in range(first):
-            nc.scalar.activation(scaled[:, block(j)], banks[5][:, block(j)], COPY, scale=gate_col[:, j : j + 1])
+                turned[r, j] = banks[b][:, block(j - cols.start // P)]
+                turn(turned[r, j], picked[r][:, block(j)], True, True)
+        for r in (2, 3):
+            for j in range(blocks[r]):
+                column = gate_col[:, (r - 2) * 8 + j : (r - 2) * 8 + j + 1]
+                nc.scalar.activation(scaled[r][:, block(j)], turned[r, j], COPY, scale=column)
+                turn(back[j], scaled[r][:, block(j)], r == 2 or j >= blocks[2], r == 3)
+        for r in range(3):
+            cols = whole if r < 2 else rest
+            nc.vector.tensor_tensor(prod[r][:], window(r, cols), gate_t[:, r, cols], MULT)
+        nc.vector.tensor_add(pair[:], prod[0][:], prod[1][:])
         for j in range(T // P):
-            nc.scalar.copy(turned[:, block(j)], banks[j][:, 0:P])
-            if j < first:
-                turn(backs[0][:, block(j)], scaled[:, block(j)], True, False)
-                turn(backs[0][:, block(j)], turned[:, block(j)], False, True)
-            else:
-                turn(backs[1][:, block(j - first)], turned[:, block(j)], True, True)
-        for i, cols in enumerate(parts):
-            nc.vector.tensor_add(res[:, cols], prod1[i][:], backs[i][:, 0 : cols.stop - cols.start])
+            if j == 1:
+                nc.vector.tensor_add(triple[:], pair[:, rest], prod[2][:])
+            nc.vector.tensor_add(res[:, block(j)], pair[:, block(j)] if j < blocks[2] else triple[:], back[j])
+        for cols in (slice(0, SPLIT), slice(SPLIT, T)):
             nc.sync.dma_start(out[:, cols], res[:, cols])

@@ -22,6 +22,7 @@ COPY = mybir.ActivationFunctionType.Copy
 
 FULL_CHUNKS = 23
 CHUNKS = [4] * FULL_CHUNKS + [2, 2, 2, 1, 1]
+PAIRED = 14
 SLABS = E * PASSES
 ORDER = list(range(SLABS - PASSES - 1)) + list(range(SLABS - PASSES, SLABS - 1)) + [SLABS - PASSES - 1, SLABS - 1]
 BANK_EXPERTS = [[0, 1, 2, 3], [4, 5, 6, 7], [8, 9, 10, 11], [12, 13, 14, 15], [16, 17, 18], [19]]
@@ -33,8 +34,9 @@ X_SCALAR = 256
 VECTOR_FROM = 19
 Y_AFTER = 17
 GATE_AFTER = 20
-SHARE = 512
+SHARE = 384
 SPLIT = 384
+COL_STEP = 8
 CODE_BUFFERS = 8
 FIRST_MULTIPLY = 3
 
@@ -45,7 +47,8 @@ XGRP = T * 4 * 2
 RANGES = SLOTS // GATHER
 LATE = [(b, a) for b in range(RANGES) for a in range(EARLY, PASSES)]
 LATE_AFTER = {1 + j: j for j in range(len(LATE))}
-WRAW_AT = [i * RAW for i in range(8)]
+RING = 8
+WRAW_AT = [i * RAW for i in range(RING)]
 XRAW_AT = [0, 2 * RAW, 4 * RAW, 6 * RAW, 6 * RAW + BIG]
 GW_AT = XRAW_AT[4] + BIG
 Y_AT = GW_AT + EARLY * BIG
@@ -53,7 +56,6 @@ GATE_AT = Y_AT + BIG
 PROD_AT = GATE_AT + BIG
 LATE_AT = PROD_AT + BIG
 XGRP_AT = [BIG, XRAW_AT[1] + BIG, GW_AT + BIG, XRAW_AT[2] + BIG, PROD_AT]
-PAIRED = 14
 
 
 def tile_moe_tk_lin_none_kernel(tc, xT, w, gate, offs, pos1, pos2, pos3, pos4, out):
@@ -167,12 +169,13 @@ def tile_moe_tk_lin_none_kernel(tc, xT, w, gate, offs, pos1, pos2, pos3, pos4, o
         def load(ci):
             if ci < PAIRED and ci % 2:
                 return
-            slab, size = firsts[ci], CHUNKS[ci] * (2 if ci < PAIRED else 1)
-            raw_at = WRAW_AT[slab // 4 % len(WRAW_AT)] + slab % 4 * (RAW // 4)
+            place, size = firsts[ci], CHUNKS[ci] * (2 if ci < PAIRED else 1)
+            raw_at = WRAW_AT[place // 4 % RING] + place % 4 * (RAW // 4)
             if ci == Y_AFTER:
                 raw_at = Y_AT
             raw = arena.tile([P, size, 4, N], F32, name=f"wraw{ci}", align_bytes=256, offset=raw_at)
-            nc.sync.dma_start(raw[:].rearrange("p u j n -> p u (j n)"), w_slabs[:, ORDER[slab] : ORDER[slab] + size, :])
+            source = w_slabs[:, ORDER[place] : ORDER[place] + size, :]
+            nc.sync.dma_start(raw[:].rearrange("p u j n -> p u (j n)"), source)
             raws[ci] = raw[:, 0 : CHUNKS[ci]]
             if ci < PAIRED:
                 raws[ci + 1] = raw[:, CHUNKS[ci] : size]
@@ -189,7 +192,7 @@ def tile_moe_tk_lin_none_kernel(tc, xT, w, gate, offs, pos1, pos2, pos3, pos4, o
                 if deferred[ci]:
                     round_slabs("vector", grp_of(ci + 1), 0, raw, size - deferred[ci], size)
             for cj in range(ci + 1, len(CHUNKS)):
-                if firsts[cj] // 4 + (cj < PAIRED) == ci + len(WRAW_AT):
+                if firsts[cj] // 4 + (cj < PAIRED) == ci + RING:
                     load(cj)
             codes = wq_pool.tile([P, 4 * N], U32, name="wcodes", align_bytes=64)
             scales = wq_pool.tile([P, 4 * N], U8, name="wscales", align_bytes=64)
@@ -207,10 +210,10 @@ def tile_moe_tk_lin_none_kernel(tc, xT, w, gate, offs, pos1, pos2, pos3, pos4, o
                 gather(late[b, a][:], words[a], b)
 
         def multiply(ci):
-            slab, size = firsts[ci] - carried[ci], widths[ci]
+            place, size = firsts[ci] - carried[ci], widths[ci]
             codes, scales = quantised.pop(ci)
             for u in range(size):
-                e, a = divmod(ORDER[slab + u], PASSES)
+                e, a = divmod(ORDER[place + u], PASSES)
                 b, i = bank_of[e]
                 here = slice(e * C, (e + 1) * C)
                 plane, k = (gbytes_a, 4 * a) if a < 4 else (gbytes_b, 0)
@@ -237,9 +240,10 @@ def tile_moe_tk_lin_none_kernel(tc, xT, w, gate, offs, pos1, pos2, pos3, pos4, o
 
         evac_at = {}
         for b, es in enumerate(BANK_EXPERTS):
-            closed = max(i for i, f in enumerate(firsts) if f - carried[i] <= ORDER.index(es[-1] * PASSES + PASSES - 1))
+            place = ORDER.index(es[-1] * PASSES + PASSES - 1)
+            closed = max(i for i, f in enumerate(firsts) if f - carried[i] <= place)
             evac_at.setdefault(max(closed + 1, Y_AFTER + 1 + b), []).append(b)
-        for ci in range(len(WRAW_AT)):
+        for ci in range(RING):
             load(ci)
         for ci in range(FIRST_MULTIPLY + 1):
             prepare(ci)
@@ -249,7 +253,7 @@ def tile_moe_tk_lin_none_kernel(tc, xT, w, gate, offs, pos1, pos2, pos3, pos4, o
             if ci < len(CHUNKS):
                 prepare(ci)
             if ci == last:
-                gate_t = arena.tile([P, 4, T], F32, name="gate_t", align_bytes=256, offset=GATE_AT)
+                gate_t = arena.tile([P, 3, T], F32, name="gate_t", align_bytes=256, offset=GATE_AT)
                 lists = (pos1, pos2, pos3, pos4)
                 for r in (0, 2):
                     nc.sync.dma_start(pos_t[r][:], lists[r])
@@ -257,11 +261,12 @@ def tile_moe_tk_lin_none_kernel(tc, xT, w, gate, offs, pos1, pos2, pos3, pos4, o
                 for r in (3, 1):
                     nc.sync.dma_start(pos_t[r][:], lists[r])
                 nc.sync.dma_start(gate_t[:, 1, :], gate[1])
-                gate_col = arena.tile([P, 16], F32, name="gate_col", align_bytes=256, offset=grp_at(GATE_AFTER + 1))
+                col_at = grp_at(GATE_AFTER + 1)
+                gate_col = arena.tile([P, 2 * COL_STEP], F32, name="gate_col", align_bytes=256, offset=col_at)
                 with nc.allow_non_contiguous_dma(reason="one weight a token and partition"):
                     for r in (2, 3):
                         tokens = SHARE if r == 2 else T
-                        columns = gate_col[:, (r - 2) * 8 : (r - 2) * 8 + tokens // P]
+                        columns = gate_col[:, (r - 2) * COL_STEP : (r - 2) * COL_STEP + tokens // P]
                         nc.sync.dma_start(columns, gate[r, 0, 0:tokens].rearrange("(j p) -> p j", p=P))
                 nc.sync.dma_start(gate_t[:, 2, SHARE:T], gate[2, :, SHARE:T])
             multiply(ci - 1)
@@ -300,7 +305,7 @@ def tile_moe_tk_lin_none_kernel(tc, xT, w, gate, offs, pos1, pos2, pos3, pos4, o
                 turn(turned[r, j], picked[r][:, block(j)], True, True)
         for r in (2, 3):
             for j in range(blocks[r]):
-                column = gate_col[:, (r - 2) * 8 + j : (r - 2) * 8 + j + 1]
+                column = gate_col[:, (r - 2) * COL_STEP + j : (r - 2) * COL_STEP + j + 1]
                 nc.scalar.activation(scaled[r][:, block(j)], turned[r, j], COPY, scale=column)
                 turn(back[j], scaled[r][:, block(j)], r == 2 or j >= blocks[2], r == 3)
         for r in range(3):
@@ -310,6 +315,6 @@ def tile_moe_tk_lin_none_kernel(tc, xT, w, gate, offs, pos1, pos2, pos3, pos4, o
         for j in range(T // P):
             if j == 1:
                 nc.vector.tensor_add(triple[:], pair[:, rest], prod[2][:])
-            nc.vector.tensor_add(res[:, block(j)], pair[:, block(j)] if j < blocks[2] else triple[:], back[j])
+            nc.vector.tensor_add(res[:, block(j)], pair[:, block(j)] if j < blocks[2] else triple[:, block(j - blocks[2])], back[j])
         for cols in (slice(0, SPLIT), slice(SPLIT, T)):
             nc.sync.dma_start(out[:, cols], res[:, cols])

@@ -20,42 +20,43 @@ MULT = mybir.AluOpType.mult
 ADD = mybir.AluOpType.add
 COPY = mybir.ActivationFunctionType.Copy
 
-FULL_CHUNKS = 23
-CHUNKS = [4] * FULL_CHUNKS + [2, 2, 2, 1, 1]
-PAIRED = 14
 SLABS = E * PASSES
+HALF = SLOTS // 2
+WINDOW = 1712
+LATE = [("a", 0), ("b", 0), ("a", 1), ("b", 1)] + [(a, 1) for a in range(PASSES)]
+FIRST = 4
+BY_SCALAR, BY_GPSIMD = 4, 3
+PERIOD = BY_SCALAR + BY_GPSIMD
+CHUNKS = [4] * 6 + [3, 2, 2, 1, 1]
+BY_VECTOR = [0] + [2] * 5 + [1] * 3 + [0, 0]
 ORDER = list(range(SLABS - PASSES - 1)) + list(range(SLABS - PASSES, SLABS - 1)) + [SLABS - PASSES - 1, SLABS - 1]
 BANK_EXPERTS = [[0, 1, 2, 3], [4, 5, 6, 7], [8, 9, 10, 11], [12, 13, 14, 15], [16, 17, 18], [19]]
-GATHER = 512
-WINDOW = 704
-EARLY = 2
+BANK_ENGINE = ["scalar", "scalar", "vector", "vector", "scalar", "scalar"]
 WALK = 4
 X_SCALAR = 256
-VECTOR_FROM = 19
-Y_AFTER = 17
-GATE_AFTER = 20
+Y_AFTER = 4
+GATE_AFTER = 3
 SHARE = 384
 SPLIT = 384
 COL_STEP = 8
 CODE_BUFFERS = 8
-FIRST_MULTIPLY = 3
 
-BIG = 4 * T * 4
-RAW = 4 * 4 * N * 4
-GRP = 4 * N * 4 * 2
-XGRP = T * 4 * 2
-RANGES = SLOTS // GATHER
-LATE = [(b, a) for b in range(RANGES) for a in range(EARLY, PASSES)]
-LATE_AFTER = {1 + j: j for j in range(len(LATE))}
-RING = 8
-WRAW_AT = [i * RAW for i in range(RING)]
-XRAW_AT = [0, 2 * RAW, 4 * RAW, 6 * RAW, 6 * RAW + BIG]
-GW_AT = XRAW_AT[4] + BIG
-Y_AT = GW_AT + EARLY * BIG
-GATE_AT = Y_AT + BIG
-PROD_AT = GATE_AT + BIG
-LATE_AT = PROD_AT + BIG
-XGRP_AT = [BIG, XRAW_AT[1] + BIG, GW_AT + BIG, XRAW_AT[2] + BIG, PROD_AT]
+RAW = 4 * N * 4
+GRP = N * 4 * 2
+XRAW = 4 * T * 4
+XGRP = XRAW // 2
+ROW = T * 4
+RING = 4 * PERIOD
+FIRST_AT = PASSES * XRAW
+EARLY_AT = FIRST_AT + FIRST * RAW
+GRP_AT = EARLY_AT + PASSES * HALF * 4
+GATE_AT = GRP_AT + 4 * 4 * GRP
+COL_AT = GATE_AT + 8 * GRP
+OUT_ROOM = [2 * GRP if what in ("a", "b") else HALF * 4 for what, half in LATE]
+ROOM = [OUT_ROOM[k] + (SLOTS * 4 if k == Y_AFTER else BY_GPSIMD * GRP) for k in range(len(LATE))]
+LATE_AT = [COL_AT + 4 * GRP + sum(ROOM[:k]) for k in range(len(LATE))]
+Y_AT = LATE_AT[Y_AFTER] + OUT_ROOM[Y_AFTER]
+XGRP_AT = [GRP_AT, GRP_AT + XGRP, GRP_AT + 2 * XGRP, LATE_AT[-2], LATE_AT[-1]]
 
 
 def tile_moe_tk_lin_none_kernel(tc, xT, w, gate, offs, pos1, pos2, pos3, pos4, out):
@@ -69,41 +70,36 @@ def tile_moe_tk_lin_none_kernel(tc, xT, w, gate, offs, pos1, pos2, pos3, pos4, o
         offs_t = keep.tile([P, SLOTS // 16], U16, name="offs_t")
         pos_t = [keep.tile([P, T // 16], U16, name=f"pos_t{r}") for r in range(4)]
 
-        words = [keep.tile([P, WINDOW], U32, name=f"words{a}", align_bytes=64) for a in range(PASSES)]
-        bytes_a = keep.tile([P, WINDOW], U8, name="bytes_a", align_bytes=64)
-        bytes_b = keep.tile([P, WINDOW], U8, name="bytes_b", align_bytes=64)
-        gwords = [
-            arena.tile([P, SLOTS], U32, name=f"gwords{a}", align_bytes=256, offset=GW_AT + a * BIG)
-            for a in range(EARLY)
-        ]
-        gbytes_a = keep.tile([P, SLOTS], U8, name="gbytes_a", align_bytes=64)
-        gbytes_b = keep.tile([P, SLOTS], U8, name="gbytes_b", align_bytes=64)
+        words = keep.tile([P, (PASSES - 1) * T + WINDOW], U32, name="words", align_bytes=64)
+        planes = {what: keep.tile([P, WINDOW], U8, name=f"bytes_{what}", align_bytes=64) for what in ("a", "b")}
         banks = [psum.tile([P, 512], F32, name=f"bank{b}") for b in range(8)]
 
-        nc.gpsimd.memset(bytes_b[:], 0)
-        nc.gpsimd.memset(bytes_a[:], 0)
-        for a in range(PASSES):
-            nc.gpsimd.memset(words[a][:, T:WINDOW].bitcast(I32), 0)
+        nc.gpsimd.memset(words[:, PASSES * T :].bitcast(I32), 0)
+        nc.gpsimd.memset(planes["a"][:].bitcast(I32), 0)
+        nc.gpsimd.memset(planes["b"][:].bitcast(I32), 0)
         ident = keep.tile([P, P], F32, name="ident")
         make_identity(nc, ident[:])
 
-        def gather(dst, src, b):
-            nc.vector.tensor_copy(dst, src[:].indirect(offs_t[:, b * GATHER // 16 : (b + 1) * GATHER // 16]))
+        gathered = {}
 
-        def gather_all(dst, src):
-            for b in range(RANGES):
-                gather(dst[:, b * GATHER : (b + 1) * GATHER], src, b)
+        def gather(what, half, at):
+            if what in planes:
+                window, dtype = planes[what][:], U8
+            else:
+                first = (PASSES - 1 - what) * T
+                window, dtype = words[:, first : first + WINDOW], U32
+            dst = arena.tile([P, HALF], dtype, name=f"gathered_{what}_{half}", align_bytes=256, offset=at)
+            nc.vector.tensor_copy(dst[:], window.indirect(offs_t[:, half * HALF // 16 : (half + 1) * HALF // 16]))
+            gathered[what, half] = dst
 
         def interleave(eng, dst, src):
             if eng == "scalar":
                 nc.scalar.copy(dst, src)
-            elif eng == "gpsimd":
-                nc.gpsimd.tensor_scalar(dst, src, 1.0, 0.0, MULT, ADD)
             else:
                 nc.vector.tensor_copy(dst, src)
 
         for a in range(PASSES):
-            raw = arena.tile([P, 4, T], F32, name=f"xraw{a}", align_bytes=256, offset=XRAW_AT[a])
+            raw = arena.tile([P, 4, T], F32, name=f"xraw{a}", align_bytes=256, offset=a * XRAW)
             nc.sync.dma_start(raw[:], xT[512 * a : 512 * (a + 1), :].rearrange("(p j) t -> p j t", j=4))
             if a == 0:
                 nc.sync.dma_start(offs_t[:], offs)
@@ -115,163 +111,147 @@ def tile_moe_tk_lin_none_kernel(tc, xT, w, gate, offs, pos1, pos2, pos3, pos4, o
                     raw[:, :, lo:hi].rearrange("p t (c i) -> p c t i", i=WALK),
                 )
             flat = grp[:].rearrange("p t j -> p (t j)")
-            plane, k = (bytes_a, 4 * a) if a < 4 else (bytes_b, 0)
+            plane, k = (planes["a"], 4 * a) if a < 4 else (planes["b"], 0)
+            first = (PASSES - 1 - a) * T
             for lo, hi in ((0, 512), (512, T)):
                 nc.vector.quantize_mx(
-                    out=words[a][:, lo:hi].bitcast(FP8X4),
+                    out=words[:, first + lo : first + hi].bitcast(FP8X4),
                     scales=plane[k:P, lo:hi],
                     in_=flat[:, 4 * lo : 4 * hi],
                 )
-            if a == 0:
-                gather_all(gwords[0], words[0])
-            if a == 2:
-                gather_all(gwords[1], words[1])
-        gather_all(gbytes_a, bytes_a)
-        gather_all(gbytes_b, bytes_b)
+            gather(a, 0, EARLY_AT + a * HALF * 4)
 
         w_slabs = w.rearrange("e (a p j) n -> p (e a) (j n)", a=PASSES, j=4)
         bank_of = {e: (b, i) for b, es in enumerate(BANK_EXPERTS) for i, e in enumerate(es)}
-        firsts = [sum(CHUNKS[:i]) for i in range(len(CHUNKS))]
-        quantised = {}
-        late = {}
+        y = arena.tile([P, SLOTS], F32, name="y", align_bytes=256, offset=Y_AT)
+        waiting = []
+        closed = []
 
-        def grp_at(ci):
-            if ci in LATE_AFTER:
-                return LATE_AT + LATE_AFTER[ci] * GRP
-            if ci == 0:
-                return Y_AT
-            if ci == GATE_AFTER:
-                return GATE_AT
-            if ci < FULL_CHUNKS:
-                return LATE_AT + (ci - len(LATE) - 1 - (ci > GATE_AFTER)) * 2 * GRP + GRP // 2
-            return PROD_AT + sum(widths[FULL_CHUNKS:ci]) * (GRP // 4)
-
-        def round_slabs(eng, grp, to, raw, u0, u1):
-            interleave(
-                eng,
-                grp[:, to : to + u1 - u0].rearrange("p u (c i) t -> p u c t i", i=WALK),
-                raw[:, u0:u1].rearrange("p u t (c i) -> p u c t i", i=WALK),
-            )
-
-        last = len(CHUNKS) - 1
-        deferred = [1 if ci >= VECTOR_FROM and s > 1 else 0 for ci, s in enumerate(CHUNKS)]
-        carried = [0] + deferred[:-1]
-        widths = [s + c - d for s, c, d in zip(CHUNKS, carried, deferred)]
-        grps = {}
-
-        def grp_of(ci):
-            if ci not in grps:
-                grps[ci] = arena.tile([P, widths[ci], N, 4], BF16, name=f"wgrp{ci}", align_bytes=256, offset=grp_at(ci))
-            return grps[ci]
-
-        raws = {}
-
-        def load(ci):
-            if ci < PAIRED and ci % 2:
-                return
-            place, size = firsts[ci], CHUNKS[ci] * (2 if ci < PAIRED else 1)
-            raw_at = WRAW_AT[place // 4 % RING] + place % 4 * (RAW // 4)
-            if ci == Y_AFTER:
-                raw_at = Y_AT
-            raw = arena.tile([P, size, 4, N], F32, name=f"wraw{ci}", align_bytes=256, offset=raw_at)
+        def load(name, place, size, at):
+            raw = arena.tile([P, size, 4, N], F32, name=name, align_bytes=256, offset=at)
             source = w_slabs[:, ORDER[place] : ORDER[place] + size, :]
             nc.sync.dma_start(raw[:].rearrange("p u j n -> p u (j n)"), source)
-            raws[ci] = raw[:, 0 : CHUNKS[ci]]
-            if ci < PAIRED:
-                raws[ci + 1] = raw[:, CHUNKS[ci] : size]
+            return raw
 
-        def prepare(ci):
-            size, raw = CHUNKS[ci], raws.pop(ci)
-            grp = grp_of(ci)
-            at = carried[ci]
-            if ci < VECTOR_FROM and ci % 2 == 0:
-                round_slabs("scalar", grp, at, raw, 0, size - 1)
-                round_slabs("gpsimd", grp, at + size - 1, raw, size - 1, size)
-            else:
-                round_slabs("scalar", grp, at, raw, 0, size - deferred[ci])
-                if deferred[ci]:
-                    round_slabs("vector", grp_of(ci + 1), 0, raw, size - deferred[ci], size)
-            for cj in range(ci + 1, len(CHUNKS)):
-                if firsts[cj] // 4 + (cj < PAIRED) == ci + RING:
-                    load(cj)
+        def grouped(name, size, at):
+            return arena.tile([P, size, N, 4], BF16, name=name, align_bytes=256, offset=at)
+
+        def round_slabs(eng, dst, src):
+            interleave(
+                eng,
+                dst.rearrange("p u (c i) t -> p u c t i", i=WALK),
+                src.rearrange("p u t (c i) -> p u c t i", i=WALK),
+            )
+
+        def quantise(grp, place, size):
             codes = wq_pool.tile([P, 4 * N], U32, name="wcodes", align_bytes=64)
             scales = wq_pool.tile([P, 4 * N], U8, name="wscales", align_bytes=64)
-            for u0, u1 in ((0, 1), (1, 3)) if widths[ci] == 3 else ((0, widths[ci]),):
-                nc.vector.quantize_mx(
-                    out=codes[:, u0 * N : u1 * N].bitcast(FP8X4),
-                    scales=scales[:, u0 * N : u1 * N],
-                    in_=grp[:, u0:u1].rearrange("p u n j -> p (u n j)"),
-                )
-            quantised[ci] = (codes, scales)
-            if ci in LATE_AFTER:
-                b, a = LATE[LATE_AFTER[ci]]
-                late_at = grp_at(ci) + LATE_AFTER[ci] % 2 * (GRP // 2)
-                late[b, a] = arena.tile([P, GATHER], U32, name=f"late{b}_{a}", align_bytes=256, offset=late_at)
-                gather(late[b, a][:], words[a], b)
-
-        def multiply(ci):
-            place, size = firsts[ci] - carried[ci], widths[ci]
-            codes, scales = quantised.pop(ci)
+            nc.vector.quantize_mx(
+                out=codes[:, 0 : size * N].bitcast(FP8X4),
+                scales=scales[:, 0 : size * N],
+                in_=grp[:].rearrange("p u n j -> p (u n j)"),
+            )
             for u in range(size):
-                e, a = divmod(ORDER[place + u], PASSES)
+                waiting.append((place + u, codes[:, u * N : (u + 1) * N], scales[:, u * N : (u + 1) * N]))
+
+        def multiply():
+            for slab in list(waiting):
+                place, codes, scales = slab
+                e, a = divmod(ORDER[place], PASSES)
+                half, at = divmod(e * C, HALF)
+                if any((what, half) not in gathered for what in ["a", "b"] + list(range(PASSES))):
+                    return
+                waiting.remove(slab)
                 b, i = bank_of[e]
-                here = slice(e * C, (e + 1) * C)
-                plane, k = (gbytes_a, 4 * a) if a < 4 else (gbytes_b, 0)
-                if a < EARLY:
-                    rhs = gwords[a][:, here]
-                else:
-                    rhs = late[e * C // GATHER, a][:, e * C % GATHER : e * C % GATHER + C]
+                plane, k = (gathered["a", half], 4 * a) if a < 4 else (gathered["b", half], 0)
                 nc.tensor.matmul_mx(
                     out=banks[b][:, i * C : (i + 1) * C],
-                    lhsT=codes[:, u * N : (u + 1) * N].bitcast(FP8X4),
-                    lhsT_scale=scales[:, u * N : (u + 1) * N],
-                    rhs=rhs.bitcast(FP8X4),
-                    rhs_scale=plane[k:P, here],
+                    lhsT=codes.bitcast(FP8X4),
+                    lhsT_scale=scales,
+                    rhs=gathered[a, half][:, at : at + C].bitcast(FP8X4),
+                    rhs_scale=plane[k:P, at : at + C],
                     start=(a == 0),
                     stop=(a == PASSES - 1),
                 )
+                if a == PASSES - 1 and e == BANK_EXPERTS[b][-1]:
+                    closed.append(b)
 
-        y = arena.tile([P, SLOTS], F32, name="y", align_bytes=256, offset=Y_AT)
+        def evacuate():
+            for b in closed:
+                first = BANK_EXPERTS[b][0] * C
+                width = len(BANK_EXPERTS[b]) * C
+                if BANK_ENGINE[b] == "scalar":
+                    nc.scalar.copy(y[:, first : first + width], banks[b][:, 0:width])
+                else:
+                    nc.vector.tensor_copy(y[:, first : first + width], banks[b][:, 0:width])
+            closed.clear()
 
-        def evacuate(b):
-            first = BANK_EXPERTS[b][0] * C
-            width = len(BANK_EXPERTS[b]) * C
-            nc.scalar.copy(y[:, first : first + width], banks[b][:, 0:width])
+        loads = [(FIRST + k * PERIOD, PERIOD, k * PERIOD % RING) for k in range(len(LATE))]
+        for size in CHUNKS:
+            place, before, at = loads[-1]
+            loads.append((place + before, size, at + before if at + before + size <= RING else 0))
+        raws = {}
 
-        evac_at = {}
-        for b, es in enumerate(BANK_EXPERTS):
-            place = ORDER.index(es[-1] * PASSES + PASSES - 1)
-            closed = max(i for i, f in enumerate(firsts) if f - carried[i] <= place)
-            evac_at.setdefault(max(closed + 1, Y_AFTER + 1 + b), []).append(b)
-        for ci in range(RING):
-            load(ci)
-        for ci in range(FIRST_MULTIPLY + 1):
-            prepare(ci)
-        for ci in range(FIRST_MULTIPLY):
-            multiply(ci)
-        for ci in range(FIRST_MULTIPLY + 1, len(CHUNKS) + 1):
-            if ci < len(CHUNKS):
-                prepare(ci)
-            if ci == last:
-                gate_t = arena.tile([P, 3, T], F32, name="gate_t", align_bytes=256, offset=GATE_AT)
-                lists = (pos1, pos2, pos3, pos4)
-                for r in (0, 2):
-                    nc.sync.dma_start(pos_t[r][:], lists[r])
-                nc.sync.dma_start(gate_t[:, 0, :], gate[0])
-                for r in (3, 1):
-                    nc.sync.dma_start(pos_t[r][:], lists[r])
-                nc.sync.dma_start(gate_t[:, 1, :], gate[1])
-                col_at = grp_at(GATE_AFTER + 1)
-                gate_col = arena.tile([P, 2 * COL_STEP], F32, name="gate_col", align_bytes=256, offset=col_at)
-                with nc.allow_non_contiguous_dma(reason="one weight a token and partition"):
-                    for r in (2, 3):
-                        tokens = SHARE if r == 2 else T
-                        columns = gate_col[:, (r - 2) * COL_STEP : (r - 2) * COL_STEP + tokens // P]
-                        nc.sync.dma_start(columns, gate[r, 0, 0:tokens].rearrange("(j p) -> p j", p=P))
-                nc.sync.dma_start(gate_t[:, 2, SHARE:T], gate[2, :, SHARE:T])
-            multiply(ci - 1)
-            for b in evac_at.get(ci, []):
-                evacuate(b)
+        def refill(done):
+            for j in range(len(raws), len(loads)):
+                place, size, at = loads[j]
+                if any(a < at + size and at < a + s for p, s, a in loads[done + 1 : j]):
+                    return
+                raws[j] = load(f"wraw{j}", place, size, at * RAW)
+
+        raw = load("wraw_first", 0, FIRST, FIRST_AT)
+        grp = grouped("wgrp_first", FIRST, Y_AT + BY_GPSIMD * GRP)
+        round_slabs("scalar", grp[:], raw[:])
+        refill(-1)
+        quantise(grp, 0, FIRST)
+
+        for k, (what, half) in enumerate(LATE):
+            place, raw = loads[k][0], raws[k]
+            border = LATE_AT[k] + OUT_ROOM[k]
+            grp = grouped(f"wgrp_s{k}", BY_SCALAR, border - 2 * GRP)
+            round_slabs("scalar", grp[:], raw[:, 0:BY_SCALAR])
+            if k > Y_AFTER:
+                evacuate()
+            quantise(grp, place, BY_SCALAR)
+            gather(what, half, LATE_AT[k])
+            grp = grouped(f"wgrp_g{k}", BY_GPSIMD, border)
+            columns = raw[:, BY_SCALAR:PERIOD].rearrange("p u t n -> p u n t")
+            nc.gpsimd.tensor_scalar(grp[:], columns, 1.0, 0.0, MULT, ADD)
+            refill(k)
+            quantise(grp, place + BY_SCALAR, BY_GPSIMD)
+            multiply()
+
+        carried = [0] + BY_VECTOR[:-1]
+        widths = [s + c - d for s, c, d in zip(CHUNKS, carried, BY_VECTOR)]
+        places = {GATE_AFTER: GATE_AT, GATE_AFTER + 1: COL_AT}
+        grps = [grouped(f"wgrp{i}", wd, places.get(i, GRP_AT + i % 4 * 4 * GRP)) for i, wd in enumerate(widths)]
+        for i, size in enumerate(CHUNKS):
+            j = len(LATE) + i
+            place, raw, own = loads[j][0], raws[j], size - BY_VECTOR[i]
+            round_slabs("scalar", grps[i][:, carried[i] :], raw[:, 0:own])
+            if BY_VECTOR[i]:
+                round_slabs("vector", grps[i + 1][:, 0 : BY_VECTOR[i]], raw[:, own:size])
+            refill(j)
+            quantise(grps[i], place - carried[i], widths[i])
+            evacuate()
+            multiply()
+        evacuate()
+
+        gate_t = arena.tile([P, 3, T], F32, name="gate_t", align_bytes=256, offset=GATE_AT)
+        lists = (pos1, pos2, pos3, pos4)
+        for r in (0, 2):
+            nc.sync.dma_start(pos_t[r][:], lists[r])
+        nc.sync.dma_start(gate_t[:, 0, :], gate[0])
+        for r in (3, 1):
+            nc.sync.dma_start(pos_t[r][:], lists[r])
+        nc.sync.dma_start(gate_t[:, 1, :], gate[1])
+        gate_col = arena.tile([P, 2 * COL_STEP], F32, name="gate_col", align_bytes=256, offset=COL_AT)
+        with nc.allow_non_contiguous_dma(reason="one weight a token and partition"):
+            for r in (2, 3):
+                tokens = SHARE if r == 2 else T
+                columns = gate_col[:, (r - 2) * COL_STEP : (r - 2) * COL_STEP + tokens // P]
+                nc.sync.dma_start(columns, gate[r, 0, 0:tokens].rearrange("(j p) -> p j", p=P))
+        nc.sync.dma_start(gate_t[:, 2, SHARE:T], gate[2, :, SHARE:T])
 
         whole, shared, rest = slice(0, T), slice(0, SHARE), slice(SHARE, T)
         blocks = {2: SHARE // P, 3: T // P}
@@ -279,12 +259,12 @@ def tile_moe_tk_lin_none_kernel(tc, xT, w, gate, offs, pos1, pos2, pos3, pos4, o
         def floats(name, width, at):
             return arena.tile([P, width], F32, name=name, align_bytes=256, offset=at)
 
-        prod = [floats(f"prod{r}", T if r < 2 else T - SHARE, PROD_AT + r * T * 4) for r in range(3)]
-        picked = {r: floats(f"picked{r}", blocks[r] * P, GW_AT + r * T * 4) for r in (2, 3)}
-        scaled = {r: floats(f"scaled{r}", blocks[r] * P, GW_AT + (r - 2) * T * 4) for r in (2, 3)}
-        pair = floats("pair", T, XRAW_AT[4])
-        triple = floats("triple", T - SHARE, XRAW_AT[4] + T * 4)
-        res = floats("res", T, XRAW_AT[4] + 2 * T * 4)
+        prod = [floats(f"prod{r}", T if r < 2 else T - SHARE, EARLY_AT + r * ROW) for r in range(3)]
+        picked = {r: floats(f"picked{r}", blocks[r] * P, EARLY_AT + (r + 1) * ROW) for r in (2, 3)}
+        scaled = {r: floats(f"scaled{r}", blocks[r] * P, EARLY_AT + (r + 3) * ROW) for r in (2, 3)}
+        pair = floats("pair", T, EARLY_AT + 7 * ROW)
+        triple = floats("triple", T - SHARE, EARLY_AT + 8 * ROW)
+        res = floats("res", T, EARLY_AT + 9 * ROW)
 
         def window(r, cols):
             return y[:].indirect(pos_t[r][:, cols.start // 16 : cols.stop // 16])

@@ -28,7 +28,7 @@ FIRST = 4
 BY_SCALAR, BY_GPSIMD = 4, 3
 PERIOD = BY_SCALAR + BY_GPSIMD
 CHUNKS = [4] * 6 + [3, 2, 2, 1, 1]
-BY_VECTOR = [0] + [2] * 5 + [1] * 3 + [0, 0]
+BY_VECTOR = [0] * 3 + [1] * 6 + [0, 0]
 ORDER = list(range(SLABS - PASSES - 1)) + list(range(SLABS - PASSES, SLABS - 1)) + [SLABS - PASSES - 1, SLABS - 1]
 BANK_EXPERTS = [[0, 1, 2, 3], [4, 5, 6, 7], [8, 9, 10, 11], [12, 13, 14, 15], [16, 17, 18], [19]]
 BANK_ENGINE = ["scalar", "scalar", "vector", "vector", "scalar", "scalar"]

@@ -27,8 +27,9 @@ LATE = [("a", 0), ("b", 0), ("a", 1), ("b", 1)] + [(a, 1) for a in range(PASSES)
 FIRST = 4
 BY_SCALAR, BY_GPSIMD = 4, 3
 PERIOD = BY_SCALAR + BY_GPSIMD
-CHUNKS = [4] * 6 + [3, 2, 2, 1, 1]
-BY_VECTOR = [0] * 3 + [1] * 6 + [0, 0]
+FULL = 6
+CHUNKS = [4] * FULL + [3, 2, 2, 1, 1]
+HELPER = [None] * 3 + ["gpsimd"] * 3 + ["vector"] * 3 + [None] * 2
 ORDER = list(range(SLABS - PASSES - 1)) + list(range(SLABS - PASSES, SLABS - 1)) + [SLABS - PASSES - 1, SLABS - 1]
 BANK_EXPERTS = [[0, 1, 2, 3], [4, 5, 6, 7], [8, 9, 10, 11], [12, 13, 14, 15], [16, 17, 18], [19]]
 BANK_ENGINE = ["scalar", "scalar", "vector", "vector", "scalar", "scalar"]
@@ -46,9 +47,12 @@ GRP = N * 4 * 2
 XRAW = 4 * T * 4
 XGRP = XRAW // 2
 ROW = T * 4
-RING = 4 * PERIOD
-FIRST_AT = PASSES * XRAW
-EARLY_AT = FIRST_AT + FIRST * RAW
+X_AT = RAW
+FIRST_AT = 2 * RAW
+OWN_AT = [15 * RAW, 25 * RAW, 0, 8 * RAW]
+REST_AT = [19 * RAW, 22 * RAW, 4 * RAW, 12 * RAW]
+CHUNK_RING = [(OWN_AT[1], 5), (OWN_AT[2], 6), (REST_AT[2], 6), (OWN_AT[3], 7), (OWN_AT[0], 8)]
+EARLY_AT = 29 * RAW
 GRP_AT = EARLY_AT + PASSES * HALF * 4
 GATE_AT = GRP_AT + 4 * 4 * GRP
 COL_AT = GATE_AT + 8 * GRP
@@ -56,7 +60,7 @@ OUT_ROOM = [2 * GRP if what in ("a", "b") else HALF * 4 for what, half in LATE]
 ROOM = [OUT_ROOM[k] + (SLOTS * 4 if k == Y_AFTER else BY_GPSIMD * GRP) for k in range(len(LATE))]
 LATE_AT = [COL_AT + 4 * GRP + sum(ROOM[:k]) for k in range(len(LATE))]
 Y_AT = LATE_AT[Y_AFTER] + OUT_ROOM[Y_AFTER]
-XGRP_AT = [GRP_AT, GRP_AT + XGRP, GRP_AT + 2 * XGRP, LATE_AT[-2], LATE_AT[-1]]
+XGRP_AT = [GRP_AT, GRP_AT + XGRP, GRP_AT + 2 * XGRP, LATE_AT[-1], 11 * RAW]
 
 
 def tile_moe_tk_lin_none_kernel(tc, xT, w, gate, offs, pos1, pos2, pos3, pos4, out):
@@ -99,7 +103,7 @@ def tile_moe_tk_lin_none_kernel(tc, xT, w, gate, offs, pos1, pos2, pos3, pos4, o
                 nc.vector.tensor_copy(dst, src)
 
         for a in range(PASSES):
-            raw = arena.tile([P, 4, T], F32, name=f"xraw{a}", align_bytes=256, offset=a * XRAW)
+            raw = arena.tile([P, 4, T], F32, name=f"xraw{a}", align_bytes=256, offset=X_AT + a * XRAW)
             nc.sync.dma_start(raw[:], xT[512 * a : 512 * (a + 1), :].rearrange("(p j) t -> p j t", j=4))
             if a == 0:
                 nc.sync.dma_start(offs_t[:], offs)
@@ -127,10 +131,10 @@ def tile_moe_tk_lin_none_kernel(tc, xT, w, gate, offs, pos1, pos2, pos3, pos4, o
         waiting = []
         closed = []
 
-        def load(name, place, size, at):
+        def load(queue, name, place, size, at):
             raw = arena.tile([P, size, 4, N], F32, name=name, align_bytes=256, offset=at)
             source = w_slabs[:, ORDER[place] : ORDER[place] + size, :]
-            nc.sync.dma_start(raw[:].rearrange("p u j n -> p u (j n)"), source)
+            queue.dma_start(raw[:].rearrange("p u j n -> p u (j n)"), source)
             return raw
 
         def grouped(name, size, at):
@@ -186,53 +190,76 @@ def tile_moe_tk_lin_none_kernel(tc, xT, w, gate, offs, pos1, pos2, pos3, pos4, o
                     nc.vector.tensor_copy(y[:, first : first + width], banks[b][:, 0:width])
             closed.clear()
 
-        loads = [(FIRST + k * PERIOD, PERIOD, k * PERIOD % RING) for k in range(len(LATE))]
-        for size in CHUNKS:
-            place, before, at = loads[-1]
-            loads.append((place + before, size, at + before if at + before + size <= RING else 0))
+        def round_on_gpsimd(dst, src):
+            nc.gpsimd.tensor_scalar(dst, src.rearrange("p u t n -> p u n t"), 1.0, 0.0, MULT, ADD)
+
+        firsts = [FIRST + k * PERIOD for k in range(len(LATE))]
+        owns, rests = {}, {}
+
+        def load_own(k):
+            if k < len(LATE):
+                owns[k] = load(nc.scalar, f"wown{k}", firsts[k], BY_SCALAR, OWN_AT[k % 4])
+
+        def load_rest(k):
+            if k < len(LATE):
+                rests[k] = load(nc.sync, f"wrest{k}", firsts[k] + BY_SCALAR, BY_GPSIMD, REST_AT[k % 4])
+
+        starts = [FIRST + len(LATE) * PERIOD + sum(CHUNKS[:i]) for i in range(len(CHUNKS))]
+        seats = [(0, 0)]
+        for before, size in zip(CHUNKS, CHUNKS[1:]):
+            seat, at = seats[-1]
+            seats.append((seat, at + before) if at + before + size <= 4 else (seat + 1, 0))
         raws = {}
 
-        def refill(done):
-            for j in range(len(raws), len(loads)):
-                place, size, at = loads[j]
-                if any(a < at + size and at < a + s for p, s, a in loads[done + 1 : j]):
-                    return
-                raws[j] = load(f"wraw{j}", place, size, at * RAW)
+        def load_seat(seat):
+            for i, (s, at) in enumerate(seats):
+                if s == seat:
+                    base = CHUNK_RING[seat % len(CHUNK_RING)][0]
+                    raws[i] = load(nc.sync, f"wraw{i}", starts[i], CHUNKS[i], base + at * RAW)
 
-        raw = load("wraw_first", 0, FIRST, FIRST_AT)
+        raw = load(nc.sync, "wraw_first", 0, FIRST, FIRST_AT)
+        for j in range(3):
+            load_own(j)
+            load_rest(j)
         grp = grouped("wgrp_first", FIRST, Y_AT + BY_GPSIMD * GRP)
         round_slabs("scalar", grp[:], raw[:])
-        refill(-1)
+        load_own(3)
+        load_rest(3)
         quantise(grp, 0, FIRST)
 
         for k, (what, half) in enumerate(LATE):
-            place, raw = loads[k][0], raws[k]
             border = LATE_AT[k] + OUT_ROOM[k]
             grp = grouped(f"wgrp_s{k}", BY_SCALAR, border - 2 * GRP)
-            round_slabs("scalar", grp[:], raw[:, 0:BY_SCALAR])
+            round_slabs("scalar", grp[:], owns[k][:])
+            load_own(k + 4)
             if k > Y_AFTER:
                 evacuate()
-            quantise(grp, place, BY_SCALAR)
+            quantise(grp, firsts[k], BY_SCALAR)
             gather(what, half, LATE_AT[k])
             grp = grouped(f"wgrp_g{k}", BY_GPSIMD, border)
-            columns = raw[:, BY_SCALAR:PERIOD].rearrange("p u t n -> p u n t")
-            nc.gpsimd.tensor_scalar(grp[:], columns, 1.0, 0.0, MULT, ADD)
-            refill(k)
-            quantise(grp, place + BY_SCALAR, BY_GPSIMD)
+            round_on_gpsimd(grp[:], rests[k][:])
+            load_rest(k + 4)
+            for seat, (at, period) in enumerate(CHUNK_RING):
+                if period == k:
+                    load_seat(seat)
+            quantise(grp, firsts[k] + BY_SCALAR, BY_GPSIMD)
             multiply()
 
-        carried = [0] + BY_VECTOR[:-1]
-        widths = [s + c - d for s, c, d in zip(CHUNKS, carried, BY_VECTOR)]
+        helped = [1 if h else 0 for h in HELPER]
+        carried = [0] + helped[:-1]
+        widths = [s + c - d for s, c, d in zip(CHUNKS, carried, helped)]
         places = {GATE_AFTER: GATE_AT, GATE_AFTER + 1: COL_AT}
         grps = [grouped(f"wgrp{i}", wd, places.get(i, GRP_AT + i % 4 * 4 * GRP)) for i, wd in enumerate(widths)]
         for i, size in enumerate(CHUNKS):
-            j = len(LATE) + i
-            place, raw, own = loads[j][0], raws[j], size - BY_VECTOR[i]
-            round_slabs("scalar", grps[i][:, carried[i] :], raw[:, 0:own])
-            if BY_VECTOR[i]:
-                round_slabs("vector", grps[i + 1][:, 0 : BY_VECTOR[i]], raw[:, own:size])
-            refill(j)
-            quantise(grps[i], place - carried[i], widths[i])
+            own = size - helped[i]
+            round_slabs("scalar", grps[i][:, carried[i] :], raws[i][:, 0:own])
+            if HELPER[i] == "vector":
+                round_slabs("vector", grps[i + 1][:, 0:1], raws[i][:, own:size])
+            if HELPER[i] == "gpsimd":
+                round_on_gpsimd(grps[i + 1][:, 0:1], raws[i][:, own:size])
+            if seats[i][1] == 0:
+                load_seat(seats[i][0] + len(CHUNK_RING))
+            quantise(grps[i], starts[i] - carried[i], widths[i])
             evacuate()
             multiply()
         evacuate()

@@ -21,8 +21,8 @@ ADD = mybir.AluOpType.add
 COPY = mybir.ActivationFunctionType.Copy
 
 SLABS = E * PASSES
-HALF = SLOTS // 2
-WINDOW = 1712
+RANGES = [(0, 11 * C), (11 * C, 9 * C)]
+WINDOW = 1888
 LATE = [("a", 0), ("b", 0), ("a", 1), ("b", 1)] + [(a, 1) for a in range(PASSES)]
 FIRST = 4
 BY_SCALAR, BY_GPSIMD = 4, 3
@@ -31,12 +31,11 @@ FULL = 6
 CHUNKS = [4] * FULL + [3, 2, 2, 1, 1]
 HELPER = [None] * 3 + ["gpsimd"] * 3 + ["vector"] * 3 + [None] * 2
 ORDER = list(range(SLABS - PASSES - 1)) + list(range(SLABS - PASSES, SLABS - 1)) + [SLABS - PASSES - 1, SLABS - 1]
-BANK_EXPERTS = [[0, 1, 2, 3], [4, 5, 6, 7], [8, 9, 10, 11], [12, 13, 14, 15], [16, 17, 18], [19]]
-BANK_ENGINE = ["scalar", "scalar", "vector", "vector", "scalar", "scalar"]
+BANK_EXPERTS = [[0, 1, 2, 3], [4, 5, 6, 7], [8, 9, 10], [11, 12, 13, 14], [15, 16, 17, 18], [19]]
+VECTOR_BANK = 3
 WALK = 4
 X_SCALAR = 256
-Y_AFTER = 4
-GATE_AFTER = 3
+GATE_AFTER = 5
 SHARE = 384
 SPLIT = 384
 COL_STEP = 8
@@ -47,19 +46,21 @@ GRP = N * 4 * 2
 XRAW = 4 * T * 4
 XGRP = XRAW // 2
 ROW = T * 4
-X_AT = RAW
+X_AT = 3 * RAW
 FIRST_AT = 2 * RAW
-OWN_AT = [15 * RAW, 25 * RAW, 0, 8 * RAW]
-REST_AT = [19 * RAW, 22 * RAW, 4 * RAW, 12 * RAW]
-CHUNK_RING = [(OWN_AT[1], 5), (OWN_AT[2], 6), (REST_AT[2], 6), (OWN_AT[3], 7), (OWN_AT[0], 8)]
-EARLY_AT = 29 * RAW
-GRP_AT = EARLY_AT + PASSES * HALF * 4
+OWN_AT = [16 * RAW, 26 * RAW, 0, 8 * RAW]
+REST_AT = [20 * RAW, 23 * RAW, 4 * RAW, 13 * RAW]
+CHUNK_RING = [(OWN_AT[1], 5), (OWN_AT[2], 6), (REST_AT[2], 6), (OWN_AT[0], 8)]
+FREED_BY_GPSIMD = 2
+Y_AFTER = 7
+Y_AT = OWN_AT[Y_AFTER % 4]
+EARLY_AT = 30 * RAW
+GRP_AT = EARLY_AT + PASSES * RANGES[0][1] * 4
 GATE_AT = GRP_AT + 4 * 4 * GRP
 COL_AT = GATE_AT + 8 * GRP
-OUT_ROOM = [2 * GRP if what in ("a", "b") else HALF * 4 for what, half in LATE]
-ROOM = [OUT_ROOM[k] + (SLOTS * 4 if k == Y_AFTER else BY_GPSIMD * GRP) for k in range(len(LATE))]
+OUT_ROOM = [2 * GRP if what in ("a", "b") else RANGES[g][1] * 4 for what, g in LATE]
+ROOM = [room + BY_GPSIMD * GRP for room in OUT_ROOM]
 LATE_AT = [COL_AT + 4 * GRP + sum(ROOM[:k]) for k in range(len(LATE))]
-Y_AT = LATE_AT[Y_AFTER] + OUT_ROOM[Y_AFTER]
 XGRP_AT = [GRP_AT, GRP_AT + XGRP, GRP_AT + 2 * XGRP, LATE_AT[-1], 11 * RAW]
 
 
@@ -86,15 +87,16 @@ def tile_moe_tk_lin_none_kernel(tc, xT, w, gate, offs, pos1, pos2, pos3, pos4, o
 
         gathered = {}
 
-        def gather(what, half, at):
+        def gather(what, g, at):
             if what in planes:
                 window, dtype = planes[what][:], U8
             else:
                 first = (PASSES - 1 - what) * T
                 window, dtype = words[:, first : first + WINDOW], U32
-            dst = arena.tile([P, HALF], dtype, name=f"gathered_{what}_{half}", align_bytes=256, offset=at)
-            nc.vector.tensor_copy(dst[:], window.indirect(offs_t[:, half * HALF // 16 : (half + 1) * HALF // 16]))
-            gathered[what, half] = dst
+            lo, size = RANGES[g]
+            dst = arena.tile([P, size], dtype, name=f"gathered_{what}_{g}", align_bytes=256, offset=at)
+            nc.vector.tensor_copy(dst[:], window.indirect(offs_t[:, lo // 16 : (lo + size) // 16]))
+            gathered[what, g] = dst
 
         def interleave(eng, dst, src):
             if eng == "scalar":
@@ -123,7 +125,7 @@ def tile_moe_tk_lin_none_kernel(tc, xT, w, gate, offs, pos1, pos2, pos3, pos4, o
                     scales=plane[k:P, lo:hi],
                     in_=flat[:, 4 * lo : 4 * hi],
                 )
-            gather(a, 0, EARLY_AT + a * HALF * 4)
+            gather(a, 0, EARLY_AT + a * RANGES[0][1] * 4)
 
         w_slabs = w.rearrange("e (a p j) n -> p (e a) (j n)", a=PASSES, j=4)
         bank_of = {e: (b, i) for b, es in enumerate(BANK_EXPERTS) for i, e in enumerate(es)}
@@ -162,17 +164,18 @@ def tile_moe_tk_lin_none_kernel(tc, xT, w, gate, offs, pos1, pos2, pos3, pos4, o
             for slab in list(waiting):
                 place, codes, scales = slab
                 e, a = divmod(ORDER[place], PASSES)
-                half, at = divmod(e * C, HALF)
-                if any((what, half) not in gathered for what in ["a", "b"] + list(range(PASSES))):
+                g = 0 if e * C < RANGES[1][0] else 1
+                at = e * C - RANGES[g][0]
+                if any((what, g) not in gathered for what in ["a", "b"] + list(range(PASSES))):
                     return
                 waiting.remove(slab)
                 b, i = bank_of[e]
-                plane, k = (gathered["a", half], 4 * a) if a < 4 else (gathered["b", half], 0)
+                plane, k = (gathered["a", g], 4 * a) if a < 4 else (gathered["b", g], 0)
                 nc.tensor.matmul_mx(
                     out=banks[b][:, i * C : (i + 1) * C],
                     lhsT=codes.bitcast(FP8X4),
                     lhsT_scale=scales,
-                    rhs=gathered[a, half][:, at : at + C].bitcast(FP8X4),
+                    rhs=gathered[a, g][:, at : at + C].bitcast(FP8X4),
                     rhs_scale=plane[k:P, at : at + C],
                     start=(a == 0),
                     stop=(a == PASSES - 1),
@@ -180,15 +183,15 @@ def tile_moe_tk_lin_none_kernel(tc, xT, w, gate, offs, pos1, pos2, pos3, pos4, o
                 if a == PASSES - 1 and e == BANK_EXPERTS[b][-1]:
                     closed.append(b)
 
-        def evacuate():
-            for b in closed:
+        def evacuate(most):
+            for b in closed[:most]:
                 first = BANK_EXPERTS[b][0] * C
                 width = len(BANK_EXPERTS[b]) * C
-                if BANK_ENGINE[b] == "scalar":
-                    nc.scalar.copy(y[:, first : first + width], banks[b][:, 0:width])
-                else:
+                if b == VECTOR_BANK:
                     nc.vector.tensor_copy(y[:, first : first + width], banks[b][:, 0:width])
-            closed.clear()
+                else:
+                    nc.scalar.copy(y[:, first : first + width], banks[b][:, 0:width])
+                closed.remove(b)
 
         def round_on_gpsimd(dst, src):
             nc.gpsimd.tensor_scalar(dst, src.rearrange("p u t n -> p u n t"), 1.0, 0.0, MULT, ADD)
@@ -215,27 +218,34 @@ def tile_moe_tk_lin_none_kernel(tc, xT, w, gate, offs, pos1, pos2, pos3, pos4, o
             for i, (s, at) in enumerate(seats):
                 if s == seat:
                     base = CHUNK_RING[seat % len(CHUNK_RING)][0]
-                    raws[i] = load(nc.sync, f"wraw{i}", starts[i], CHUNKS[i], base + at * RAW)
+                    raws[i] = arena.tile(
+                        [P, CHUNKS[i], 4, N], F32, name=f"wraw{i}", align_bytes=256, offset=base + at * RAW
+                    )
+                    cut = 2 if i < FULL and i != FREED_BY_GPSIMD else 0
+                    for queue, lo, hi in ((nc.scalar, 0, cut), (nc.sync, cut, CHUNKS[i])):
+                        if hi > lo:
+                            source = w_slabs[:, ORDER[starts[i]] + lo : ORDER[starts[i]] + hi, :]
+                            queue.dma_start(raws[i][:, lo:hi].rearrange("p u j n -> p u (j n)"), source)
 
         raw = load(nc.sync, "wraw_first", 0, FIRST, FIRST_AT)
         for j in range(3):
             load_own(j)
             load_rest(j)
-        grp = grouped("wgrp_first", FIRST, Y_AT + BY_GPSIMD * GRP)
+        grp = grouped("wgrp_first", FIRST, COL_AT)
         round_slabs("scalar", grp[:], raw[:])
         load_own(3)
         load_rest(3)
         quantise(grp, 0, FIRST)
 
-        for k, (what, half) in enumerate(LATE):
+        for k, (what, g) in enumerate(LATE):
             border = LATE_AT[k] + OUT_ROOM[k]
             grp = grouped(f"wgrp_s{k}", BY_SCALAR, border - 2 * GRP)
             round_slabs("scalar", grp[:], owns[k][:])
             load_own(k + 4)
-            if k > Y_AFTER:
-                evacuate()
+            if k == Y_AFTER:
+                evacuate(2)
             quantise(grp, firsts[k], BY_SCALAR)
-            gather(what, half, LATE_AT[k])
+            gather(what, g, LATE_AT[k])
             grp = grouped(f"wgrp_g{k}", BY_GPSIMD, border)
             round_on_gpsimd(grp[:], rests[k][:])
             load_rest(k + 4)
@@ -260,9 +270,10 @@ def tile_moe_tk_lin_none_kernel(tc, xT, w, gate, offs, pos1, pos2, pos3, pos4, o
             if seats[i][1] == 0:
                 load_seat(seats[i][0] + len(CHUNK_RING))
             quantise(grps[i], starts[i] - carried[i], widths[i])
-            evacuate()
+            if i > 0:
+                evacuate(1)
             multiply()
-        evacuate()
+        evacuate(2)
 
         gate_t = arena.tile([P, 3, T], F32, name="gate_t", align_bytes=256, offset=GATE_AT)
         lists = (pos1, pos2, pos3, pos4)

@@ -33,7 +33,7 @@ HELPER = [None] * 3 + ["gpsimd"] * 3 + ["vector"] * 3 + [None] * 2
 ORDER = list(range(SLABS - PASSES - 1)) + list(range(SLABS - PASSES, SLABS - 1)) + [SLABS - PASSES - 1, SLABS - 1]
 BANK_EXPERTS = [[0, 1, 2, 3], [4, 5, 6, 7], [8, 9, 10], [11, 12, 13, 14], [15, 16, 17, 18], [19]]
 VECTOR_BANK = 3
-WALK = 4
+WALK = 2
 X_SCALAR = 256
 GATE_AFTER = 5
 SHARE = 384

@@ -48,13 +48,13 @@ XGRP = XRAW // 2
 ROW = T * 4
 X_AT = 3 * RAW
 FIRST_AT = 2 * RAW
-OWN_AT = [16 * RAW, 26 * RAW, 0, 8 * RAW]
-REST_AT = [20 * RAW, 23 * RAW, 4 * RAW, 13 * RAW]
-CHUNK_RING = [(OWN_AT[1], 5), (OWN_AT[2], 6), (REST_AT[2], 6), (OWN_AT[0], 8)]
+OWN_AT = [16 * RAW, 25 * RAW, 0, 8 * RAW]
+REST_AT = [20 * RAW, 4 * RAW, 13 * RAW]
+CHUNK_RING = [(OWN_AT[1], 5), (OWN_AT[2], 6), (REST_AT[0], 6), (OWN_AT[0], 8)]
 FREED_BY_GPSIMD = 2
 Y_AFTER = 7
 Y_AT = OWN_AT[Y_AFTER % 4]
-EARLY_AT = 30 * RAW
+EARLY_AT = 29 * RAW
 GRP_AT = EARLY_AT + PASSES * RANGES[0][1] * 4
 GATE_AT = GRP_AT + 4 * 4 * GRP
 COL_AT = GATE_AT + 8 * GRP
@@ -130,7 +130,8 @@ def tile_moe_tk_lin_none_kernel(tc, xT, w, gate, offs, pos1, pos2, pos3, pos4, o
         w_slabs = w.rearrange("e (a p j) n -> p (e a) (j n)", a=PASSES, j=4)
         bank_of = {e: (b, i) for b, es in enumerate(BANK_EXPERTS) for i, e in enumerate(es)}
         y = arena.tile([P, SLOTS], F32, name="y", align_bytes=256, offset=Y_AT)
-        waiting = []
+        waiting = {}
+        done = []
         closed = []
 
         def load(queue, name, place, size, at):
@@ -158,17 +159,18 @@ def tile_moe_tk_lin_none_kernel(tc, xT, w, gate, offs, pos1, pos2, pos3, pos4, o
                 in_=grp[:].rearrange("p u n j -> p (u n j)"),
             )
             for u in range(size):
-                waiting.append((place + u, codes[:, u * N : (u + 1) * N], scales[:, u * N : (u + 1) * N]))
+                waiting[place + u] = (codes[:, u * N : (u + 1) * N], scales[:, u * N : (u + 1) * N])
 
         def multiply():
-            for slab in list(waiting):
-                place, codes, scales = slab
+            while len(done) in waiting:
+                place = len(done)
+                codes, scales = waiting[place]
                 e, a = divmod(ORDER[place], PASSES)
                 g = 0 if e * C < RANGES[1][0] else 1
                 at = e * C - RANGES[g][0]
                 if any((what, g) not in gathered for what in ["a", "b"] + list(range(PASSES))):
                     return
-                waiting.remove(slab)
+                done.append(place)
                 b, i = bank_of[e]
                 plane, k = (gathered["a", g], 4 * a) if a < 4 else (gathered["b", g], 0)
                 nc.tensor.matmul_mx(
@@ -196,16 +198,17 @@ def tile_moe_tk_lin_none_kernel(tc, xT, w, gate, offs, pos1, pos2, pos3, pos4, o
         def round_on_gpsimd(dst, src):
             nc.gpsimd.tensor_scalar(dst, src.rearrange("p u t n -> p u n t"), 1.0, 0.0, MULT, ADD)
 
-        firsts = [FIRST + k * PERIOD for k in range(len(LATE))]
+        own_first = [FIRST + max(k * PERIOD - BY_GPSIMD, 0) for k in range(len(LATE))]
+        rest_first = [at + BY_SCALAR for at in own_first[1:]] + [own_first[-1] + PERIOD]
         owns, rests = {}, {}
 
         def load_own(k):
             if k < len(LATE):
-                owns[k] = load(nc.scalar, f"wown{k}", firsts[k], BY_SCALAR, OWN_AT[k % 4])
+                owns[k] = load(nc.scalar, f"wown{k}", own_first[k], BY_SCALAR, OWN_AT[k % 4])
 
         def load_rest(k):
             if k < len(LATE):
-                rests[k] = load(nc.sync, f"wrest{k}", firsts[k] + BY_SCALAR, BY_GPSIMD, REST_AT[k % 4])
+                rests[k] = load(nc.sync, f"wrest{k}", rest_first[k], BY_GPSIMD, REST_AT[k % 3])
 
         starts = [FIRST + len(LATE) * PERIOD + sum(CHUNKS[:i]) for i in range(len(CHUNKS))]
         seats = [(0, 0)]
@@ -228,13 +231,14 @@ def tile_moe_tk_lin_none_kernel(tc, xT, w, gate, offs, pos1, pos2, pos3, pos4, o
                             queue.dma_start(raws[i][:, lo:hi].rearrange("p u j n -> p u (j n)"), source)
 
         raw = load(nc.sync, "wraw_first", 0, FIRST, FIRST_AT)
-        for j in range(3):
-            load_own(j)
-            load_rest(j)
+        load_own(0)
+        load_own(1)
+        load_rest(0)
         grp = grouped("wgrp_first", FIRST, COL_AT)
         round_slabs("scalar", grp[:], raw[:])
-        load_own(3)
-        load_rest(3)
+        for k in (2, 3):
+            load_own(k)
+            load_rest(k - 1)
         quantise(grp, 0, FIRST)
 
         for k, (what, g) in enumerate(LATE):
@@ -244,15 +248,15 @@ def tile_moe_tk_lin_none_kernel(tc, xT, w, gate, offs, pos1, pos2, pos3, pos4, o
             load_own(k + 4)
             if k == Y_AFTER:
                 evacuate(2)
-            quantise(grp, firsts[k], BY_SCALAR)
+            quantise(grp, own_first[k], BY_SCALAR)
             gather(what, g, LATE_AT[k])
             grp = grouped(f"wgrp_g{k}", BY_GPSIMD, border)
             round_on_gpsimd(grp[:], rests[k][:])
-            load_rest(k + 4)
+            load_rest(k + 3)
             for seat, (at, period) in enumerate(CHUNK_RING):
                 if period == k:
                     load_seat(seat)
-            quantise(grp, firsts[k] + BY_SCALAR, BY_GPSIMD)
+            quantise(grp, rest_first[k], BY_GPSIMD)
             multiply()
 
         helped = [1 if h else 0 for h in HELPER]

@@ -34,7 +34,11 @@ ORDER = list(range(SLABS - PASSES - 1)) + list(range(SLABS - PASSES, SLABS - 1))
 BANK_EXPERTS = [[0, 1, 2, 3], [4, 5, 6, 7], [8, 9, 10], [11, 12, 13, 14], [15, 16, 17, 18], [19]]
 VECTOR_BANK = 3
 WALK = 2
-X_SCALAR = 256
+X_SHARES = {
+    0: [(0, 192, "scalar"), (192, 512, "vector"), (512, T, "scalar")],
+    1: [(0, 384, "scalar"), (384, T, "gpsimd")],
+    2: [(0, 512, "scalar"), (512, T, "scalar")],
+}
 GATE_AFTER = 5
 SHARE = 384
 SPLIT = 384
@@ -110,7 +114,11 @@ def tile_moe_tk_lin_none_kernel(tc, xT, w, gate, offs, pos1, pos2, pos3, pos4, o
             if a == 0:
                 nc.sync.dma_start(offs_t[:], offs)
             grp = arena.tile([P, T, 4], BF16, name=f"xgrp{a}", align_bytes=256, offset=XGRP_AT[a])
-            for lo, hi, eng in ((0, X_SCALAR, "scalar"), (X_SCALAR, T, "vector")) if a == 0 else ((0, T, "scalar"),):
+            for lo, hi, eng in X_SHARES.get(a, [(0, T, "scalar")]):
+                if eng == "gpsimd":
+                    columns = raw[:, :, lo:hi].rearrange("p t c -> p c t")
+                    nc.gpsimd.tensor_copy(grp[:, lo:hi, :], columns)
+                    continue
                 interleave(
                     eng,
                     grp[:, lo:hi, :].rearrange("p (c i) t -> p c t i", i=WALK),

@@ -30,6 +30,7 @@ PERIOD = BY_SCALAR + BY_GPSIMD
 FULL = 6
 CHUNKS = [4] * FULL + [3, 2, 2, 1, 1]
 HELPER = [None] * 3 + ["gpsimd"] * 3 + ["vector"] * 3 + [None] * 2
+HELPED = [0] * 3 + [1] * 3 + [2, 1, 1] + [0] * 2
 ORDER = list(range(SLABS - PASSES - 1)) + list(range(SLABS - PASSES, SLABS - 1)) + [SLABS - PASSES - 1, SLABS - 1]
 BANK_EXPERTS = [[0, 1, 2, 3], [4, 5, 6, 7], [8, 9, 10], [11, 12, 13, 14], [15, 16, 17, 18], [19]]
 VECTOR_BANK = 3
@@ -40,7 +41,7 @@ X_SHARES = {
     2: [(0, 512, "scalar"), (512, T, "scalar")],
 }
 GATE_AFTER = 5
-SHARE = 384
+SHARE = 512
 SPLIT = 384
 COL_STEP = 8
 CODE_BUFFERS = 8
@@ -232,8 +233,9 @@ def tile_moe_tk_lin_none_kernel(tc, xT, w, gate, offs, pos1, pos2, pos3, pos4, o
                     raws[i] = arena.tile(
                         [P, CHUNKS[i], 4, N], F32, name=f"wraw{i}", align_bytes=256, offset=base + at * RAW
                     )
-                    cut = 2 if i < FULL and i != FREED_BY_GPSIMD else 0
-                    for queue, lo, hi in ((nc.scalar, 0, cut), (nc.sync, cut, CHUNKS[i])):
+                    first = nc.scalar if i < FULL and i != FREED_BY_GPSIMD else nc.sync
+                    cut = CHUNKS[i] // 2 if i < FULL else CHUNKS[i] - HELPED[i]
+                    for queue, lo, hi in ((first, 0, cut), (nc.sync, cut, CHUNKS[i])):
                         if hi > lo:
                             source = w_slabs[:, ORDER[starts[i]] + lo : ORDER[starts[i]] + hi, :]
                             queue.dma_start(raws[i][:, lo:hi].rearrange("p u j n -> p u (j n)"), source)
@@ -267,16 +269,15 @@ def tile_moe_tk_lin_none_kernel(tc, xT, w, gate, offs, pos1, pos2, pos3, pos4, o
             quantise(grp, rest_first[k], BY_GPSIMD)
             multiply()
 
-        helped = [1 if h else 0 for h in HELPER]
-        carried = [0] + helped[:-1]
-        widths = [s + c - d for s, c, d in zip(CHUNKS, carried, helped)]
+        carried = [0] + HELPED[:-1]
+        widths = [s + c - d for s, c, d in zip(CHUNKS, carried, HELPED)]
         places = {GATE_AFTER: GATE_AT, GATE_AFTER + 1: COL_AT}
         grps = [grouped(f"wgrp{i}", wd, places.get(i, GRP_AT + i % 4 * 4 * GRP)) for i, wd in enumerate(widths)]
         for i, size in enumerate(CHUNKS):
-            own = size - helped[i]
+            own = size - HELPED[i]
             round_slabs("scalar", grps[i][:, carried[i] :], raws[i][:, 0:own])
             if HELPER[i] == "vector":
-                round_slabs("vector", grps[i + 1][:, 0:1], raws[i][:, own:size])
+                round_slabs("vector", grps[i + 1][:, 0 : HELPED[i]], raws[i][:, own:size])
             if HELPER[i] == "gpsimd":
                 round_on_gpsimd(grps[i + 1][:, 0:1], raws[i][:, own:size])
             if seats[i][1] == 0:
@@ -341,7 +342,8 @@ def tile_moe_tk_lin_none_kernel(tc, xT, w, gate, offs, pos1, pos2, pos3, pos4, o
         for r in range(3):
             cols = whole if r < 2 else rest
             nc.vector.tensor_tensor(prod[r][:], window(r, cols), gate_t[:, r, cols], MULT)
-        nc.vector.tensor_add(pair[:], prod[0][:], prod[1][:])
+        for cols in (shared, rest):
+            nc.vector.tensor_add(pair[:, cols], prod[0][:, cols], prod[1][:, cols])
         for j in range(T // P):
             if j == 1:
                 nc.vector.tensor_add(triple[:], pair[:, rest], prod[2][:])

@@ -32,8 +32,8 @@ CHUNKS = [4] * FULL + [3, 2, 2, 1, 1]
 HELPER = [None] * 3 + ["gpsimd"] * 3 + ["vector"] * 3 + [None] * 2
 HELPED = [0] * 3 + [1] * 3 + [2, 1, 1] + [0] * 2
 ORDER = list(range(SLABS - PASSES - 1)) + list(range(SLABS - PASSES, SLABS - 1)) + [SLABS - PASSES - 1, SLABS - 1]
-BANK_EXPERTS = [[0, 1, 2, 3], [4, 5, 6, 7], [8, 9, 10], [11, 12, 13, 14], [15, 16, 17, 18], [19]]
-VECTOR_BANK = 3
+BANK_EXPERTS = [[0, 1, 2, 3], [4, 5, 6, 7], [8, 9, 10], [11, 12, 13, 14], [15, 16], [17, 18], [19]]
+VECTOR_BANKS = (3, 6)
 WALK = 2
 X_SHARES = {
     0: [(0, 192, "scalar"), (192, 512, "vector"), (512, T, "scalar")],
@@ -198,7 +198,7 @@ def tile_moe_tk_lin_none_kernel(tc, xT, w, gate, offs, pos1, pos2, pos3, pos4, o
             for b in closed[:most]:
                 first = BANK_EXPERTS[b][0] * C
                 width = len(BANK_EXPERTS[b]) * C
-                if b == VECTOR_BANK:
+                if b in VECTOR_BANKS:
                     nc.vector.tensor_copy(y[:, first : first + width], banks[b][:, 0:width])
                 else:
                     nc.scalar.copy(y[:, first : first + width], banks[b][:, 0:width])

from contextlib import ExitStack

import concourse.mybir as mybir
from concourse.masks import make_identity

K, T, E, C, N = 2560, 640, 20, 128, 128
SLOTS = E * C
P = 128
PASSES = 5
FLOPS = 2 * SLOTS * K * N

F32 = mybir.dt.float32
BF16 = mybir.dt.bfloat16
I32 = mybir.dt.int32
U32 = mybir.dt.uint32
U16 = mybir.dt.uint16
U8 = mybir.dt.uint8
FP8X4 = mybir.dt.float8_e4m3fn_x4
MULT = mybir.AluOpType.mult
ADD = mybir.AluOpType.add
COPY = mybir.ActivationFunctionType.Copy

SLABS = E * PASSES
RANGES = [(0, 11 * C), (11 * C, 9 * C)]
WINDOW = 1888
LATE = [("a", 0), ("b", 0), ("a", 1), ("b", 1)] + [(a, 1) for a in range(PASSES)]
FIRST = 4
BY_SCALAR, BY_GPSIMD = 4, 3
PERIOD = BY_SCALAR + BY_GPSIMD
FULL = 6
CHUNKS = [4] * FULL + [3, 2, 2, 1, 1]
HELPER = [None] * 3 + ["gpsimd"] * 3 + ["vector"] * 3 + [None] * 2
HELPED = [0] * 3 + [1] * 3 + [2, 1, 1] + [0] * 2
ORDER = list(range(SLABS - PASSES - 1)) + list(range(SLABS - PASSES, SLABS - 1)) + [SLABS - PASSES - 1, SLABS - 1]
BANK_EXPERTS = [[0, 1, 2, 3], [4, 5, 6, 7], [8, 9, 10], [11, 12, 13, 14], [15, 16], [17, 18], [19]]
VECTOR_BANKS = (3, 6)
WALK = 2
X_SHARES = {
    0: [(0, 192, "scalar"), (192, 512, "vector"), (512, T, "scalar")],
    1: [(0, 384, "scalar"), (384, T, "gpsimd")],
    2: [(0, 512, "scalar"), (512, T, "scalar")],
}
GATE_AFTER = 5
SHARE = 512
SPLIT = 384
COL_STEP = 8
CODE_BUFFERS = 8

RAW = 4 * N * 4
GRP = N * 4 * 2
XRAW = 4 * T * 4
XGRP = XRAW // 2
ROW = T * 4
X_AT = 3 * RAW
FIRST_AT = 2 * RAW
OWN_AT = [16 * RAW, 25 * RAW, 0, 8 * RAW]
REST_AT = [20 * RAW, 4 * RAW, 13 * RAW]
CHUNK_RING = [(OWN_AT[1], 5), (OWN_AT[2], 6), (REST_AT[0], 6), (OWN_AT[0], 8)]
FREED_BY_GPSIMD = 2
Y_AFTER = 7
Y_AT = OWN_AT[Y_AFTER % 4]
EARLY_AT = 29 * RAW
GRP_AT = EARLY_AT + PASSES * RANGES[0][1] * 4
GATE_AT = GRP_AT + 4 * 4 * GRP
COL_AT = GATE_AT + 8 * GRP
OUT_ROOM = [2 * GRP if what in ("a", "b") else RANGES[g][1] * 4 for what, g in LATE]
ROOM = [room + BY_GPSIMD * GRP for room in OUT_ROOM]
LATE_AT = [COL_AT + 4 * GRP + sum(ROOM[:k]) for k in range(len(LATE))]
XGRP_AT = [GRP_AT, GRP_AT + XGRP, GRP_AT + 2 * XGRP, LATE_AT[-1], 11 * RAW]


def tile_moe_tk_lin_none_kernel(tc, xT, w, gate, offs, pos1, pos2, pos3, pos4, out):
    nc = tc.nc
    with ExitStack() as ctx:
        keep = ctx.enter_context(tc.tile_pool(name="keep", bufs=1))
        arena = ctx.enter_context(tc.tile_pool(name="arena", bufs=1))
        wq_pool = ctx.enter_context(tc.tile_pool(name="wq", bufs=CODE_BUFFERS))
        psum = ctx.enter_context(tc.psum_pool(name="psum", bufs=1))

        offs_t = keep.tile([P, SLOTS // 16], U16, name="offs_t")
        pos_t = [keep.tile([P, T // 16], U16, name=f"pos_t{r}") for r in range(4)]

        words = keep.tile([P, (PASSES - 1) * T + WINDOW], U32, name="words", align_bytes=64)
        planes = {what: keep.tile([P, WINDOW], U8, name=f"bytes_{what}", align_bytes=64) for what in ("a", "b")}
        banks = [psum.tile([P, 512], F32, name=f"bank{b}") for b in range(8)]

        nc.gpsimd.memset(words[:, PASSES * T :].bitcast(I32), 0)
        nc.gpsimd.memset(planes["a"][:].bitcast(I32), 0)
        nc.gpsimd.memset(planes["b"][:].bitcast(I32), 0)
        ident = keep.tile([P, P], F32, name="ident")
        make_identity(nc, ident[:])

        gathered = {}

        def gather(what, g, at):
            if what in planes:
                window, dtype = planes[what][:], U8
            else:
                first = (PASSES - 1 - what) * T
                window, dtype = words[:, first : first + WINDOW], U32
            lo, size = RANGES[g]
            dst = arena.tile([P, size], dtype, name=f"gathered_{what}_{g}", align_bytes=256, offset=at)
            nc.vector.tensor_copy(dst[:], window.indirect(offs_t[:, lo // 16 : (lo + size) // 16]))
            gathered[what, g] = dst

        def interleave(eng, dst, src):
            if eng == "scalar":
                nc.scalar.copy(dst, src)
            else:
                nc.vector.tensor_copy(dst, src)

        for a in range(PASSES):
            raw = arena.tile([P, 4, T], F32, name=f"xraw{a}", align_bytes=256, offset=X_AT + a * XRAW)
            nc.sync.dma_start(raw[:], xT[512 * a : 512 * (a + 1), :].rearrange("(p j) t -> p j t", j=4))
            if a == 0:
                nc.sync.dma_start(offs_t[:], offs)
            grp = arena.tile([P, T, 4], BF16, name=f"xgrp{a}", align_bytes=256, offset=XGRP_AT[a])
            for lo, hi, eng in X_SHARES.get(a, [(0, T, "scalar")]):
                if eng == "gpsimd":
                    columns = raw[:, :, lo:hi].rearrange("p t c -> p c t")
                    nc.gpsimd.tensor_copy(grp[:, lo:hi, :], columns)
                    continue
                interleave(
                    eng,
                    grp[:, lo:hi, :].rearrange("p (c i) t -> p c t i", i=WALK),
                    raw[:, :, lo:hi].rearrange("p t (c i) -> p c t i", i=WALK),
                )
            flat = grp[:].rearrange("p t j -> p (t j)")
            plane, k = (planes["a"], 4 * a) if a < 4 else (planes["b"], 0)
            first = (PASSES - 1 - a) * T
            for lo, hi in ((0, 512), (512, T)):
                nc.vector.quantize_mx(
                    out=words[:, first + lo : first + hi].bitcast(FP8X4),
                    scales=plane[k:P, lo:hi],
                    in_=flat[:, 4 * lo : 4 * hi],
                )
            gather(a, 0, EARLY_AT + a * RANGES[0][1] * 4)

        w_slabs = w.rearrange("e (a p j) n -> p (e a) (j n)", a=PASSES, j=4)
        bank_of = {e: (b, i) for b, es in enumerate(BANK_EXPERTS) for i, e in enumerate(es)}
        y = arena.tile([P, SLOTS], F32, name="y", align_bytes=256, offset=Y_AT)
        waiting = {}
        done = []
        closed = []

        def load(queue, name, place, size, at):
            raw = arena.tile([P, size, 4, N], F32, name=name, align_bytes=256, offset=at)
            source = w_slabs[:, ORDER[place] : ORDER[place] + size, :]
            queue.dma_start(raw[:].rearrange("p u j n -> p u (j n)"), source)
            return raw

        def grouped(name, size, at):
            return arena.tile([P, size, N, 4], BF16, name=name, align_bytes=256, offset=at)

        def round_slabs(eng, dst, src):
            interleave(
                eng,
                dst.rearrange("p u (c i) t -> p u c t i", i=WALK),
                src.rearrange("p u t (c i) -> p u c t i", i=WALK),
            )

        def quantise(grp, place, size):
            codes = wq_pool.tile([P, 4 * N], U32, name="wcodes", align_bytes=64)
            scales = wq_pool.tile([P, 4 * N], U8, name="wscales", align_bytes=64)
            nc.vector.quantize_mx(
                out=codes[:, 0 : size * N].bitcast(FP8X4),
                scales=scales[:, 0 : size * N],
                in_=grp[:].rearrange("p u n j -> p (u n j)"),
            )
            for u in range(size):
                waiting[place + u] = (codes[:, u * N : (u + 1) * N], scales[:, u * N : (u + 1) * N])

        def multiply():
            while len(done) in waiting:
                place = len(done)
                codes, scales = waiting[place]
                e, a = divmod(ORDER[place], PASSES)
                g = 0 if e * C < RANGES[1][0] else 1
                at = e * C - RANGES[g][0]
                if any((what, g) not in gathered for what in ["a", "b"] + list(range(PASSES))):
                    return
                done.append(place)
                b, i = bank_of[e]
                plane, k = (gathered["a", g], 4 * a) if a < 4 else (gathered["b", g], 0)
                nc.tensor.matmul_mx(
                    out=banks[b][:, i * C : (i + 1) * C],
                    lhsT=codes.bitcast(FP8X4),
                    lhsT_scale=scales,
                    rhs=gathered[a, g][:, at : at + C].bitcast(FP8X4),
                    rhs_scale=plane[k:P, at : at + C],
                    start=(a == 0),
                    stop=(a == PASSES - 1),
                )
                if a == PASSES - 1 and e == BANK_EXPERTS[b][-1]:
                    closed.append(b)

        def evacuate(most):
            for b in closed[:most]:
                first = BANK_EXPERTS[b][0] * C
                width = len(BANK_EXPERTS[b]) * C
                if b in VECTOR_BANKS:
                    nc.vector.tensor_copy(y[:, first : first + width], banks[b][:, 0:width])
                else:
                    nc.scalar.copy(y[:, first : first + width], banks[b][:, 0:width])
                closed.remove(b)

        def round_on_gpsimd(dst, src):
            nc.gpsimd.tensor_scalar(dst, src.rearrange("p u t n -> p u n t"), 1.0, 0.0, MULT, ADD)

        own_first = [FIRST + max(k * PERIOD - BY_GPSIMD, 0) for k in range(len(LATE))]
        rest_first = [at + BY_SCALAR for at in own_first[1:]] + [own_first[-1] + PERIOD]
        owns, rests = {}, {}

        def load_own(k):
            if k < len(LATE):
                owns[k] = load(nc.scalar, f"wown{k}", own_first[k], BY_SCALAR, OWN_AT[k % 4])

        def load_rest(k):
            if k < len(LATE):
                rests[k] = load(nc.sync, f"wrest{k}", rest_first[k], BY_GPSIMD, REST_AT[k % 3])

        starts = [FIRST + len(LATE) * PERIOD + sum(CHUNKS[:i]) for i in range(len(CHUNKS))]
        seats = [(0, 0)]
        for before, size in zip(CHUNKS, CHUNKS[1:]):
            seat, at = seats[-1]
            seats.append((seat, at + before) if at + before + size <= 4 else (seat + 1, 0))
        raws = {}

        def load_seat(seat):
            for i, (s, at) in enumerate(seats):
                if s == seat:
                    base = CHUNK_RING[seat % len(CHUNK_RING)][0]
                    raws[i] = arena.tile(
                        [P, CHUNKS[i], 4, N], F32, name=f"wraw{i}", align_bytes=256, offset=base + at * RAW
                    )
                    first = nc.scalar if i < FULL and i != FREED_BY_GPSIMD else nc.sync
                    cut = CHUNKS[i] // 2 if i < FULL else CHUNKS[i] - HELPED[i]
                    for queue, lo, hi in ((first, 0, cut), (nc.sync, cut, CHUNKS[i])):
                        if hi > lo:
                            source = w_slabs[:, ORDER[starts[i]] + lo : ORDER[starts[i]] + hi, :]
                            queue.dma_start(raws[i][:, lo:hi].rearrange("p u j n -> p u (j n)"), source)

        raw = load(nc.sync, "wraw_first", 0, FIRST, FIRST_AT)
        load_own(0)
        load_own(1)
        load_rest(0)
        grp = grouped("wgrp_first", FIRST, COL_AT)
        round_slabs("scalar", grp[:], raw[:])
        for k in (2, 3):
            load_own(k)
            load_rest(k - 1)
        quantise(grp, 0, FIRST)

        for k, (what, g) in enumerate(LATE):
            border = LATE_AT[k] + OUT_ROOM[k]
            grp = grouped(f"wgrp_s{k}", BY_SCALAR, border - 2 * GRP)
            round_slabs("scalar", grp[:], owns[k][:])
            load_own(k + 4)
            if k == Y_AFTER:
                evacuate(2)
            quantise(grp, own_first[k], BY_SCALAR)
            gather(what, g, LATE_AT[k])
            grp = grouped(f"wgrp_g{k}", BY_GPSIMD, border)
            round_on_gpsimd(grp[:], rests[k][:])
            load_rest(k + 3)
            for seat, (at, period) in enumerate(CHUNK_RING):
                if period == k:
                    load_seat(seat)
            quantise(grp, rest_first[k], BY_GPSIMD)
            multiply()

        carried = [0] + HELPED[:-1]
        widths = [s + c - d for s, c, d in zip(CHUNKS, carried, HELPED)]
        places = {GATE_AFTER: GATE_AT, GATE_AFTER + 1: COL_AT}
        grps = [grouped(f"wgrp{i}", wd, places.get(i, GRP_AT + i % 4 * 4 * GRP)) for i, wd in enumerate(widths)]
        for i, size in enumerate(CHUNKS):
            own = size - HELPED[i]
            round_slabs("scalar", grps[i][:, carried[i] :], raws[i][:, 0:own])
            if HELPER[i] == "vector":
                round_slabs("vector", grps[i + 1][:, 0 : HELPED[i]], raws[i][:, own:size])
            if HELPER[i] == "gpsimd":
                round_on_gpsimd(grps[i + 1][:, 0:1], raws[i][:, own:size])
            if seats[i][1] == 0:
                load_seat(seats[i][0] + len(CHUNK_RING))
            quantise(grps[i], starts[i] - carried[i], widths[i])
            if i > 0:
                evacuate(1)
            multiply()
        evacuate(2)

        gate_t = arena.tile([P, 3, T], F32, name="gate_t", align_bytes=256, offset=GATE_AT)
        lists = (pos1, pos2, pos3, pos4)
        for r in (0, 2):
            nc.sync.dma_start(pos_t[r][:], lists[r])
        nc.sync.dma_start(gate_t[:, 0, :], gate[0])
        for r in (3, 1):
            nc.sync.dma_start(pos_t[r][:], lists[r])
        nc.sync.dma_start(gate_t[:, 1, :], gate[1])
        gate_col = arena.tile([P, 2 * COL_STEP], F32, name="gate_col", align_bytes=256, offset=COL_AT)
        with nc.allow_non_contiguous_dma(reason="one weight a token and partition"):
            for r in (2, 3):
                tokens = SHARE if r == 2 else T
                columns = gate_col[:, (r - 2) * COL_STEP : (r - 2) * COL_STEP + tokens // P]
                nc.sync.dma_start(columns, gate[r, 0, 0:tokens].rearrange("(j p) -> p j", p=P))
        nc.sync.dma_start(gate_t[:, 2, SHARE:T], gate[2, :, SHARE:T])

        whole, shared, rest = slice(0, T), slice(0, SHARE), slice(SHARE, T)
        blocks = {2: SHARE // P, 3: T // P}

        def floats(name, width, at):
            return arena.tile([P, width], F32, name=name, align_bytes=256, offset=at)

        prod = [floats(f"prod{r}", T if r < 2 else T - SHARE, EARLY_AT + r * ROW) for r in range(3)]
        picked = {r: floats(f"picked{r}", blocks[r] * P, EARLY_AT + (r + 1) * ROW) for r in (2, 3)}
        scaled = {r: floats(f"scaled{r}", blocks[r] * P, EARLY_AT + (r + 3) * ROW) for r in (2, 3)}
        pair = floats("pair", T, EARLY_AT + 7 * ROW)
        triple = floats("triple", T - SHARE, EARLY_AT + 8 * ROW)
        res = floats("res", T, EARLY_AT + 9 * ROW)

        def window(r, cols):
            return y[:].indirect(pos_t[r][:, cols.start // 16 : cols.stop // 16])

        def turn(dst, src, start, stop):
            nc.tensor.matmul(dst, lhsT=src, rhs=ident[:], is_transpose=True, start=start, stop=stop)

        def block(j):
            return slice(j * P, (j + 1) * P)

        picks = [(2, shared), (3, slice(0, SPLIT)), (3, slice(SPLIT, T))]
        back = [banks[len(picks) + j][:, 0:P] for j in range(T // P)]
        turned = {}
        for b, (r, cols) in enumerate(picks):
            nc.scalar.activation(picked[r][:, cols], window(r, cols), COPY)
            for j in range(cols.start // P, cols.stop // P):
                turned[r, j] = banks[b][:, block(j - cols.start // P)]
                turn(turned[r, j], picked[r][:, block(j)], True, True)
        for r in (2, 3):
            for j in range(blocks[r]):
                column = gate_col[:, (r - 2) * COL_STEP + j : (r - 2) * COL_STEP + j + 1]
                nc.scalar.activation(scaled[r][:, block(j)], turned[r, j], COPY, scale=column)
                turn(back[j], scaled[r][:, block(j)], r == 2 or j >= blocks[2], r == 3)
        for r in range(3):
            cols = whole if r < 2 else rest
            nc.vector.tensor_tensor(prod[r][:], window(r, cols), gate_t[:, r, cols], MULT)
        for cols in (shared, rest):
            nc.vector.tensor_add(pair[:, cols], prod[0][:, cols], prod[1][:, cols])
        for j in range(T // P):
            if j == 1:
                nc.vector.tensor_add(triple[:], pair[:, rest], prod[2][:])
            nc.vector.tensor_add(res[:, block(j)], pair[:, block(j)] if j < blocks[2] else triple[:, block(j - blocks[2])], back[j])
        for cols in (slice(0, SPLIT), slice(SPLIT, T)):
            nc.sync.dma_start(out[:, cols], res[:, cols])
